import numpy as np
import ml_dtypes


def mxq(x, axis, fmt="e4m3"):
    dtype, down = {"e4m3": (ml_dtypes.float8_e4m3fn, 7), "e5m2": (ml_dtypes.float8_e5m2, 14)}[fmt]
    v = np.moveaxis(np.asarray(x, np.float32).astype(ml_dtypes.bfloat16).astype(np.float64), axis, -1)
    blocks = v.reshape(v.shape[:-1] + (-1, 32))
    amax = np.abs(blocks).max(-1, keepdims=True)
    byte = np.maximum(np.where(amax > 0, np.frexp(amax)[1] - 1 + 127, 0) - down, 1)
    scale = np.exp2(byte - 127.0)
    codes = (blocks / scale).astype(np.float32).astype(dtype).astype(np.float64)
    return np.moveaxis((codes * scale).reshape(v.shape), -1, axis)


WIDE = False


def mx_kscale(k):
    if not WIDE:
        return np.ones(k)
    levels = np.array([18, -18])
    if k % 512:
        return np.exp2(np.random.permutation(np.resize(levels, k // 32))).repeat(32)
    a = np.empty((k // 512, 16))
    for p in range(k // 512):
        a[p, :8] = np.random.permutation(np.resize(levels, 8))
        for g in range(8):
            far = levels[np.abs(levels - a[p, g]) >= 10]
            a[p, g + 8] = far[np.random.randint(len(far))]
    return np.exp2(a.ravel()).repeat(32)


def f64(x):
    return np.asarray(x).astype(np.float64)


def striped(idx):
    return np.tile(np.asarray(idx).reshape(-1, 16).T, (8, 1)).astype(np.uint16)


def unstriped(offs):
    return offs[:16].T.reshape(-1).astype(np.int64)


B, N, T, D, DV, R = 1, 512, 2048, 512, 512, 512


def setup_inputs():
    n = np.random.standard_normal
    idx = np.random.permutation(T)[:B * N]
    s = mx_kscale(D)[:, None]
    z = mx_kscale(R)[:, None]
    v = mx_kscale(DV)[:, None]
    q = n((B, D, R))
    do = n((B, DV, R))
    u = np.ones(T)
    u[idx] = mx_kscale(B * N)
    r = np.random.uniform(0.5, 2.0, T) * u
    return {
        "qT": (q * s).astype(np.float32),
        "kT": (n((D, T)) * (1.00 / np.sqrt(D)) / s / r).astype(np.float32),
        "vT": (n((DV, T)) / np.sqrt(DV) / v).astype(np.float32),
        "doT": (do * v).astype(np.float32),
        "rw": (np.random.uniform(0.5, 1.5, (B, R, 1)) * 1.0 / np.sqrt(R) * z).astype(np.float32),
        "ts": np.tile(r, (128, 1)).astype(np.float32),
        "qm": (q.transpose(0, 2, 1) / z).astype(np.float32),
        "offs": striped(idx),
    }


def reference(qT, kT, vT, doT, rw, ts, qm, offs):
    idx = unstriped(offs)
    pick = lambda x: x[:, idx].reshape(x.shape[0], B, N).transpose(1, 0, 2)
    k = pick(f64(kT))
    a = mxq(f64(qT), 1, "e4m3").transpose(0, 2, 1) @ mxq(k, 1, "e4m3")
    ts_ = pick(f64(ts))[:, :1, :]
    a = a * ts_
    p = np.tanh(a)
    dp = mxq(f64(doT), 1, "e5m2").transpose(0, 2, 1) @ mxq(pick(f64(vT)), 1, "e4m3")
    ds = f64(rw) * dp * (1.0 - p * p)
    ds = ts_ * ds
    gq = mxq(ds, 2, "e5m2") @ mxq(k, 2, "e4m3").transpose(0, 2, 1)
    dk = mxq(f64(qm), 1, "e4m3").transpose(0, 2, 1) @ mxq(ds, 1, "e5m2")
    gk = np.zeros((D, T))
    gk[:, idx] = dk.transpose(1, 0, 2).reshape(D, B * N)
    return gq, gk

@@ -1,0 +1,212 @@
+from contextlib import ExitStack
+
+import concourse.mybir as mybir
+from concourse.masks import make_identity
+
+N, T, D, DV, R = 512, 2048, 512, 512, 512
+FLOPS = 2 * N * R * (3 * D + DV)
+
+F32 = mybir.dt.float32
+BF16 = mybir.dt.bfloat16
+U32 = mybir.dt.uint32
+U16 = mybir.dt.uint16
+U8 = mybir.dt.uint8
+E4 = mybir.dt.float8_e4m3fn_x4
+E5 = mybir.dt.float8_e5m2_x4
+ACT = mybir.ActivationFunctionType
+ALU = mybir.AluOpType
+
+P = 128
+PACK = 4
+W = 512
+HALF = W // 2
+
+
+def tile_attend_gat_tnh_qk_ts_kernel(tc, qT, kT, vT, doT, rw, ts, qm, offs, out_0, out_1):
+    nc = tc.nc
+    with ExitStack() as ctx:
+        keep = ctx.enter_context(tc.tile_pool(name="keep", bufs=1))
+        ring = ctx.enter_context(tc.tile_pool(name="ring", bufs=2))
+        mm = ctx.enter_context(tc.psum_pool(name="mm", bufs=4))
+        tr = ctx.enter_context(tc.psum_pool(name="tr", bufs=3))
+        gate = ctx.enter_context(tc.psum_pool(name="gate", bufs=1))
+
+        def operand(name):
+            values = keep.tile([P, W * PACK], BF16, name=name + "_values", align_bytes=64)
+            codes = keep.tile([P, W], U32, name=name + "_codes", align_bytes=64)
+            scales = keep.tile([P, W], U8, name=name + "_scales", align_bytes=64)
+            return values, codes, scales
+
+        def quantize(op, fmt, first=0, count=W):
+            values, codes, scales = op
+            nc.vector.quantize_mx(
+                out=codes[:, first:first + count].bitcast(fmt),
+                scales=scales[:, first:first + count],
+                in_=values[:, PACK * first:PACK * (first + count)],
+            )
+
+        def product(stationary, fmt_s, block, moving, fmt_m):
+            acc = mm.tile([P, W], F32, name="acc")
+            cols = slice(block * P, (block + 1) * P)
+            nc.tensor.matmul_mx(
+                out=acc[:],
+                lhsT=stationary[1][:, cols].bitcast(fmt_s),
+                lhsT_scale=stationary[2][:, cols],
+                rhs=moving[1][:].bitcast(fmt_m),
+                rhs_scale=moving[2][:],
+                start=True,
+                stop=True,
+            )
+            return acc
+
+        def dealt(values):
+            return values[:].rearrange("p (t m j) -> p m j t", t=PACK, j=PACK)
+
+        offsets = keep.tile([P, N // 16], U16, name="offsets")
+        nc.sync.dma_start(offsets[:], offs)
+
+        ts_pool = keep.tile([P, T], F32, name="ts_pool")
+        nc.vector.memset(ts_pool[:], 0.0)
+
+        k_pool = [keep.tile([P, T], F32, name="k_pool%d" % j) for j in range(PACK)]
+        v_pool = [keep.tile([P, T], F32, name="v_pool%d" % j) for j in range(PACK)]
+        q_raw = [keep.tile([P, PACK, HALF], F32, name="q_raw%d" % h) for h in range(2)]
+        do_raw = [keep.tile([P, PACK, HALF], F32, name="do_raw%d" % h) for h in range(2)]
+        qm_raw = keep.tile([P, PACK, D], F32, name="qm_raw")
+        rw_col = keep.tile([P, PACK], F32, name="rw_col")
+
+        k_rows = kT.rearrange("(p j) t -> p j t", j=PACK)
+        v_rows = vT.rearrange("(p j) t -> p j t", j=PACK)
+        q_rows = qT[0].rearrange("(p j) r -> p j r", j=PACK)
+        do_rows = doT[0].rearrange("(p j) r -> p j r", j=PACK)
+        for j in range(PACK):
+            nc.sync.dma_start(k_pool[j][:], k_rows[:, j, :])
+        nc.sync.dma_start(ts_pool[0:1, :], ts[0:1, :])
+        nc.sync.dma_start(rw_col[:], rw[0].rearrange("(p t) o -> p (t o)", t=PACK))
+        for h in range(2):
+            nc.sync.dma_start(q_raw[h][:], q_rows[:, :, h * HALF:(h + 1) * HALF])
+        for j in range(PACK):
+            nc.sync.dma_start(v_pool[j][:], v_rows[:, j, :])
+        for h in range(2):
+            nc.sync.dma_start(do_raw[h][:], do_rows[:, :, h * HALF:(h + 1) * HALF])
+        nc.sync.dma_start(qm_raw[:], qm[0].rearrange("(p j) d -> p j d", j=PACK))
+
+        ident32 = keep.tile([P, P], F32, name="ident32")
+        ident16 = keep.tile([P, P], BF16, name="ident16")
+        make_identity(nc, ident32[:])
+        make_identity(nc, ident16[:])
+
+        k_listed = keep.tile([P, PACK, N], F32, name="k_listed")
+        k_d = operand("k_d")
+        k_i = operand("k_i")
+        for j in range(PACK):
+            nc.vector.tensor_copy(k_listed[:, j, :], k_pool[j][:].indirect(offsets[:]))
+            turned = tr.tile([P, PACK, P], F32, name="turned", tag="turned")
+            for t in range(PACK):
+                nc.tensor.transpose(turned[:, t, :], k_listed[:, j, t::PACK], ident32[:])
+            nc.scalar.copy(
+                k_i[0][:, j * W:(j + 1) * W].rearrange("p (c t) -> p c t", t=PACK),
+                turned[:].rearrange("p t c -> p c t"),
+            )
+        nc.vector.tensor_copy(dealt(k_d[0]), k_listed[:].rearrange("p j (m t) -> p m j t", t=PACK))
+        quantize(k_d, E4)
+
+        q_d = operand("q_d")
+        for h in range(2):
+            nc.scalar.copy(
+                dealt(q_d[0])[:, h * 64:(h + 1) * 64],
+                q_raw[h][:].rearrange("p j (m t) -> p m j t", t=PACK),
+            )
+        quantize(q_d, E4)
+
+        ts_listed = keep.tile([P, N], F32, name="ts_listed")
+        nc.vector.tensor_copy(ts_listed[:], ts_pool[:].indirect(offsets[:]))
+        ts_turned = tr.tile([P, PACK, P], F32, name="ts_turned", tag="turned")
+        for t in range(PACK):
+            nc.tensor.transpose(ts_turned[:, t, :], ts_listed[:, t::PACK], ident32[:])
+        ts_col = keep.tile([P, PACK], F32, name="ts_col")
+        nc.scalar.copy(ts_col[:], ts_turned[:, :, 0])
+
+        rw_neg = keep.tile([P, PACK], F32, name="rw_neg")
+        nc.vector.tensor_scalar(rw_neg[:], rw_col[:], -1.0, None, ALU.mult)
+        rw_wide = gate.tile([P, PACK, P], F32, name="rw_wide")
+        for t in range(PACK):
+            nc.tensor.transpose(rw_wide[:, t, :], rw_neg[:, t:t + 1].to_broadcast([P, P]), ident32[:])
+
+        v_listed = keep.tile([P, PACK, N], F32, name="v_listed")
+        v_e = operand("v_e")
+        for j in range(PACK):
+            nc.vector.tensor_copy(v_listed[:, j, :], v_pool[j][:].indirect(offsets[:]))
+        nc.vector.tensor_copy(dealt(v_e[0]), v_listed[:].rearrange("p j (m t) -> p m j t", t=PACK))
+        quantize(v_e, E4)
+
+        slope = keep.tile([P, PACK, R], F32, name="slope")
+        for t in range(PACK):
+            score = product(k_d, E4, t, q_d, E4)
+            weight = ring.tile([P, R], F32, name="weight")
+            nc.scalar.activation(weight[:], score[:], ACT.Tanh, scale=ts_col[:, t:t + 1])
+            squared = ring.tile([P, R], F32, name="squared")
+            nc.scalar.activation(squared[:], weight[:], ACT.Square)
+            nc.vector.scalar_tensor_tensor(
+                slope[:, t, :], squared[:], 1.0, rw_wide[:].rearrange("p t m -> p (t m)"), ALU.subtract, ALU.mult
+            )
+
+        do_e = operand("do_e")
+        for h in range(2):
+            nc.scalar.copy(
+                dealt(do_e[0])[:, h * 64:(h + 1) * 64],
+                do_raw[h][:].rearrange("p j (m t) -> p m j t", t=PACK),
+            )
+        quantize(do_e, E5)
+
+        ds = keep.tile([P, PACK, R], BF16, name="ds")
+        ds_r = operand("ds_r")
+        for t in range(PACK):
+            dp = product(v_e, E4, t, do_e, E5)
+            nc.vector.scalar_tensor_tensor(ds[:, t, :], dp[:], ts_col[:, t:t + 1], slope[:, t, :], ALU.mult, ALU.mult)
+        for t in range(PACK):
+            ds_turned = tr.tile([P, PACK, P], BF16, name="ds_turned", tag="turned")
+            for u in range(PACK):
+                nc.tensor.transpose(ds_turned[:, u, :], ds[:, t, u * P:(u + 1) * P], ident16[:])
+            nc.scalar.copy(
+                ds_r[0][:, t * W:(t + 1) * W].rearrange("p (c u) -> p c u", u=PACK),
+                ds_turned[:].rearrange("p u c -> p c u"),
+            )
+            quantize(ds_r, E5, t * P, P)
+
+        qm_r = operand("qm_r")
+        for c in range(PACK):
+            nc.vector.tensor_copy(
+                qm_r[0][:, c * W:(c + 1) * W].rearrange("p (c i j) -> p c j i", i=PACK, j=PACK),
+                qm_raw[:, :, c * P:(c + 1) * P].rearrange("p j (c i) -> p c j i", i=PACK),
+            )
+            quantize(qm_r, E4, c * P, P)
+
+        for c in range(PACK):
+            dk = product(qm_r, E4, c, ds_r, E5)
+            dk_listed = keep.tile([P, N], F32, name="dk_listed%d" % c)
+            nc.scalar.copy(
+                dk_listed[:].rearrange("p (m t) -> p m t", t=PACK),
+                dk[:].rearrange("p (t m) -> p m t", t=PACK),
+            )
+            placed = keep.tile([P, T], F32, name="placed%d" % c)
+            nc.gpsimd.memset(placed[:], 0.0)
+            nc.vector.tensor_copy(placed[:].indirect(offsets[:]), dk_listed[:])
+            nc.sync.dma_start(out_1[c * P:(c + 1) * P, :], placed[:])
+
+        quantize(k_i, E4)
+        ds_i = operand("ds_i")
+        gq_rows = out_0[0].rearrange("(m u) d -> m u d", u=PACK)
+        for u in range(PACK):
+            nc.scalar.copy(
+                ds_i[0][:, u * W:(u + 1) * W].rearrange("p (c i t) -> p c t i", i=PACK, t=PACK),
+                ds[:, :, u * P:(u + 1) * P].rearrange("p t (c i) -> p c t i", i=PACK),
+            )
+            quantize(ds_i, E5, u * P, P)
+            gq = product(ds_i, E5, u, k_i, E4)
+            gq_out = keep.tile([P, D], F32, name="gq_out%d" % u)
+            nc.scalar.copy(
+                gq_out[:].rearrange("p (c j) -> p c j", j=PACK),
+                gq[:].rearrange("p (j c) -> p c j", j=PACK),
+            )
+            nc.scalar.dma_start(gq_rows[:, u, :], gq_out[:])

@@ -8,6 +8,7 @@ FLOPS = 2 * N * R * (3 * D + DV)
 
 F32 = mybir.dt.float32
 BF16 = mybir.dt.bfloat16
+I32 = mybir.dt.int32
 U32 = mybir.dt.uint32
 U16 = mybir.dt.uint16
 U8 = mybir.dt.uint8
@@ -26,13 +27,13 @@ def tile_attend_gat_tnh_qk_ts_kernel(tc, qT, kT, vT, doT, rw, ts, qm, offs, out_
     nc = tc.nc
     with ExitStack() as ctx:
         keep = ctx.enter_context(tc.tile_pool(name="keep", bufs=1))
-        ring = ctx.enter_context(tc.tile_pool(name="ring", bufs=2))
+        stream = ctx.enter_context(tc.tile_pool(name="stream", bufs=4))
         mm = ctx.enter_context(tc.psum_pool(name="mm", bufs=4))
         tr = ctx.enter_context(tc.psum_pool(name="tr", bufs=3))
         gate = ctx.enter_context(tc.psum_pool(name="gate", bufs=1))
 
-        def operand(name):
-            values = keep.tile([P, W * PACK], BF16, name=name + "_values", align_bytes=64)
+        def operand(name, tag=None):
+            values = keep.tile([P, W * PACK], BF16, name=name + "_values", tag=tag or name, align_bytes=64)
             codes = keep.tile([P, W], U32, name=name + "_codes", align_bytes=64)
             scales = keep.tile([P, W], U8, name=name + "_scales", align_bytes=64)
             return values, codes, scales
@@ -62,42 +63,58 @@ def tile_attend_gat_tnh_qk_ts_kernel(tc, qT, kT, vT, doT, rw, ts, qm, offs, out_
         def dealt(values):
             return values[:].rearrange("p (t m j) -> p m j t", t=PACK, j=PACK)
 
+        def shared_operand(name, raw, fmt, tag_scalar, tag_vector):
+            codes = keep.tile([P, W], U32, name=name + "_codes", align_bytes=64)
+            scales = keep.tile([P, W], U8, name=name + "_scales", align_bytes=64)
+            rows = raw[:].rearrange("p j (m t) -> p m j t", t=PACK)
+            halves = []
+            for h, tag, copy in ((0, tag_scalar, nc.scalar.copy), (1, tag_vector, nc.vector.tensor_copy)):
+                values = keep.tile([P, HALF * PACK], BF16, name=name + "_values%d" % h, tag=tag, align_bytes=64)
+                copy(values[:].rearrange("p (t m j) -> p m j t", t=2, j=PACK), rows[:, :, :, 2 * h:2 * h + 2])
+                halves.append(values)
+            for h in range(2):
+                nc.vector.quantize_mx(
+                    out=codes[:, h * HALF:(h + 1) * HALF].bitcast(fmt),
+                    scales=scales[:, h * HALF:(h + 1) * HALF],
+                    in_=halves[h][:],
+                )
+            return halves, codes, scales
+
         offsets = keep.tile([P, N // 16], U16, name="offsets")
         nc.sync.dma_start(offsets[:], offs)
 
         ts_pool = keep.tile([P, T], F32, name="ts_pool")
-        nc.vector.memset(ts_pool[:], 0.0)
+        nc.vector.memset(ts_pool[:].bitcast(I32), 0)
 
-        k_pool = [keep.tile([P, T], F32, name="k_pool%d" % j) for j in range(PACK)]
-        v_pool = [keep.tile([P, T], F32, name="v_pool%d" % j) for j in range(PACK)]
-        q_raw = [keep.tile([P, PACK, HALF], F32, name="q_raw%d" % h) for h in range(2)]
-        do_raw = [keep.tile([P, PACK, HALF], F32, name="do_raw%d" % h) for h in range(2)]
-        qm_raw = keep.tile([P, PACK, D], F32, name="qm_raw")
         rw_col = keep.tile([P, PACK], F32, name="rw_col")
+
+        def load(name, shape, rows):
+            landed = stream.tile(shape, F32, name=name, tag="landed")
+            nc.sync.dma_start(landed[:], rows)
+            return landed
 
         k_rows = kT.rearrange("(p j) t -> p j t", j=PACK)
         v_rows = vT.rearrange("(p j) t -> p j t", j=PACK)
         q_rows = qT[0].rearrange("(p j) r -> p j r", j=PACK)
         do_rows = doT[0].rearrange("(p j) r -> p j r", j=PACK)
-        for j in range(PACK):
-            nc.sync.dma_start(k_pool[j][:], k_rows[:, j, :])
+        k_pool = [load("k_pool%d" % j, [P, T], k_rows[:, j, :]) for j in range(2)]
         nc.sync.dma_start(ts_pool[0:1, :], ts[0:1, :])
         nc.sync.dma_start(rw_col[:], rw[0].rearrange("(p t) o -> p (t o)", t=PACK))
-        for h in range(2):
-            nc.sync.dma_start(q_raw[h][:], q_rows[:, :, h * HALF:(h + 1) * HALF])
-        for j in range(PACK):
-            nc.sync.dma_start(v_pool[j][:], v_rows[:, j, :])
-        for h in range(2):
-            nc.sync.dma_start(do_raw[h][:], do_rows[:, :, h * HALF:(h + 1) * HALF])
-        nc.sync.dma_start(qm_raw[:], qm[0].rearrange("(p j) d -> p j d", j=PACK))
+        k_pool += [load("k_pool%d" % j, [P, T], k_rows[:, j, :]) for j in range(2, PACK)]
+        q_raw = load("q_raw", [P, PACK, R], q_rows)
+        v_pool = [load("v_pool%d" % j, [P, T], v_rows[:, j, :]) for j in range(PACK)]
+        do_raw = load("do_raw", [P, PACK, R], do_rows)
+        qm_raw = load("qm_raw", [P, PACK, D], qm[0].rearrange("(p j) d -> p j d", j=PACK))
 
         ident32 = keep.tile([P, P], F32, name="ident32")
         ident16 = keep.tile([P, P], BF16, name="ident16")
         make_identity(nc, ident32[:])
         make_identity(nc, ident16[:])
 
+        placed = [keep.tile([P, T], F32, name="placed%d" % c) for c in range(PACK)]
+
         k_listed = keep.tile([P, PACK, N], F32, name="k_listed")
-        k_d = operand("k_d")
+        k_d = operand("k_d", "k_then_q_then_v")
         k_i = operand("k_i")
         for j in range(PACK):
             nc.vector.tensor_copy(k_listed[:, j, :], k_pool[j][:].indirect(offsets[:]))
@@ -108,16 +125,9 @@ def tile_attend_gat_tnh_qk_ts_kernel(tc, qT, kT, vT, doT, rw, ts, qm, offs, out_
                 k_i[0][:, j * W:(j + 1) * W].rearrange("p (c t) -> p c t", t=PACK),
                 turned[:].rearrange("p t c -> p c t"),
             )
-        nc.vector.tensor_copy(dealt(k_d[0]), k_listed[:].rearrange("p j (m t) -> p m j t", t=PACK))
-        quantize(k_d, E4)
-
-        q_d = operand("q_d")
-        for h in range(2):
-            nc.scalar.copy(
-                dealt(q_d[0])[:, h * 64:(h + 1) * 64],
-                q_raw[h][:].rearrange("p j (m t) -> p m j t", t=PACK),
-            )
-        quantize(q_d, E4)
+        for c in range(PACK):
+            engine = nc.vector if c < 2 else nc.gpsimd
+            engine.memset(placed[c][:].bitcast(I32), 0)
 
         ts_listed = keep.tile([P, N], F32, name="ts_listed")
         nc.vector.tensor_copy(ts_listed[:], ts_pool[:].indirect(offsets[:]))
@@ -133,34 +143,36 @@ def tile_attend_gat_tnh_qk_ts_kernel(tc, qT, kT, vT, doT, rw, ts, qm, offs, out_
         for t in range(PACK):
             nc.tensor.transpose(rw_wide[:, t, :], rw_neg[:, t:t + 1].to_broadcast([P, P]), ident32[:])
 
-        v_listed = keep.tile([P, PACK, N], F32, name="v_listed")
-        v_e = operand("v_e")
+        nc.vector.tensor_copy(dealt(k_d[0]), k_listed[:].rearrange("p j (m t) -> p m j t", t=PACK))
+        quantize(k_d, E4)
+
+        q_d = shared_operand("q_d", q_raw, E4, "q_half", "k_then_q_then_v")
+
+        v_listed = keep.tile([P, PACK, N], F32, name="v_listed", tag="k_then_q_then_v", align_bytes=64)
+        slope = keep.tile([P, PACK, R], F32, name="slope", tag="slope_then_qm", align_bytes=64)
+        weight = keep.tile([P, PACK, R], F32, name="weight")
+        squared = keep.tile([P, 2, R], F32, name="squared")
+        for t in range(PACK):
+            score = product(k_d, E4, t, q_d, E4)
+            nc.scalar.activation(weight[:, t, :], score[:], ACT.Tanh, scale=ts_col[:, t:t + 1])
+            square = squared[:, t, :] if t < 2 else v_listed[:, t, :]
+            nc.scalar.activation(square, weight[:, t, :], ACT.Square)
+            nc.vector.scalar_tensor_tensor(
+                slope[:, t, :], square, 1.0, rw_wide[:].rearrange("p t m -> p (t m)"), ALU.subtract, ALU.mult
+            )
+
+        quantize(k_i, E4)
+
+        v_e = operand("v_e", "v_then_do")
         for j in range(PACK):
             nc.vector.tensor_copy(v_listed[:, j, :], v_pool[j][:].indirect(offsets[:]))
         nc.vector.tensor_copy(dealt(v_e[0]), v_listed[:].rearrange("p j (m t) -> p m j t", t=PACK))
         quantize(v_e, E4)
 
-        slope = keep.tile([P, PACK, R], F32, name="slope")
-        for t in range(PACK):
-            score = product(k_d, E4, t, q_d, E4)
-            weight = ring.tile([P, R], F32, name="weight")
-            nc.scalar.activation(weight[:], score[:], ACT.Tanh, scale=ts_col[:, t:t + 1])
-            squared = ring.tile([P, R], F32, name="squared")
-            nc.scalar.activation(squared[:], weight[:], ACT.Square)
-            nc.vector.scalar_tensor_tensor(
-                slope[:, t, :], squared[:], 1.0, rw_wide[:].rearrange("p t m -> p (t m)"), ALU.subtract, ALU.mult
-            )
-
-        do_e = operand("do_e")
-        for h in range(2):
-            nc.scalar.copy(
-                dealt(do_e[0])[:, h * 64:(h + 1) * 64],
-                do_raw[h][:].rearrange("p j (m t) -> p m j t", t=PACK),
-            )
-        quantize(do_e, E5)
+        do_e = shared_operand("do_e", do_raw, E5, "do_half", "v_then_do")
 
         ds = keep.tile([P, PACK, R], BF16, name="ds")
-        ds_r = operand("ds_r")
+        ds_r = operand("ds_r", "ds_r_then_ds_i")
         for t in range(PACK):
             dp = product(v_e, E4, t, do_e, E5)
             nc.vector.scalar_tensor_tensor(ds[:, t, :], dp[:], ts_col[:, t:t + 1], slope[:, t, :], ALU.mult, ALU.mult)
@@ -174,7 +186,7 @@ def tile_attend_gat_tnh_qk_ts_kernel(tc, qT, kT, vT, doT, rw, ts, qm, offs, out_
             )
             quantize(ds_r, E5, t * P, P)
 
-        qm_r = operand("qm_r")
+        qm_r = operand("qm_r", "slope_then_qm")
         for c in range(PACK):
             nc.vector.tensor_copy(
                 qm_r[0][:, c * W:(c + 1) * W].rearrange("p (c i j) -> p c j i", i=PACK, j=PACK),
@@ -182,27 +194,30 @@ def tile_attend_gat_tnh_qk_ts_kernel(tc, qT, kT, vT, doT, rw, ts, qm, offs, out_
             )
             quantize(qm_r, E4, c * P, P)
 
-        for c in range(PACK):
-            dk = product(qm_r, E4, c, ds_r, E5)
+        dk = [product(qm_r, E4, c, ds_r, E5) for c in range(PACK)]
+
+        def place(c):
             dk_listed = keep.tile([P, N], F32, name="dk_listed%d" % c)
             nc.scalar.copy(
                 dk_listed[:].rearrange("p (m t) -> p m t", t=PACK),
-                dk[:].rearrange("p (t m) -> p m t", t=PACK),
+                dk[c][:].rearrange("p (t m) -> p m t", t=PACK),
             )
-            placed = keep.tile([P, T], F32, name="placed%d" % c)
-            nc.gpsimd.memset(placed[:], 0.0)
-            nc.vector.tensor_copy(placed[:].indirect(offsets[:]), dk_listed[:])
-            nc.sync.dma_start(out_1[c * P:(c + 1) * P, :], placed[:])
+            nc.vector.tensor_copy(placed[c][:].indirect(offsets[:]), dk_listed[:])
+            nc.sync.dma_start(out_1[c * P:(c + 1) * P, :], placed[c][:])
 
-        quantize(k_i, E4)
-        ds_i = operand("ds_i")
-        gq_rows = out_0[0].rearrange("(m u) d -> m u d", u=PACK)
+        place(0)
+        ds_i = operand("ds_i", "ds_r_then_ds_i")
         for u in range(PACK):
             nc.scalar.copy(
                 ds_i[0][:, u * W:(u + 1) * W].rearrange("p (c i t) -> p c t i", i=PACK, t=PACK),
                 ds[:, :, u * P:(u + 1) * P].rearrange("p t (c i) -> p c t i", i=PACK),
             )
             quantize(ds_i, E5, u * P, P)
+        place(1)
+        place(2)
+
+        gq_rows = out_0[0].rearrange("(m u) d -> m u d", u=PACK)
+        for u in range(PACK):
             gq = product(ds_i, E5, u, k_i, E4)
             gq_out = keep.tile([P, D], F32, name="gq_out%d" % u)
             nc.scalar.copy(
@@ -210,3 +225,4 @@ def tile_attend_gat_tnh_qk_ts_kernel(tc, qT, kT, vT, doT, rw, ts, qm, offs, out_
                 gq[:].rearrange("p (j c) -> p c j", j=PACK),
             )
             nc.scalar.dma_start(gq_rows[:, u, :], gq_out[:])
+        place(3)

@@ -47,7 +47,7 @@ def tile_attend_gat_tnh_qk_ts_kernel(tc, qT, kT, vT, doT, rw, ts, qm, offs, out_
             )
 
         def product(stationary, fmt_s, block, moving, fmt_m):
-            acc = mm.tile([P, W], F32, name="acc")
+            acc = mm.tile([P, W], F32, name="acc", tag="acc")
             cols = slice(block * P, (block + 1) * P)
             nc.tensor.matmul_mx(
                 out=acc[:],
@@ -63,12 +63,12 @@ def tile_attend_gat_tnh_qk_ts_kernel(tc, qT, kT, vT, doT, rw, ts, qm, offs, out_
         def dealt(values):
             return values[:].rearrange("p (t m j) -> p m j t", t=PACK, j=PACK)
 
-        def shared_operand(name, raw, fmt, tag_scalar, tag_vector):
+        def shared_operand(name, raw, fmt, tag_vector, tag_scalar):
             codes = keep.tile([P, W], U32, name=name + "_codes", align_bytes=64)
             scales = keep.tile([P, W], U8, name=name + "_scales", align_bytes=64)
             rows = raw[:].rearrange("p j (m t) -> p m j t", t=PACK)
             halves = []
-            for h, tag, copy in ((0, tag_scalar, nc.scalar.copy), (1, tag_vector, nc.vector.tensor_copy)):
+            for h, tag, copy in ((0, tag_vector, nc.vector.tensor_copy), (1, tag_scalar, nc.scalar.copy)):
                 values = keep.tile([P, HALF * PACK], BF16, name=name + "_values%d" % h, tag=tag, align_bytes=64)
                 copy(values[:].rearrange("p (t m j) -> p m j t", t=2, j=PACK), rows[:, :, :, 2 * h:2 * h + 2])
                 halves.append(values)
@@ -113,18 +113,11 @@ def tile_attend_gat_tnh_qk_ts_kernel(tc, qT, kT, vT, doT, rw, ts, qm, offs, out_
 
         placed = [keep.tile([P, T], F32, name="placed%d" % c) for c in range(PACK)]
 
-        k_listed = keep.tile([P, PACK, N], F32, name="k_listed")
-        k_d = operand("k_d", "k_then_q_then_v")
-        k_i = operand("k_i")
+        k_listed = keep.tile([P, PACK, N], F32, name="k_listed", tag="k_then_q_then_v", align_bytes=64)
+        k_d = operand("k_d")
         for j in range(PACK):
             nc.vector.tensor_copy(k_listed[:, j, :], k_pool[j][:].indirect(offsets[:]))
-            turned = tr.tile([P, PACK, P], F32, name="turned", tag="turned")
-            for t in range(PACK):
-                nc.tensor.transpose(turned[:, t, :], k_listed[:, j, t::PACK], ident32[:])
-            nc.scalar.copy(
-                k_i[0][:, j * W:(j + 1) * W].rearrange("p (c t) -> p c t", t=PACK),
-                turned[:].rearrange("p t c -> p c t"),
-            )
+
         for c in range(PACK):
             engine = nc.vector if c < 2 else nc.gpsimd
             engine.memset(placed[c][:].bitcast(I32), 0)
@@ -146,33 +139,40 @@ def tile_attend_gat_tnh_qk_ts_kernel(tc, qT, kT, vT, doT, rw, ts, qm, offs, out_
         nc.vector.tensor_copy(dealt(k_d[0]), k_listed[:].rearrange("p j (m t) -> p m j t", t=PACK))
         quantize(k_d, E4)
 
-        q_d = shared_operand("q_d", q_raw, E4, "q_half", "k_then_q_then_v")
+        q_d = shared_operand("q_d", q_raw, E4, "k_then_q_then_v", "q_half")
 
         v_listed = keep.tile([P, PACK, N], F32, name="v_listed", tag="k_then_q_then_v", align_bytes=64)
         slope = keep.tile([P, PACK, R], F32, name="slope", tag="slope_then_qm", align_bytes=64)
-        weight = keep.tile([P, PACK, R], F32, name="weight")
-        squared = keep.tile([P, 2, R], F32, name="squared")
+        weight = keep.tile([P, PACK, R], F32, name="weight", tag="weight_then_k", align_bytes=64)
+        squared = keep.tile([P, 3, R], F32, name="squared")
         for t in range(PACK):
             score = product(k_d, E4, t, q_d, E4)
             nc.scalar.activation(weight[:, t, :], score[:], ACT.Tanh, scale=ts_col[:, t:t + 1])
-            square = squared[:, t, :] if t < 2 else v_listed[:, t, :]
+            square = squared[:, t, :] if t < 3 else v_listed[:, t, :]
             nc.scalar.activation(square, weight[:, t, :], ACT.Square)
             nc.vector.scalar_tensor_tensor(
                 slope[:, t, :], square, 1.0, rw_wide[:].rearrange("p t m -> p (t m)"), ALU.subtract, ALU.mult
             )
 
-        quantize(k_i, E4)
+        k_i_values = keep.tile([P, W * PACK], BF16, name="k_i_values", tag="weight_then_k", align_bytes=64)
+        k_planes = k_d[0][:].rearrange("p (t m j) -> p j t m", t=PACK, j=PACK)
+        for j in range(PACK):
+            turned = mm.tile([P, PACK, P], BF16, name="turned", tag="acc")
+            for t in range(PACK):
+                nc.tensor.transpose(turned[:, t, :], k_planes[:, j, t, :], ident16[:])
+            nc.scalar.copy(
+                k_i_values[:, j * W:(j + 1) * W].rearrange("p (c t) -> p c t", t=PACK),
+                turned[:].rearrange("p t c -> p c t"),
+            )
 
-        v_e = operand("v_e", "v_then_do")
         for j in range(PACK):
             nc.vector.tensor_copy(v_listed[:, j, :], v_pool[j][:].indirect(offsets[:]))
-        nc.vector.tensor_copy(dealt(v_e[0]), v_listed[:].rearrange("p j (m t) -> p m j t", t=PACK))
-        quantize(v_e, E4)
+        v_e = shared_operand("v_e", v_listed, E4, "v_then_do", "v_half")
 
-        do_e = shared_operand("do_e", do_raw, E5, "do_half", "v_then_do")
+        do_e = shared_operand("do_e", do_raw, E5, "v_then_do", "k_then_q_then_v")
 
         ds = keep.tile([P, PACK, R], BF16, name="ds")
-        ds_r = operand("ds_r", "ds_r_then_ds_i")
+        ds_r = operand("ds_r", "ds_r_then_qm")
         for t in range(PACK):
             dp = product(v_e, E4, t, do_e, E5)
             nc.vector.scalar_tensor_tensor(ds[:, t, :], dp[:], ts_col[:, t:t + 1], slope[:, t, :], ALU.mult, ALU.mult)
@@ -186,15 +186,26 @@ def tile_attend_gat_tnh_qk_ts_kernel(tc, qT, kT, vT, doT, rw, ts, qm, offs, out_
             )
             quantize(ds_r, E5, t * P, P)
 
-        qm_r = operand("qm_r", "slope_then_qm")
-        for c in range(PACK):
+        k_i = (
+            k_i_values,
+            keep.tile([P, W], U32, name="k_i_codes", tag="k_then_q_then_v", align_bytes=64),
+            keep.tile([P, W], U8, name="k_i_scales", align_bytes=64),
+        )
+        quantize(k_i, E4)
+
+        qm_first = keep.tile([P, W], BF16, name="qm_first", tag="slope_then_qm", align_bytes=64)
+        qm_later = keep.tile([P, PACK - 1, W], BF16, name="qm_later", tag="ds_r_then_qm", align_bytes=64)
+
+        def key_gradient(c):
+            values = qm_first[:] if c == 0 else qm_later[:, c - 1, :]
             nc.vector.tensor_copy(
-                qm_r[0][:, c * W:(c + 1) * W].rearrange("p (c i j) -> p c j i", i=PACK, j=PACK),
+                values.rearrange("p (c i j) -> p c j i", i=PACK, j=PACK),
                 qm_raw[:, :, c * P:(c + 1) * P].rearrange("p j (c i) -> p c j i", i=PACK),
             )
-            quantize(qm_r, E4, c * P, P)
-
-        dk = [product(qm_r, E4, c, ds_r, E5) for c in range(PACK)]
+            codes = keep.tile([P, P], U32, name="qm_codes%d" % c, tag="qm_then_ds_i" if c == 0 else "qm_codes%d" % c, align_bytes=64)
+            scales = keep.tile([P, P], U8, name="qm_scales%d" % c, align_bytes=64)
+            nc.vector.quantize_mx(out=codes[:].bitcast(E4), scales=scales[:], in_=values)
+            return product((values, codes, scales), E4, 0, ds_r, E5)
 
         def place(c):
             dk_listed = keep.tile([P, N], F32, name="dk_listed%d" % c)
@@ -205,8 +216,10 @@ def tile_attend_gat_tnh_qk_ts_kernel(tc, qT, kT, vT, doT, rw, ts, qm, offs, out_
             nc.vector.tensor_copy(placed[c][:].indirect(offsets[:]), dk_listed[:])
             nc.sync.dma_start(out_1[c * P:(c + 1) * P, :], placed[c][:])
 
+        dk = [key_gradient(0)]
         place(0)
-        ds_i = operand("ds_i", "ds_r_then_ds_i")
+        dk += [key_gradient(c) for c in range(1, PACK)]
+        ds_i = operand("ds_i", "qm_then_ds_i")
         for u in range(PACK):
             nc.scalar.copy(
                 ds_i[0][:, u * W:(u + 1) * W].rearrange("p (c i t) -> p c t i", i=PACK, t=PACK),

@@ -21,29 +21,31 @@ P = 128
 PACK = 4
 W = 512
 HALF = W // 2
+WINDOWS = 3
 
 
 def tile_attend_gat_tnh_qk_ts_kernel(tc, qT, kT, vT, doT, rw, ts, qm, offs, out_0, out_1):
     nc = tc.nc
     with ExitStack() as ctx:
         keep = ctx.enter_context(tc.tile_pool(name="keep", bufs=1))
-        stream = ctx.enter_context(tc.tile_pool(name="stream", bufs=4))
         mm = ctx.enter_context(tc.psum_pool(name="mm", bufs=4))
         tr = ctx.enter_context(tc.psum_pool(name="tr", bufs=3))
         gate = ctx.enter_context(tc.psum_pool(name="gate", bufs=1))
 
-        def operand(name, tag=None):
-            values = keep.tile([P, W * PACK], BF16, name=name + "_values", tag=tag or name, align_bytes=64)
-            codes = keep.tile([P, W], U32, name=name + "_codes", align_bytes=64)
-            scales = keep.tile([P, W], U8, name=name + "_scales", align_bytes=64)
-            return values, codes, scales
+        def quantized(name, width=W, tag=None):
+            codes = keep.tile([P, width], U32, name=name + "_codes", tag=tag or name + "_codes", align_bytes=64)
+            scales = keep.tile([P, width], U8, name=name + "_scales", align_bytes=64)
+            return codes, scales
 
-        def quantize(op, fmt, first=0, count=W):
-            values, codes, scales = op
+        def values(name, columns, tag=None):
+            return keep.tile([P, columns * PACK], BF16, name=name, tag=tag or name, align_bytes=64)
+
+        def quantize(op, fmt, first, source):
+            count = source.shape[1] // PACK
             nc.vector.quantize_mx(
-                out=codes[:, first:first + count].bitcast(fmt),
-                scales=scales[:, first:first + count],
-                in_=values[:, PACK * first:PACK * (first + count)],
+                out=op[0][:, first:first + count].bitcast(fmt),
+                scales=op[1][:, first:first + count],
+                in_=source,
             )
 
         def product(stationary, fmt_s, block, moving, fmt_m):
@@ -51,34 +53,24 @@ def tile_attend_gat_tnh_qk_ts_kernel(tc, qT, kT, vT, doT, rw, ts, qm, offs, out_
             cols = slice(block * P, (block + 1) * P)
             nc.tensor.matmul_mx(
                 out=acc[:],
-                lhsT=stationary[1][:, cols].bitcast(fmt_s),
-                lhsT_scale=stationary[2][:, cols],
-                rhs=moving[1][:].bitcast(fmt_m),
-                rhs_scale=moving[2][:],
+                lhsT=stationary[0][:, cols].bitcast(fmt_s),
+                lhsT_scale=stationary[1][:, cols],
+                rhs=moving[0][:].bitcast(fmt_m),
+                rhs_scale=moving[1][:],
                 start=True,
                 stop=True,
             )
             return acc
 
-        def dealt(values):
-            return values[:].rearrange("p (t m j) -> p m j t", t=PACK, j=PACK)
+        def interleave(copy, target, rows):
+            copy(
+                target.rearrange("p (c i j) -> p c j i", i=PACK, j=PACK),
+                rows.rearrange("p j (c i) -> p c j i", i=PACK),
+            )
 
-        def shared_operand(name, raw, fmt, tag_vector, tag_scalar):
-            codes = keep.tile([P, W], U32, name=name + "_codes", align_bytes=64)
-            scales = keep.tile([P, W], U8, name=name + "_scales", align_bytes=64)
-            rows = raw[:].rearrange("p j (m t) -> p m j t", t=PACK)
-            halves = []
-            for h, tag, copy in ((0, tag_vector, nc.vector.tensor_copy), (1, tag_scalar, nc.scalar.copy)):
-                values = keep.tile([P, HALF * PACK], BF16, name=name + "_values%d" % h, tag=tag, align_bytes=64)
-                copy(values[:].rearrange("p (t m j) -> p m j t", t=2, j=PACK), rows[:, :, :, 2 * h:2 * h + 2])
-                halves.append(values)
-            for h in range(2):
-                nc.vector.quantize_mx(
-                    out=codes[:, h * HALF:(h + 1) * HALF].bitcast(fmt),
-                    scales=scales[:, h * HALF:(h + 1) * HALF],
-                    in_=halves[h][:],
-                )
-            return halves, codes, scales
+        def gather_plane(target, j, pool_plane):
+            dealt = target[:].rearrange("p (t m j) -> p j m t", t=PACK, j=PACK)
+            nc.vector.tensor_copy(dealt[:, j, :, :], pool_plane[:].indirect(offsets[:]))
 
         offsets = keep.tile([P, N // 16], U16, name="offsets")
         nc.sync.dma_start(offsets[:], offs)
@@ -89,44 +81,40 @@ def tile_attend_gat_tnh_qk_ts_kernel(tc, qT, kT, vT, doT, rw, ts, qm, offs, out_
         rw_col = keep.tile([P, PACK], F32, name="rw_col")
 
         def load(name, shape, rows):
-            landed = stream.tile(shape, F32, name=name, tag="landed")
+            landed = keep.tile(shape, F32, name=name, tag=name, align_bytes=64)
             nc.sync.dma_start(landed[:], rows)
             return landed
 
+        def load_halves(name, rows):
+            return [load(name + "%d" % h, [P, PACK, HALF], rows[:, :, h * HALF:(h + 1) * HALF]) for h in range(2)]
+
         k_rows = kT.rearrange("(p j) t -> p j t", j=PACK)
         v_rows = vT.rearrange("(p j) t -> p j t", j=PACK)
-        q_rows = qT[0].rearrange("(p j) r -> p j r", j=PACK)
-        do_rows = doT[0].rearrange("(p j) r -> p j r", j=PACK)
         k_pool = [load("k_pool%d" % j, [P, T], k_rows[:, j, :]) for j in range(2)]
         nc.sync.dma_start(ts_pool[0:1, :], ts[0:1, :])
         nc.sync.dma_start(rw_col[:], rw[0].rearrange("(p t) o -> p (t o)", t=PACK))
         k_pool += [load("k_pool%d" % j, [P, T], k_rows[:, j, :]) for j in range(2, PACK)]
-        q_raw = load("q_raw", [P, PACK, R], q_rows)
+        q_raw = load_halves("q_raw", qT[0].rearrange("(p j) r -> p j r", j=PACK))
         v_pool = [load("v_pool%d" % j, [P, T], v_rows[:, j, :]) for j in range(PACK)]
-        do_raw = load("do_raw", [P, PACK, R], do_rows)
+        do_raw = load_halves("do_raw", doT[0].rearrange("(p j) r -> p j r", j=PACK))
         qm_raw = load("qm_raw", [P, PACK, D], qm[0].rearrange("(p j) d -> p j d", j=PACK))
 
-        ident32 = keep.tile([P, P], F32, name="ident32")
-        ident16 = keep.tile([P, P], BF16, name="ident16")
-        make_identity(nc, ident32[:])
-        make_identity(nc, ident16[:])
+        ident = keep.tile([P, P], F32, name="ident")
+        make_identity(nc, ident[:])
 
-        placed = [keep.tile([P, T], F32, name="placed%d" % c) for c in range(PACK)]
-
-        k_listed = keep.tile([P, PACK, N], F32, name="k_listed", tag="k_then_q_then_v", align_bytes=64)
-        k_d = operand("k_d")
-        for j in range(PACK):
-            nc.vector.tensor_copy(k_listed[:, j, :], k_pool[j][:].indirect(offsets[:]))
-
-        for c in range(PACK):
-            engine = nc.vector if c < 2 else nc.gpsimd
+        placed = [keep.tile([P, T], F32, name="placed%d" % c) for c in range(WINDOWS)]
+        for c in range(WINDOWS):
+            engine = nc.vector if c < 1 else nc.gpsimd
             engine.memset(placed[c][:].bitcast(I32), 0)
+
+        k_values = values("k_values", W)
+        gather_plane(k_values, 0, k_pool[0])
 
         ts_listed = keep.tile([P, N], F32, name="ts_listed")
         nc.vector.tensor_copy(ts_listed[:], ts_pool[:].indirect(offsets[:]))
         ts_turned = tr.tile([P, PACK, P], F32, name="ts_turned", tag="turned")
         for t in range(PACK):
-            nc.tensor.transpose(ts_turned[:, t, :], ts_listed[:, t::PACK], ident32[:])
+            nc.tensor.transpose(ts_turned[:, t, :], ts_listed[:, t::PACK], ident[:])
         ts_col = keep.tile([P, PACK], F32, name="ts_col")
         nc.scalar.copy(ts_col[:], ts_turned[:, :, 0])
 
@@ -134,78 +122,90 @@ def tile_attend_gat_tnh_qk_ts_kernel(tc, qT, kT, vT, doT, rw, ts, qm, offs, out_
         nc.vector.tensor_scalar(rw_neg[:], rw_col[:], -1.0, None, ALU.mult)
         rw_wide = gate.tile([P, PACK, P], F32, name="rw_wide")
         for t in range(PACK):
-            nc.tensor.transpose(rw_wide[:, t, :], rw_neg[:, t:t + 1].to_broadcast([P, P]), ident32[:])
+            nc.tensor.transpose(rw_wide[:, t, :], rw_neg[:, t:t + 1].to_broadcast([P, P]), ident[:])
 
-        nc.vector.tensor_copy(dealt(k_d[0]), k_listed[:].rearrange("p j (m t) -> p m j t", t=PACK))
-        quantize(k_d, E4)
+        for j in range(1, PACK):
+            gather_plane(k_values, j, k_pool[j])
+        k_d = quantized("k_d")
+        quantize(k_d, E4, 0, k_values[:])
 
-        q_d = shared_operand("q_d", q_raw, E4, "k_then_q_then_v", "q_half")
+        def halves(op, raw, fmt, parts):
+            interleave(nc.scalar.copy, parts[0], raw[0][:])
+            interleave(nc.vector.tensor_copy, parts[1], raw[1][:])
+            for h in range(2):
+                quantize(op, fmt, h * HALF, parts[h])
 
-        v_listed = keep.tile([P, PACK, N], F32, name="v_listed", tag="k_then_q_then_v", align_bytes=64)
-        slope = keep.tile([P, PACK, R], F32, name="slope", tag="slope_then_qm", align_bytes=64)
-        weight = keep.tile([P, PACK, R], F32, name="weight", tag="weight_then_k", align_bytes=64)
-        squared = keep.tile([P, 3, R], F32, name="squared")
+        v_values = values("v_values", W)
+        nc.vector.memset(v_values[:, 0:PACK], 1.0)
+        q_d = quantized("q_d")
+        halves(q_d, q_raw, E4, [values("q_first", HALF)[:], v_values[:, HALF * PACK:]])
+
+        k_i_values = values("k_i_values", W, "q_raw0")
+        k_words = k_values[:].bitcast(F32).rearrange("p (t m w) -> p w t m", t=PACK, w=2)
+        for w in range(2):
+            turned = tr.tile([P, PACK, P], F32, name="k_turned", tag="turned")
+            for t in range(PACK):
+                nc.tensor.transpose(turned[:, t, :], k_words[:, w, t, :], ident[:])
+            nc.scalar.copy(
+                k_i_values[:, w * 2 * W:(w + 1) * 2 * W].rearrange("p (c t) -> p c t", t=PACK),
+                turned[:].rearrange("p t c -> p (t c)").bitcast(BF16).rearrange("p (t c) -> p c t", t=PACK),
+            )
+
+        k_i = quantized("k_i")
+        slope = keep.tile([P, PACK, R], F32, name="slope", tag="slope", align_bytes=64)
+        weight = keep.tile([P, PACK, R], F32, name="weight", tag="weight", align_bytes=64)
+        squared = keep.tile([P, PACK, R], F32, name="squared")
         for t in range(PACK):
             score = product(k_d, E4, t, q_d, E4)
             nc.scalar.activation(weight[:, t, :], score[:], ACT.Tanh, scale=ts_col[:, t:t + 1])
-            square = squared[:, t, :] if t < 3 else v_listed[:, t, :]
-            nc.scalar.activation(square, weight[:, t, :], ACT.Square)
+            nc.scalar.activation(squared[:, t, :], weight[:, t, :], ACT.Square)
+            gather_plane(v_values, t, v_pool[t])
+            if t == 0:
+                quantize(k_i, E4, 0, k_i_values[:])
+            if t == PACK - 1:
+                v_e = quantized("v_e")
+                quantize(v_e, E4, 0, v_values[:])
+                do_e = quantized("do_e", tag="v_pool3")
+                halves(do_e, do_raw, E5, [values("do_first", HALF, "weight")[:], v_values[:, HALF * PACK:]])
             nc.vector.scalar_tensor_tensor(
-                slope[:, t, :], square, 1.0, rw_wide[:].rearrange("p t m -> p (t m)"), ALU.subtract, ALU.mult
+                slope[:, t, :].rearrange("p (m u) -> p m u", u=PACK),
+                squared[:, t, :].rearrange("p (m u) -> p m u", u=PACK),
+                v_values[:, t + 1:t + 2] if t < PACK - 1 else 1.0,
+                rw_wide[:].rearrange("p u m -> p m u"),
+                ALU.subtract,
+                ALU.mult,
             )
 
-        k_i_values = keep.tile([P, W * PACK], BF16, name="k_i_values", tag="weight_then_k", align_bytes=64)
-        k_planes = k_d[0][:].rearrange("p (t m j) -> p j t m", t=PACK, j=PACK)
-        for j in range(PACK):
-            turned = mm.tile([P, PACK, P], BF16, name="turned", tag="acc")
-            for t in range(PACK):
-                nc.tensor.transpose(turned[:, t, :], k_planes[:, j, t, :], ident16[:])
-            nc.scalar.copy(
-                k_i_values[:, j * W:(j + 1) * W].rearrange("p (c t) -> p c t", t=PACK),
-                turned[:].rearrange("p t c -> p c t"),
-            )
-
-        for j in range(PACK):
-            nc.vector.tensor_copy(v_listed[:, j, :], v_pool[j][:].indirect(offsets[:]))
-        v_e = shared_operand("v_e", v_listed, E4, "v_then_do", "v_half")
-
-        do_e = shared_operand("do_e", do_raw, E5, "v_then_do", "k_then_q_then_v")
-
-        ds = keep.tile([P, PACK, R], BF16, name="ds")
-        ds_r = operand("ds_r", "ds_r_then_qm")
+        ds = keep.tile([P, PACK * R], BF16, name="ds")
         for t in range(PACK):
             dp = product(v_e, E4, t, do_e, E5)
-            nc.vector.scalar_tensor_tensor(ds[:, t, :], dp[:], ts_col[:, t:t + 1], slope[:, t, :], ALU.mult, ALU.mult)
-        for t in range(PACK):
-            ds_turned = tr.tile([P, PACK, P], BF16, name="ds_turned", tag="turned")
-            for u in range(PACK):
-                nc.tensor.transpose(ds_turned[:, u, :], ds[:, t, u * P:(u + 1) * P], ident16[:])
-            nc.scalar.copy(
-                ds_r[0][:, t * W:(t + 1) * W].rearrange("p (c u) -> p c u", u=PACK),
-                ds_turned[:].rearrange("p u c -> p c u"),
+            nc.vector.scalar_tensor_tensor(
+                ds[:, t * R:(t + 1) * R], dp[:], ts_col[:, t:t + 1], slope[:, t, :], ALU.mult, ALU.mult
             )
-            quantize(ds_r, E5, t * P, P)
 
-        k_i = (
-            k_i_values,
-            keep.tile([P, W], U32, name="k_i_codes", tag="k_then_q_then_v", align_bytes=64),
-            keep.tile([P, W], U8, name="k_i_scales", align_bytes=64),
-        )
-        quantize(k_i, E4)
+        qm_all = values("qm_values", D, "do_raw0")
+        qm_values = [qm_all[:, c * W:(c + 1) * W] for c in range(PACK)]
+        interleave(nc.scalar.copy, qm_values[0], qm_raw[:, :, 0:P])
+        qm_r = quantized("qm_r", tag="slope")
 
-        qm_first = keep.tile([P, W], BF16, name="qm_first", tag="slope_then_qm", align_bytes=64)
-        qm_later = keep.tile([P, PACK - 1, W], BF16, name="qm_later", tag="ds_r_then_qm", align_bytes=64)
+        ds_r = quantized("ds_r")
+        for t in range(PACK):
+            ds_words = ds[:, t * R:(t + 1) * R].bitcast(F32)
+            ds_turned = tr.tile([P, 2, P], F32, name="ds_turned", tag="turned")
+            for w in range(2):
+                nc.tensor.transpose(ds_turned[:, w, :], ds_words[:, w::2], ident[:])
+            ds_r_values = values("ds_r_values%d" % t, P)
+            nc.scalar.copy(
+                ds_r_values[:].bitcast(F32).rearrange("p (m w) -> p m w", w=2),
+                ds_turned[:].rearrange("p w m -> p m w"),
+            )
+            quantize(ds_r, E5, t * P, ds_r_values[:])
 
         def key_gradient(c):
-            values = qm_first[:] if c == 0 else qm_later[:, c - 1, :]
-            nc.vector.tensor_copy(
-                values.rearrange("p (c i j) -> p c j i", i=PACK, j=PACK),
-                qm_raw[:, :, c * P:(c + 1) * P].rearrange("p j (c i) -> p c j i", i=PACK),
-            )
-            codes = keep.tile([P, P], U32, name="qm_codes%d" % c, tag="qm_then_ds_i" if c == 0 else "qm_codes%d" % c, align_bytes=64)
-            scales = keep.tile([P, P], U8, name="qm_scales%d" % c, align_bytes=64)
-            nc.vector.quantize_mx(out=codes[:].bitcast(E4), scales=scales[:], in_=values)
-            return product((values, codes, scales), E4, 0, ds_r, E5)
+            if c > 0:
+                interleave(nc.scalar.copy, qm_values[c], qm_raw[:, :, c * P:(c + 1) * P])
+            quantize(qm_r, E4, c * P, qm_values[c])
+            return product(qm_r, E4, c, ds_r, E5)
 
         def place(c):
             dk_listed = keep.tile([P, N], F32, name="dk_listed%d" % c)
@@ -213,29 +213,28 @@ def tile_attend_gat_tnh_qk_ts_kernel(tc, qT, kT, vT, doT, rw, ts, qm, offs, out_
                 dk_listed[:].rearrange("p (m t) -> p m t", t=PACK),
                 dk[c][:].rearrange("p (t m) -> p m t", t=PACK),
             )
-            nc.vector.tensor_copy(placed[c][:].indirect(offsets[:]), dk_listed[:])
-            nc.sync.dma_start(out_1[c * P:(c + 1) * P, :], placed[c][:])
+            window = placed[c % WINDOWS]
+            nc.vector.tensor_copy(window[:].indirect(offsets[:]), dk_listed[:])
+            nc.sync.dma_start(out_1[c * P:(c + 1) * P, :], window[:])
 
         dk = [key_gradient(0)]
         place(0)
         dk += [key_gradient(c) for c in range(1, PACK)]
-        ds_i = operand("ds_i", "qm_then_ds_i")
+        ds_i = quantized("ds_i")
+        ds_rows = ds[:].rearrange("p (t r) -> p t r", t=PACK)
         for u in range(PACK):
-            nc.scalar.copy(
-                ds_i[0][:, u * W:(u + 1) * W].rearrange("p (c i t) -> p c t i", i=PACK, t=PACK),
-                ds[:, :, u * P:(u + 1) * P].rearrange("p t (c i) -> p c t i", i=PACK),
-            )
-            quantize(ds_i, E5, u * P, P)
+            ds_i_values = values("ds_i_values%d" % u, P)
+            interleave(nc.vector.tensor_copy, ds_i_values[:], ds_rows[:, :, u * P:(u + 1) * P])
+            quantize(ds_i, E5, u * P, ds_i_values[:])
         place(1)
         place(2)
 
-        gq_rows = out_0[0].rearrange("(m u) d -> m u d", u=PACK)
         for u in range(PACK):
             gq = product(ds_i, E5, u, k_i, E4)
             gq_out = keep.tile([P, D], F32, name="gq_out%d" % u)
             nc.scalar.copy(
-                gq_out[:].rearrange("p (c j) -> p c j", j=PACK),
-                gq[:].rearrange("p (j c) -> p c j", j=PACK),
+                gq_out[:].rearrange("p (c w e) -> p c w e", w=2, e=2),
+                gq[:].rearrange("p (w c e) -> p c w e", w=2, e=2),
             )
-            nc.scalar.dma_start(gq_rows[:, u, :], gq_out[:])
+            nc.scalar.dma_start(out_0[0, u * P:(u + 1) * P, :], gq_out[:])
         place(3)

@@ -22,6 +22,7 @@ PACK = 4
 W = 512
 HALF = W // 2
 WINDOWS = 3
+RUN = 8
 
 
 def tile_attend_gat_tnh_qk_ts_kernel(tc, qT, kT, vT, doT, rw, ts, qm, offs, out_0, out_1):
@@ -68,9 +69,19 @@ def tile_attend_gat_tnh_qk_ts_kernel(tc, qT, kT, vT, doT, rw, ts, qm, offs, out_
                 rows.rearrange("p j (c i) -> p c j i", i=PACK),
             )
 
-        def gather_plane(target, j, pool_plane):
-            dealt = target[:].rearrange("p (t m j) -> p j m t", t=PACK, j=PACK)
-            nc.vector.tensor_copy(dealt[:, j, :, :], pool_plane[:].indirect(offsets[:]))
+        def gather(listed, j, pool_plane):
+            nc.vector.tensor_copy(listed[:, j * N:(j + 1) * N], pool_plane[:].indirect(offsets[:]))
+
+        def deal_and_quantize(name, listed):
+            ops = [quantized(name + "%d" % t, P) for t in range(PACK)]
+            planes = listed[:].rearrange("p (j g t h i) -> p t g h j i", j=PACK, t=PACK, h=2, i=PACK)
+            blocks = [values(name + "_values%d" % t, P) for t in range(PACK)]
+            for t in range(PACK):
+                copy = nc.vector.tensor_copy if t < 2 else nc.scalar.copy
+                copy(blocks[t][:].rearrange("p (g h i j) -> p g h j i", h=2, i=PACK, j=PACK), planes[:, t])
+            for t in range(PACK):
+                quantize(ops[t], E4, 0, blocks[t][:])
+            return ops
 
         offsets = keep.tile([P, N // 16], U16, name="offsets")
         nc.sync.dma_start(offsets[:], offs)
@@ -85,18 +96,15 @@ def tile_attend_gat_tnh_qk_ts_kernel(tc, qT, kT, vT, doT, rw, ts, qm, offs, out_
             nc.sync.dma_start(landed[:], rows)
             return landed
 
-        def load_halves(name, rows):
-            return [load(name + "%d" % h, [P, PACK, HALF], rows[:, :, h * HALF:(h + 1) * HALF]) for h in range(2)]
-
         k_rows = kT.rearrange("(p j) t -> p j t", j=PACK)
         v_rows = vT.rearrange("(p j) t -> p j t", j=PACK)
         k_pool = [load("k_pool%d" % j, [P, T], k_rows[:, j, :]) for j in range(2)]
         nc.sync.dma_start(ts_pool[0:1, :], ts[0:1, :])
         nc.sync.dma_start(rw_col[:], rw[0].rearrange("(p t) o -> p (t o)", t=PACK))
         k_pool += [load("k_pool%d" % j, [P, T], k_rows[:, j, :]) for j in range(2, PACK)]
-        q_raw = load_halves("q_raw", qT[0].rearrange("(p j) r -> p j r", j=PACK))
+        q_raw = load("q_raw", [P, PACK, R], qT[0].rearrange("(p j) r -> p j r", j=PACK))
+        do_raw = load("do_raw", [P, PACK, R], doT[0].rearrange("(p j) r -> p j r", j=PACK))
         v_pool = [load("v_pool%d" % j, [P, T], v_rows[:, j, :]) for j in range(PACK)]
-        do_raw = load_halves("do_raw", doT[0].rearrange("(p j) r -> p j r", j=PACK))
         qm_raw = load("qm_raw", [P, PACK, D], qm[0].rearrange("(p j) d -> p j d", j=PACK))
 
         ident = keep.tile([P, P], F32, name="ident")
@@ -108,13 +116,19 @@ def tile_attend_gat_tnh_qk_ts_kernel(tc, qT, kT, vT, doT, rw, ts, qm, offs, out_
             engine.memset(placed[c][:].bitcast(I32), 0)
 
         k_values = values("k_values", W)
-        gather_plane(k_values, 0, k_pool[0])
+        k_dealt = k_values[:].rearrange("p (t g a j) -> p j g t a", t=PACK, a=RUN, j=PACK)
+        nc.vector.tensor_copy(k_dealt[:, 0], k_pool[0][:].indirect(offsets[:]))
 
         ts_listed = keep.tile([P, N], F32, name="ts_listed")
         nc.vector.tensor_copy(ts_listed[:], ts_pool[:].indirect(offsets[:]))
+        ts_dealt = keep.tile([P, PACK, P], F32, name="ts_dealt")
+        nc.scalar.copy(
+            ts_dealt[:].rearrange("p t (g a) -> p t g a", a=RUN),
+            ts_listed[:].rearrange("p (g t a) -> p t g a", t=PACK, a=RUN),
+        )
         ts_turned = tr.tile([P, PACK, P], F32, name="ts_turned", tag="turned")
         for t in range(PACK):
-            nc.tensor.transpose(ts_turned[:, t, :], ts_listed[:, t::PACK], ident[:])
+            nc.tensor.transpose(ts_turned[:, t, :], ts_dealt[:, t, :], ident[:])
         ts_col = keep.tile([P, PACK], F32, name="ts_col")
         nc.scalar.copy(ts_col[:], ts_turned[:, :, 0])
 
@@ -125,25 +139,52 @@ def tile_attend_gat_tnh_qk_ts_kernel(tc, qT, kT, vT, doT, rw, ts, qm, offs, out_
             nc.tensor.transpose(rw_wide[:, t, :], rw_neg[:, t:t + 1].to_broadcast([P, P]), ident[:])
 
         for j in range(1, PACK):
-            gather_plane(k_values, j, k_pool[j])
+            nc.vector.tensor_copy(k_dealt[:, j], k_pool[j][:].indirect(offsets[:]))
         k_d = quantized("k_d")
         quantize(k_d, E4, 0, k_values[:])
 
-        def halves(op, raw, fmt, parts):
-            interleave(nc.scalar.copy, parts[0], raw[0][:])
-            interleave(nc.vector.tensor_copy, parts[1], raw[1][:])
+        v_listed = keep.tile([P, PACK * N], F32, name="v_listed", tag="listed", align_bytes=64)
+        parts = [values("half%d" % h, HALF, "half%d" % h) for h in range(2)]
+
+        def halves(name, raw, fmt):
+            op = quantized(name)
+            interleave(nc.vector.tensor_copy, parts[0][:], raw[:, :, :HALF])
+            interleave(nc.scalar.copy, parts[1][:], raw[:, :, HALF:])
             for h in range(2):
-                quantize(op, fmt, h * HALF, parts[h])
+                quantize(op, fmt, h * HALF, parts[h][:])
+            return op
 
-        v_values = values("v_values", W)
-        nc.vector.memset(v_values[:, 0:PACK], 1.0)
-        q_d = quantized("q_d")
-        halves(q_d, q_raw, E4, [values("q_first", HALF)[:], v_values[:, HALF * PACK:]])
+        q_d = halves("q_d", q_raw, E4)
+        do_e = quantized("do_e")
+        do_values = values("do_values", R, "half1")
+        interleave(nc.vector.tensor_copy, do_values[:], do_raw[:])
+        quantize(do_e, E5, 0, do_values[:])
 
-        k_i_values = values("k_i_values", W, "q_raw0")
+        slope = keep.tile([P, PACK, R], F32, name="slope", tag="slope", align_bytes=64)
+        weight = keep.tile([P, PACK, R], F32, name="weight", tag="weight", align_bytes=64)
+        squared = keep.tile([P, 2, R], F32, name="squared")
+        squares = [squared[:, t, :] for t in range(2)] + [v_listed[:, t * N:(t + 1) * N] for t in range(2, PACK)]
+        for t in range(PACK):
+            score = product(k_d, E4, t, q_d, E4)
+            nc.scalar.activation(weight[:, t, :], score[:], ACT.Tanh, scale=ts_col[:, t:t + 1])
+            nc.scalar.activation(squares[t], weight[:, t, :], ACT.Square)
+            if t == 0:
+                gather(v_listed, 0, v_pool[0])
+            nc.vector.scalar_tensor_tensor(
+                slope[:, t, :].rearrange("p (m u) -> p m u", u=PACK),
+                squares[t].rearrange("p (m u) -> p m u", u=PACK),
+                1.0,
+                rw_wide[:].rearrange("p u m -> p m u"),
+                ALU.subtract,
+                ALU.mult,
+            )
+            if t > 0:
+                gather(v_listed, t, v_pool[t])
+
         k_words = k_values[:].bitcast(F32).rearrange("p (t m w) -> p w t m", t=PACK, w=2)
+        k_i_values = values("k_i_values", W, "weight")
         for w in range(2):
-            turned = tr.tile([P, PACK, P], F32, name="k_turned", tag="turned")
+            turned = mm.tile([P, PACK, P], F32, name="k_turned", tag="acc")
             for t in range(PACK):
                 nc.tensor.transpose(turned[:, t, :], k_words[:, w, t, :], ident[:])
             nc.scalar.copy(
@@ -151,39 +192,18 @@ def tile_attend_gat_tnh_qk_ts_kernel(tc, qT, kT, vT, doT, rw, ts, qm, offs, out_
                 turned[:].rearrange("p t c -> p (t c)").bitcast(BF16).rearrange("p (t c) -> p c t", t=PACK),
             )
 
+        v_e = deal_and_quantize("v_e", v_listed)
         k_i = quantized("k_i")
-        slope = keep.tile([P, PACK, R], F32, name="slope", tag="slope", align_bytes=64)
-        weight = keep.tile([P, PACK, R], F32, name="weight", tag="weight", align_bytes=64)
-        squared = keep.tile([P, PACK, R], F32, name="squared")
-        for t in range(PACK):
-            score = product(k_d, E4, t, q_d, E4)
-            nc.scalar.activation(weight[:, t, :], score[:], ACT.Tanh, scale=ts_col[:, t:t + 1])
-            nc.scalar.activation(squared[:, t, :], weight[:, t, :], ACT.Square)
-            gather_plane(v_values, t, v_pool[t])
-            if t == 0:
-                quantize(k_i, E4, 0, k_i_values[:])
-            if t == PACK - 1:
-                v_e = quantized("v_e")
-                quantize(v_e, E4, 0, v_values[:])
-                do_e = quantized("do_e", tag="v_pool3")
-                halves(do_e, do_raw, E5, [values("do_first", HALF, "weight")[:], v_values[:, HALF * PACK:]])
-            nc.vector.scalar_tensor_tensor(
-                slope[:, t, :].rearrange("p (m u) -> p m u", u=PACK),
-                squared[:, t, :].rearrange("p (m u) -> p m u", u=PACK),
-                v_values[:, t + 1:t + 2] if t < PACK - 1 else 1.0,
-                rw_wide[:].rearrange("p u m -> p m u"),
-                ALU.subtract,
-                ALU.mult,
-            )
+        quantize(k_i, E4, 0, k_i_values[:])
 
         ds = keep.tile([P, PACK * R], BF16, name="ds")
         for t in range(PACK):
-            dp = product(v_e, E4, t, do_e, E5)
+            dp = product(v_e[t], E4, 0, do_e, E5)
             nc.vector.scalar_tensor_tensor(
                 ds[:, t * R:(t + 1) * R], dp[:], ts_col[:, t:t + 1], slope[:, t, :], ALU.mult, ALU.mult
             )
 
-        qm_all = values("qm_values", D, "do_raw0")
+        qm_all = values("qm_values", D, "v_pool3")
         qm_values = [qm_all[:, c * W:(c + 1) * W] for c in range(PACK)]
         interleave(nc.scalar.copy, qm_values[0], qm_raw[:, :, 0:P])
         qm_r = quantized("qm_r", tag="slope")
@@ -210,8 +230,8 @@ def tile_attend_gat_tnh_qk_ts_kernel(tc, qT, kT, vT, doT, rw, ts, qm, offs, out_
         def place(c):
             dk_listed = keep.tile([P, N], F32, name="dk_listed%d" % c)
             nc.scalar.copy(
-                dk_listed[:].rearrange("p (m t) -> p m t", t=PACK),
-                dk[c][:].rearrange("p (t m) -> p m t", t=PACK),
+                dk_listed[:].rearrange("p (g t a) -> p g t a", t=PACK, a=RUN),
+                dk[c][:].rearrange("p (t g a) -> p g t a", t=PACK, a=RUN),
             )
             window = placed[c % WINDOWS]
             nc.vector.tensor_copy(window[:].indirect(offsets[:]), dk_listed[:])

@@ -22,16 +22,16 @@ PACK = 4
 W = 512
 HALF = W // 2
 WINDOWS = 3
-RUN = 8
 
 
 def tile_attend_gat_tnh_qk_ts_kernel(tc, qT, kT, vT, doT, rw, ts, qm, offs, out_0, out_1):
     nc = tc.nc
     with ExitStack() as ctx:
         keep = ctx.enter_context(tc.tile_pool(name="keep", bufs=1))
-        mm = ctx.enter_context(tc.psum_pool(name="mm", bufs=4))
-        tr = ctx.enter_context(tc.psum_pool(name="tr", bufs=3))
-        gate = ctx.enter_context(tc.psum_pool(name="gate", bufs=1))
+        psum = ctx.enter_context(tc.psum_pool(name="psum", bufs=1))
+
+        def bank(number, shape):
+            return psum.tile(shape, F32, name="bank%d" % number, tag="bank%d" % number)
 
         def quantized(name, width=W, tag=None):
             codes = keep.tile([P, width], U32, name=name + "_codes", tag=tag or name + "_codes", align_bytes=64)
@@ -49,15 +49,15 @@ def tile_attend_gat_tnh_qk_ts_kernel(tc, qT, kT, vT, doT, rw, ts, qm, offs, out_
                 in_=source,
             )
 
-        def product(stationary, fmt_s, block, moving, fmt_m):
-            acc = mm.tile([P, W], F32, name="acc", tag="acc")
+        def product(number, stationary, fmt_s, block, moving, fmt_m, first=0):
+            acc = bank(number, [P, W])
             cols = slice(block * P, (block + 1) * P)
             nc.tensor.matmul_mx(
                 out=acc[:],
                 lhsT=stationary[0][:, cols].bitcast(fmt_s),
                 lhsT_scale=stationary[1][:, cols],
-                rhs=moving[0][:].bitcast(fmt_m),
-                rhs_scale=moving[1][:],
+                rhs=moving[0][:, first:first + W].bitcast(fmt_m),
+                rhs_scale=moving[1][:, first:first + W],
                 start=True,
                 stop=True,
             )
@@ -69,22 +69,20 @@ def tile_attend_gat_tnh_qk_ts_kernel(tc, qT, kT, vT, doT, rw, ts, qm, offs, out_
                 rows.rearrange("p j (c i) -> p c j i", i=PACK),
             )
 
-        def gather(listed, j, pool_plane):
-            nc.vector.tensor_copy(listed[:, j * N:(j + 1) * N], pool_plane[:].indirect(offsets[:]))
-
-        def deal_and_quantize(name, listed):
-            ops = [quantized(name + "%d" % t, P) for t in range(PACK)]
-            planes = listed[:].rearrange("p (j g t h i) -> p t g h j i", j=PACK, t=PACK, h=2, i=PACK)
-            blocks = [values(name + "_values%d" % t, P) for t in range(PACK)]
-            for t in range(PACK):
-                copy = nc.vector.tensor_copy if t < 2 else nc.scalar.copy
-                copy(blocks[t][:].rearrange("p (g h i j) -> p g h j i", h=2, i=PACK, j=PACK), planes[:, t])
-            for t in range(PACK):
-                quantize(ops[t], E4, 0, blocks[t][:])
-            return ops
+        def turn(source, target, banks):
+            words = source[:].bitcast(F32).rearrange("p (s i w) -> p w i s", i=PACK, w=2)
+            for w in range(2):
+                turned = bank(banks[w], [P, PACK, P])
+                for i in range(PACK):
+                    nc.tensor.transpose(turned[:, i, :], words[:, w, i, :], ident[:])
+                nc.scalar.copy(
+                    target[:, w * 2 * W:(w + 1) * 2 * W].rearrange("s (e p i) -> s e p i", e=2, i=PACK),
+                    turned[:].rearrange("s i p -> s (i p)").bitcast(BF16).rearrange("s (i p e) -> s e p i", i=PACK, e=2),
+                )
 
         offsets = keep.tile([P, N // 16], U16, name="offsets")
         nc.sync.dma_start(offsets[:], offs)
+        list_halves = [offsets[:, h * HALF // 16:(h + 1) * HALF // 16] for h in range(2)]
 
         ts_pool = keep.tile([P, T], F32, name="ts_pool")
         nc.vector.memset(ts_pool[:].bitcast(I32), 0)
@@ -116,145 +114,148 @@ def tile_attend_gat_tnh_qk_ts_kernel(tc, qT, kT, vT, doT, rw, ts, qm, offs, out_
             engine.memset(placed[c][:].bitcast(I32), 0)
 
         k_values = values("k_values", W)
-        k_dealt = k_values[:].rearrange("p (t g a j) -> p j g t a", t=PACK, a=RUN, j=PACK)
-        nc.vector.tensor_copy(k_dealt[:, 0], k_pool[0][:].indirect(offsets[:]))
+        k_planes = k_values[:].rearrange("p (s j) -> p j s", j=PACK)
+        nc.vector.tensor_copy(k_planes[:, 0, :], k_pool[0][:].indirect(offsets[:]))
 
         ts_listed = keep.tile([P, N], F32, name="ts_listed")
         nc.vector.tensor_copy(ts_listed[:], ts_pool[:].indirect(offsets[:]))
-        ts_dealt = keep.tile([P, PACK, P], F32, name="ts_dealt")
-        nc.scalar.copy(
-            ts_dealt[:].rearrange("p t (g a) -> p t g a", a=RUN),
-            ts_listed[:].rearrange("p (g t a) -> p t g a", t=PACK, a=RUN),
-        )
-        ts_turned = tr.tile([P, PACK, P], F32, name="ts_turned", tag="turned")
+        ts_turned = bank(5, [P, PACK, P])
         for t in range(PACK):
-            nc.tensor.transpose(ts_turned[:, t, :], ts_dealt[:, t, :], ident[:])
+            nc.tensor.transpose(ts_turned[:, t, :], ts_listed[:, t * P:(t + 1) * P], ident[:])
         ts_col = keep.tile([P, PACK], F32, name="ts_col")
         nc.scalar.copy(ts_col[:], ts_turned[:, :, 0])
 
         rw_neg = keep.tile([P, PACK], F32, name="rw_neg")
         nc.vector.tensor_scalar(rw_neg[:], rw_col[:], -1.0, None, ALU.mult)
-        rw_wide = gate.tile([P, PACK, P], F32, name="rw_wide")
+        rw_wide = bank(4, [P, PACK, P])
         for t in range(PACK):
             nc.tensor.transpose(rw_wide[:, t, :], rw_neg[:, t:t + 1].to_broadcast([P, P]), ident[:])
 
         for j in range(1, PACK):
-            nc.vector.tensor_copy(k_dealt[:, j], k_pool[j][:].indirect(offsets[:]))
+            nc.vector.tensor_copy(k_planes[:, j, :], k_pool[j][:].indirect(offsets[:]))
         k_d = quantized("k_d")
         quantize(k_d, E4, 0, k_values[:])
 
-        v_listed = keep.tile([P, PACK * N], F32, name="v_listed", tag="listed", align_bytes=64)
-        parts = [values("half%d" % h, HALF, "half%d" % h) for h in range(2)]
+        q_d = quantized("q_d")
+        q_parts = [values("q_half%d" % h, HALF) for h in range(2)]
+        interleave(nc.vector.tensor_copy, q_parts[0][:], q_raw[:, :, :HALF])
+        interleave(nc.scalar.copy, q_parts[1][:], q_raw[:, :, HALF:])
+        for h in range(2):
+            quantize(q_d, E4, h * HALF, q_parts[h][:])
 
-        def halves(name, raw, fmt):
-            op = quantized(name)
-            interleave(nc.vector.tensor_copy, parts[0][:], raw[:, :, :HALF])
-            interleave(nc.scalar.copy, parts[1][:], raw[:, :, HALF:])
-            for h in range(2):
-                quantize(op, fmt, h * HALF, parts[h][:])
-            return op
-
-        q_d = halves("q_d", q_raw, E4)
-        do_e = quantized("do_e")
-        do_values = values("do_values", R, "half1")
+        grads = quantized("do_then_ds_r", 2 * W)
+        do_values = values("do_values", R, "q_half1")
         interleave(nc.vector.tensor_copy, do_values[:], do_raw[:])
-        quantize(do_e, E5, 0, do_values[:])
+        quantize(grads, E5, 0, do_values[:])
 
-        slope = keep.tile([P, PACK, R], F32, name="slope", tag="slope", align_bytes=64)
+        v_listed = keep.tile([P, PACK * N], F32, name="v_listed", tag="v_listed", align_bytes=64)
+
+        def gather_values(j):
+            nc.vector.tensor_copy(v_listed[:, j * N:(j + 1) * N], v_pool[j][:].indirect(offsets[:]))
+
+        slope = [keep.tile([P, R], F32, name="slope%d" % t, tag="slope%d" % t, align_bytes=64) for t in range(PACK)]
         weight = keep.tile([P, PACK, R], F32, name="weight", tag="weight", align_bytes=64)
         squared = keep.tile([P, 2, R], F32, name="squared")
         squares = [squared[:, t, :] for t in range(2)] + [v_listed[:, t * N:(t + 1) * N] for t in range(2, PACK)]
         for t in range(PACK):
-            score = product(k_d, E4, t, q_d, E4)
+            score = product(t, k_d, E4, t, q_d, E4)
             nc.scalar.activation(weight[:, t, :], score[:], ACT.Tanh, scale=ts_col[:, t:t + 1])
             nc.scalar.activation(squares[t], weight[:, t, :], ACT.Square)
             if t == 0:
-                gather(v_listed, 0, v_pool[0])
+                gather_values(0)
             nc.vector.scalar_tensor_tensor(
-                slope[:, t, :].rearrange("p (m u) -> p m u", u=PACK),
+                slope[t][:].rearrange("p (m u) -> p m u", u=PACK),
                 squares[t].rearrange("p (m u) -> p m u", u=PACK),
                 1.0,
                 rw_wide[:].rearrange("p u m -> p m u"),
                 ALU.subtract,
                 ALU.mult,
             )
-            if t > 0:
-                gather(v_listed, t, v_pool[t])
+            if 0 < t < PACK - 1:
+                gather_values(t)
 
-        k_words = k_values[:].bitcast(F32).rearrange("p (t m w) -> p w t m", t=PACK, w=2)
         k_i_values = values("k_i_values", W, "weight")
-        for w in range(2):
-            turned = mm.tile([P, PACK, P], F32, name="k_turned", tag="acc")
-            for t in range(PACK):
-                nc.tensor.transpose(turned[:, t, :], k_words[:, w, t, :], ident[:])
-            nc.scalar.copy(
-                k_i_values[:, w * 2 * W:(w + 1) * 2 * W].rearrange("p (c t) -> p c t", t=PACK),
-                turned[:].rearrange("p t c -> p (t c)").bitcast(BF16).rearrange("p (t c) -> p c t", t=PACK),
+        turn(k_values, k_i_values, (0, 1))
+
+        last = (PACK - 1) * N
+        for h in range(2):
+            nc.vector.tensor_copy(
+                v_listed[:, last + h * HALF:last + (h + 1) * HALF], v_pool[PACK - 1][:].indirect(list_halves[h])
             )
-
-        v_e = deal_and_quantize("v_e", v_listed)
-        k_i = quantized("k_i")
-        quantize(k_i, E4, 0, k_i_values[:])
-
-        ds = keep.tile([P, PACK * R], BF16, name="ds")
+        v_rows_listed = v_listed[:].rearrange("p (j s) -> p j s", j=PACK)
+        v_e = []
+        v_values = [values("v_values%d" % t, P) for t in range(PACK)]
         for t in range(PACK):
-            dp = product(v_e[t], E4, 0, do_e, E5)
-            nc.vector.scalar_tensor_tensor(
-                ds[:, t * R:(t + 1) * R], dp[:], ts_col[:, t:t + 1], slope[:, t, :], ALU.mult, ALU.mult
-            )
-
-        qm_all = values("qm_values", D, "v_pool3")
-        qm_values = [qm_all[:, c * W:(c + 1) * W] for c in range(PACK)]
-        interleave(nc.scalar.copy, qm_values[0], qm_raw[:, :, 0:P])
-        qm_r = quantized("qm_r", tag="slope")
-
-        ds_r = quantized("ds_r")
+            copy = nc.vector.tensor_copy if t == 1 else nc.scalar.copy
+            interleave(copy, v_values[t][:], v_rows_listed[:, :, t * P:(t + 1) * P])
         for t in range(PACK):
-            ds_words = ds[:, t * R:(t + 1) * R].bitcast(F32)
-            ds_turned = tr.tile([P, 2, P], F32, name="ds_turned", tag="turned")
+            v_e.append(quantized("v_e%d" % t, P))
+            quantize(v_e[t], E4, 0, v_values[t][:])
+
+        ds = [keep.tile([P, R], BF16, name="ds%d" % t) for t in range(PACK)]
+        for t in range(PACK):
+            dp = product(t, v_e[t], E4, 0, grads, E5)
+            nc.vector.scalar_tensor_tensor(ds[t][:], dp[:], ts_col[:, t:t + 1], slope[t][:], ALU.mult, ALU.mult)
+
+        qm_values = values("qm_values", D, "v_pool3")
+        qm_r = [quantized("qm_r%d" % c, P, "slope%d" % (c - 1) if c else None) for c in range(PACK)]
+
+        def quantize_qm(c):
+            interleave(nc.scalar.copy, qm_values[:, c * W:(c + 1) * W], qm_raw[:, :, c * P:(c + 1) * P])
+            quantize(qm_r[c], E4, 0, qm_values[:, c * W:(c + 1) * W])
+
+        ds_r_values = values("ds_r_values", W)
+
+        def quantize_ds_r(t):
+            ds_words = ds[t][:].bitcast(F32)
+            ds_turned = bank((5, 6, 7, 4)[t], [P, 2, P])
             for w in range(2):
                 nc.tensor.transpose(ds_turned[:, w, :], ds_words[:, w::2], ident[:])
-            ds_r_values = values("ds_r_values%d" % t, P)
-            nc.scalar.copy(
-                ds_r_values[:].bitcast(F32).rearrange("p (m w) -> p m w", w=2),
-                ds_turned[:].rearrange("p w m -> p m w"),
-            )
-            quantize(ds_r, E5, t * P, ds_r_values[:])
+            block = ds_r_values[:, t * W:(t + 1) * W]
+            nc.scalar.copy(block.bitcast(F32).rearrange("p (m w) -> p m w", w=2), ds_turned[:].rearrange("p w m -> p m w"))
+            quantize(grads, E5, W + t * P, block)
 
-        def key_gradient(c):
-            if c > 0:
-                interleave(nc.scalar.copy, qm_values[c], qm_raw[:, :, c * P:(c + 1) * P])
-            quantize(qm_r, E4, c * P, qm_values[c])
-            return product(qm_r, E4, c, ds_r, E5)
+        def store(c):
+            nc.sync.dma_start(out_1[c * P:(c + 1) * P, :], placed[c % WINDOWS][:])
 
-        def place(c):
-            dk_listed = keep.tile([P, N], F32, name="dk_listed%d" % c)
-            nc.scalar.copy(
-                dk_listed[:].rearrange("p (g t a) -> p g t a", t=PACK, a=RUN),
-                dk[c][:].rearrange("p (t g a) -> p g t a", t=PACK, a=RUN),
-            )
-            window = placed[c % WINDOWS]
-            nc.vector.tensor_copy(window[:].indirect(offsets[:]), dk_listed[:])
-            nc.sync.dma_start(out_1[c * P:(c + 1) * P, :], window[:])
+        def place(c, number, tag=None):
+            dk = product(number, qm_r[c], E4, 0, grads, E5, W)
+            dk_listed = keep.tile([P, N], F32, name="dk_listed%d" % c, tag=tag or "dk_listed%d" % c, align_bytes=64)
+            nc.scalar.copy(dk_listed[:], dk[:])
+            nc.vector.tensor_copy(placed[c % WINDOWS][:].indirect(offsets[:]), dk_listed[:])
+            store(c)
 
-        dk = [key_gradient(0)]
-        place(0)
-        dk += [key_gradient(c) for c in range(1, PACK)]
+        def place_half(h):
+            dk = product(h, qm_r[0], E4, 0, grads, E5, HALF * (h + 1))
+            dk_listed = keep.tile([P, HALF], F32, name="dk_half%d" % h)
+            nc.scalar.copy(dk_listed[:], dk[:, HALF:])
+            nc.vector.tensor_copy(placed[0][:].indirect(list_halves[h]), dk_listed[:])
+
+        quantize_qm(0)
+        for h in range(2):
+            quantize_ds_r(2 * h)
+            quantize_ds_r(2 * h + 1)
+            place_half(h)
+        store(0)
+        for c in range(1, PACK):
+            quantize_qm(c)
+        place(1, 2)
+        k_i = quantized("k_i", tag="slope3")
+        quantize(k_i, E4, 0, k_i_values[:])
+
+        ds_i_values = values("ds_i_values", W)
+        turn(ds_r_values, ds_i_values, (1, 2))
         ds_i = quantized("ds_i")
-        ds_rows = ds[:].rearrange("p (t r) -> p t r", t=PACK)
-        for u in range(PACK):
-            ds_i_values = values("ds_i_values%d" % u, P)
-            interleave(nc.vector.tensor_copy, ds_i_values[:], ds_rows[:, :, u * P:(u + 1) * P])
-            quantize(ds_i, E5, u * P, ds_i_values[:])
-        place(1)
-        place(2)
+        quantize(ds_i, E5, 0, ds_i_values[:])
+        place(2, 3, "ds_r_values")
 
+        gq_rows = out_0[0].rearrange("(m u) d -> m u d", u=PACK)
         for u in range(PACK):
-            gq = product(ds_i, E5, u, k_i, E4)
+            gq = product((0, 4, 6, 7)[u], ds_i, E5, u, k_i, E4)
             gq_out = keep.tile([P, D], F32, name="gq_out%d" % u)
             nc.scalar.copy(
-                gq_out[:].rearrange("p (c w e) -> p c w e", w=2, e=2),
-                gq[:].rearrange("p (w c e) -> p c w e", w=2, e=2),
+                gq_out[:].rearrange("p (c j) -> p c j", j=PACK),
+                gq[:].rearrange("p (j c) -> p c j", j=PACK),
             )
-            nc.scalar.dma_start(out_0[0, u * P:(u + 1) * P, :], gq_out[:])
-        place(3)
+            nc.scalar.dma_start(gq_rows[:, u, :], gq_out[:])
+        place(3, 5)

@@ -69,16 +69,15 @@ def tile_attend_gat_tnh_qk_ts_kernel(tc, qT, kT, vT, doT, rw, ts, qm, offs, out_
                 rows.rearrange("p j (c i) -> p c j i", i=PACK),
             )
 
-        def turn(source, target, banks):
+        def turn(source, w, target, number):
             words = source[:].bitcast(F32).rearrange("p (s i w) -> p w i s", i=PACK, w=2)
-            for w in range(2):
-                turned = bank(banks[w], [P, PACK, P])
-                for i in range(PACK):
-                    nc.tensor.transpose(turned[:, i, :], words[:, w, i, :], ident[:])
-                nc.scalar.copy(
-                    target[:, w * 2 * W:(w + 1) * 2 * W].rearrange("s (e p i) -> s e p i", e=2, i=PACK),
-                    turned[:].rearrange("s i p -> s (i p)").bitcast(BF16).rearrange("s (i p e) -> s e p i", i=PACK, e=2),
-                )
+            turned = bank(number, [P, PACK, P])
+            for i in range(PACK):
+                nc.tensor.transpose(turned[:, i, :], words[:, w, i, :], ident[:])
+            nc.scalar.copy(
+                target.rearrange("s (e p i) -> s e p i", e=2, i=PACK),
+                turned[:].rearrange("s i p -> s (i p)").bitcast(BF16).rearrange("s (i p e) -> s e p i", i=PACK, e=2),
+            )
 
         offsets = keep.tile([P, N // 16], U16, name="offsets")
         nc.sync.dma_start(offsets[:], offs)
@@ -143,6 +142,9 @@ def tile_attend_gat_tnh_qk_ts_kernel(tc, qT, kT, vT, doT, rw, ts, qm, offs, out_
         for h in range(2):
             quantize(q_d, E4, h * HALF, q_parts[h][:])
 
+        k_i_first = values("k_i_first", HALF, "q_raw")
+        turn(k_values, 0, k_i_first[:], 6)
+
         grads = quantized("do_then_ds_r", 2 * W)
         do_values = values("do_values", R, "q_half1")
         interleave(nc.vector.tensor_copy, do_values[:], do_raw[:])
@@ -174,8 +176,8 @@ def tile_attend_gat_tnh_qk_ts_kernel(tc, qT, kT, vT, doT, rw, ts, qm, offs, out_
             if 0 < t < PACK - 1:
                 gather_values(t)
 
-        k_i_values = values("k_i_values", W, "weight")
-        turn(k_values, k_i_values, (0, 1))
+        k_i_second = values("k_i_second", HALF, "weight")
+        turn(k_values, 1, k_i_second[:], 0)
 
         last = (PACK - 1) * N
         for h in range(2):
@@ -241,10 +243,12 @@ def tile_attend_gat_tnh_qk_ts_kernel(tc, qT, kT, vT, doT, rw, ts, qm, offs, out_
             quantize_qm(c)
         place(1, 2)
         k_i = quantized("k_i", tag="slope3")
-        quantize(k_i, E4, 0, k_i_values[:])
+        quantize(k_i, E4, 0, k_i_first[:])
+        quantize(k_i, E4, HALF, k_i_second[:])
 
         ds_i_values = values("ds_i_values", W)
-        turn(ds_r_values, ds_i_values, (1, 2))
+        for w in range(2):
+            turn(ds_r_values, w, ds_i_values[:, w * 2 * W:(w + 1) * 2 * W], 1 + w)
         ds_i = quantized("ds_i")
         quantize(ds_i, E5, 0, ds_i_values[:])
         place(2, 3, "ds_r_values")

@@ -147,24 +147,30 @@ def tile_attend_gat_tnh_qk_ts_kernel(tc, qT, kT, vT, doT, rw, ts, qm, offs, out_
 
         grads = quantized("do_then_ds_r", 2 * W)
         do_values = values("do_values", R, "q_half1")
-        interleave(nc.vector.tensor_copy, do_values[:], do_raw[:])
-        quantize(grads, E5, 0, do_values[:])
+        share = R - P
+        interleave(nc.scalar.copy, do_values[:, share * PACK:], do_raw[:, :, share:])
+        for first, end in ((0, HALF), (HALF, share)):
+            interleave(nc.vector.tensor_copy, do_values[:, first * PACK:end * PACK], do_raw[:, :, first:end])
+        for h in range(2):
+            quantize(grads, E5, h * HALF, do_values[:, h * 2 * W:(h + 1) * 2 * W])
 
         v_listed = keep.tile([P, PACK * N], F32, name="v_listed", tag="v_listed", align_bytes=64)
 
         def gather_values(j):
             nc.vector.tensor_copy(v_listed[:, j * N:(j + 1) * N], v_pool[j][:].indirect(offsets[:]))
 
-        slope = [keep.tile([P, R], F32, name="slope%d" % t, tag="slope%d" % t, align_bytes=64) for t in range(PACK)]
+        slope_tags = ("slope0", "slope1", "slope2", "v_pool2")
+        slope = []
         weight = keep.tile([P, PACK, R], F32, name="weight", tag="weight", align_bytes=64)
-        squared = keep.tile([P, 2, R], F32, name="squared")
-        squares = [squared[:, t, :] for t in range(2)] + [v_listed[:, t * N:(t + 1) * N] for t in range(2, PACK)]
+        squared = keep.tile([P, 3, R], F32, name="squared")
+        squares = [squared[:, 0, :], squared[:, 1, :], v_listed[:, 3 * N - P:3 * N - P + R], squared[:, 2, :]]
         for t in range(PACK):
             score = product(t, k_d, E4, t, q_d, E4)
             nc.scalar.activation(weight[:, t, :], score[:], ACT.Tanh, scale=ts_col[:, t:t + 1])
             nc.scalar.activation(squares[t], weight[:, t, :], ACT.Square)
             if t == 0:
                 gather_values(0)
+            slope.append(keep.tile([P, R], F32, name="slope%d" % t, tag=slope_tags[t], align_bytes=64))
             nc.vector.scalar_tensor_tensor(
                 slope[t][:].rearrange("p (m u) -> p m u", u=PACK),
                 squares[t].rearrange("p (m u) -> p m u", u=PACK),
@@ -242,7 +248,7 @@ def tile_attend_gat_tnh_qk_ts_kernel(tc, qT, kT, vT, doT, rw, ts, qm, offs, out_
         for c in range(1, PACK):
             quantize_qm(c)
         place(1, 2)
-        k_i = quantized("k_i", tag="slope3")
+        k_i = quantized("k_i", tag=slope_tags[3])
         quantize(k_i, E4, 0, k_i_first[:])
         quantize(k_i, E4, HALF, k_i_second[:])
 

@@ -63,10 +63,16 @@ def tile_attend_gat_tnh_qk_ts_kernel(tc, qT, kT, vT, doT, rw, ts, qm, offs, out_
             )
             return acc
 
-        def interleave(copy, target, rows):
+        def interleave(copy, target, rows, run=PACK):
             copy(
-                target.rearrange("p (c i j) -> p c j i", i=PACK, j=PACK),
-                rows.rearrange("p j (c i) -> p c j i", i=PACK),
+                target.rearrange("p (c i j) -> p c j i", i=run, j=PACK),
+                rows.rearrange("p j (c i) -> p c j i", i=run),
+            )
+
+        def deal(copy, target, rows, first, end):
+            copy(
+                target.rearrange("p (u m j) -> p m j u", u=PACK, j=PACK)[:, first:end],
+                rows[:].rearrange("p j (m u) -> p m j u", u=PACK)[:, first:end],
             )
 
         def turn(source, w, target, number):
@@ -130,75 +136,58 @@ def tile_attend_gat_tnh_qk_ts_kernel(tc, qT, kT, vT, doT, rw, ts, qm, offs, out_
         for t in range(PACK):
             nc.tensor.transpose(rw_wide[:, t, :], rw_neg[:, t:t + 1].to_broadcast([P, P]), ident[:])
 
+        rw_row = keep.tile([P, R], F32, name="rw_row")
+        nc.scalar.copy(rw_row[:].rearrange("p (m u) -> p m u", u=PACK), rw_wide[:].rearrange("p u m -> p m u"))
+
         for j in range(1, PACK):
             nc.vector.tensor_copy(k_planes[:, j, :], k_pool[j][:].indirect(offsets[:]))
         k_d = quantized("k_d")
         quantize(k_d, E4, 0, k_values[:])
 
-        q_d = quantized("q_d")
-        q_parts = [values("q_half%d" % h, HALF) for h in range(2)]
-        interleave(nc.vector.tensor_copy, q_parts[0][:], q_raw[:, :, :HALF])
-        interleave(nc.scalar.copy, q_parts[1][:], q_raw[:, :, HALF:])
-        for h in range(2):
-            quantize(q_d, E4, h * HALF, q_parts[h][:])
-
-        k_i_first = values("k_i_first", HALF, "q_raw")
+        k_i_first = values("k_i_first", HALF)
         turn(k_values, 0, k_i_first[:], 6)
 
-        grads = quantized("do_then_ds_r", 2 * W)
-        do_values = values("do_values", R, "q_half1")
+        q_d = quantized("q_d")
+        q_values = values("q_values", R)
         share = R - P
+        interleave(nc.vector.tensor_copy, q_values[:, :share * PACK], q_raw[:, :, :share])
+        interleave(nc.scalar.copy, q_values[:, share * PACK:], q_raw[:, :, share:])
+        quantize(q_d, E4, 0, q_values[:])
+        k_i_second = values("k_i_second", HALF, "q_raw")
+        turn(k_values, 1, k_i_second[:], 7)
+        k_i = quantized("k_i", tag="q_values")
+        quantize(k_i, E4, 0, k_i_first[:])
+
+        grads = quantized("do_then_ds_r", 2 * W)
+        do_values = values("do_values", R)
+        interleave(nc.vector.tensor_copy, do_values[:, :share * PACK], do_raw[:, :, :share])
         interleave(nc.scalar.copy, do_values[:, share * PACK:], do_raw[:, :, share:])
-        for first, end in ((0, HALF), (HALF, share)):
-            interleave(nc.vector.tensor_copy, do_values[:, first * PACK:end * PACK], do_raw[:, :, first:end])
-        for h in range(2):
-            quantize(grads, E5, h * HALF, do_values[:, h * 2 * W:(h + 1) * 2 * W])
+        quantize(k_i, E4, HALF, k_i_second[:])
+        quantize(grads, E5, 0, do_values[:])
 
-        v_listed = keep.tile([P, PACK * N], F32, name="v_listed", tag="v_listed", align_bytes=64)
+        v_values = values("v_values", W)
+        v_planes = v_values[:].rearrange("p (s j) -> p j s", j=PACK)
 
-        def gather_values(j):
-            nc.vector.tensor_copy(v_listed[:, j * N:(j + 1) * N], v_pool[j][:].indirect(offsets[:]))
-
-        slope_tags = ("slope0", "slope1", "slope2", "v_pool2")
         slope = []
-        weight = keep.tile([P, PACK, R], F32, name="weight", tag="weight", align_bytes=64)
-        squared = keep.tile([P, 3, R], F32, name="squared")
-        squares = [squared[:, 0, :], squared[:, 1, :], v_listed[:, 3 * N - P:3 * N - P + R], squared[:, 2, :]]
+        weight = keep.tile([P, PACK, R], F32, name="weight")
+        squared = keep.tile([P, PACK, R], F32, name="squared")
         for t in range(PACK):
+            if t < PACK - 1:
+                nc.vector.tensor_copy(v_planes[:, t, :], v_pool[t][:].indirect(offsets[:]))
             score = product(t, k_d, E4, t, q_d, E4)
             nc.scalar.activation(weight[:, t, :], score[:], ACT.Tanh, scale=ts_col[:, t:t + 1])
-            nc.scalar.activation(squares[t], weight[:, t, :], ACT.Square)
-            if t == 0:
-                gather_values(0)
-            slope.append(keep.tile([P, R], F32, name="slope%d" % t, tag=slope_tags[t], align_bytes=64))
-            nc.vector.scalar_tensor_tensor(
-                slope[t][:].rearrange("p (m u) -> p m u", u=PACK),
-                squares[t].rearrange("p (m u) -> p m u", u=PACK),
-                1.0,
-                rw_wide[:].rearrange("p u m -> p m u"),
-                ALU.subtract,
-                ALU.mult,
-            )
-            if 0 < t < PACK - 1:
-                gather_values(t)
+            nc.scalar.activation(squared[:, t, :], weight[:, t, :], ACT.Square)
+            slope.append(keep.tile([P, R], F32, name="slope%d" % t, tag="slope%d" % t, align_bytes=64))
+            nc.gpsimd.tensor_scalar(weight[:, t, :], squared[:, t, :], 1.0, -1.0, ALU.mult, ALU.add)
+            nc.gpsimd.tensor_tensor(slope[t][:], weight[:, t, :], rw_row[:], ALU.mult)
 
-        k_i_second = values("k_i_second", HALF, "weight")
-        turn(k_values, 1, k_i_second[:], 0)
-
-        last = (PACK - 1) * N
+        v_e = [quantized("v_e%d" % t, P) for t in range(PACK)]
         for h in range(2):
             nc.vector.tensor_copy(
-                v_listed[:, last + h * HALF:last + (h + 1) * HALF], v_pool[PACK - 1][:].indirect(list_halves[h])
+                v_planes[:, PACK - 1, h * HALF:(h + 1) * HALF], v_pool[PACK - 1][:].indirect(list_halves[h])
             )
-        v_rows_listed = v_listed[:].rearrange("p (j s) -> p j s", j=PACK)
-        v_e = []
-        v_values = [values("v_values%d" % t, P) for t in range(PACK)]
         for t in range(PACK):
-            copy = nc.vector.tensor_copy if t == 1 else nc.scalar.copy
-            interleave(copy, v_values[t][:], v_rows_listed[:, :, t * P:(t + 1) * P])
-        for t in range(PACK):
-            v_e.append(quantized("v_e%d" % t, P))
-            quantize(v_e[t], E4, 0, v_values[t][:])
+            quantize(v_e[t], E4, 0, v_values[:, t * W:(t + 1) * W])
 
         ds = [keep.tile([P, R], BF16, name="ds%d" % t) for t in range(PACK)]
         for t in range(PACK):
@@ -248,9 +237,6 @@ def tile_attend_gat_tnh_qk_ts_kernel(tc, qT, kT, vT, doT, rw, ts, qm, offs, out_
         for c in range(1, PACK):
             quantize_qm(c)
         place(1, 2)
-        k_i = quantized("k_i", tag=slope_tags[3])
-        quantize(k_i, E4, 0, k_i_first[:])
-        quantize(k_i, E4, HALF, k_i_second[:])
 
         ds_i_values = values("ds_i_values", W)
         for w in range(2):

@@ -178,7 +178,10 @@ def tile_attend_gat_tnh_qk_ts_kernel(tc, qT, kT, vT, doT, rw, ts, qm, offs, out_
             nc.scalar.activation(weight[:, t, :], score[:], ACT.Tanh, scale=ts_col[:, t:t + 1])
             nc.scalar.activation(squared[:, t, :], weight[:, t, :], ACT.Square)
             slope.append(keep.tile([P, R], F32, name="slope%d" % t, tag="slope%d" % t, align_bytes=64))
-            nc.gpsimd.tensor_scalar(weight[:, t, :], squared[:, t, :], 1.0, -1.0, ALU.mult, ALU.add)
+            if t < 2:
+                nc.gpsimd.tensor_scalar(weight[:, t, :], squared[:, t, :], 1.0, -1.0, ALU.mult, ALU.add)
+            else:
+                nc.scalar.activation(weight[:, t, :], squared[:, t, :], ACT.Identity, bias=-1.0)
             nc.gpsimd.tensor_tensor(slope[t][:], weight[:, t, :], rw_row[:], ALU.mult)
 
         v_e = [quantized("v_e%d" % t, P) for t in range(PACK)]
@@ -236,22 +239,24 @@ def tile_attend_gat_tnh_qk_ts_kernel(tc, qT, kT, vT, doT, rw, ts, qm, offs, out_
         store(0)
         for c in range(1, PACK):
             quantize_qm(c)
-        place(1, 2)
 
         ds_i_values = values("ds_i_values", W)
         for w in range(2):
-            turn(ds_r_values, w, ds_i_values[:, w * 2 * W:(w + 1) * 2 * W], 1 + w)
+            turn(ds_r_values, w, ds_i_values[:, w * 2 * W:(w + 1) * 2 * W], 2 + w)
         ds_i = quantized("ds_i")
         quantize(ds_i, E5, 0, ds_i_values[:])
-        place(2, 3, "ds_r_values")
+        place(1, 5, "ds_r_values")
 
         gq_rows = out_0[0].rearrange("(m u) d -> m u d", u=PACK)
-        for u in range(PACK):
-            gq = product((0, 4, 6, 7)[u], ds_i, E5, u, k_i, E4)
-            gq_out = keep.tile([P, D], F32, name="gq_out%d" % u)
-            nc.scalar.copy(
-                gq_out[:].rearrange("p (c j) -> p c j", j=PACK),
-                gq[:].rearrange("p (j c) -> p c j", j=PACK),
-            )
-            nc.scalar.dma_start(gq_rows[:, u, :], gq_out[:])
-        place(3, 5)
+        for pair in range(2):
+            gq_out = keep.tile([P, 2, D], F32, name="gq_out%d" % pair)
+            for e in range(2):
+                u = 2 * pair + e
+                gq = product((0, 1, 6, 7)[u], ds_i, E5, u, k_i, E4)
+                nc.scalar.copy(
+                    gq_out[:, e, :].rearrange("p (c j) -> p c j", j=PACK),
+                    gq[:].rearrange("p (j c) -> p c j", j=PACK),
+                )
+            nc.scalar.dma_start(gq_rows[:, 2 * pair:2 * pair + 2, :], gq_out[:])
+        place(2, 4)
+        place(3, 2)

@@ -118,6 +118,9 @@ def tile_attend_gat_tnh_qk_ts_kernel(tc, qT, kT, vT, doT, rw, ts, qm, offs, out_
             engine = nc.vector if c < 1 else nc.gpsimd
             engine.memset(placed[c][:].bitcast(I32), 0)
 
+        zeros = keep.tile([P, P], F32, name="zeros")
+        nc.gpsimd.memset(zeros[:], 0.0)
+
         k_values = values("k_values", W)
         k_planes = k_values[:].rearrange("p (s j) -> p j s", j=PACK)
         nc.vector.tensor_copy(k_planes[:, 0, :], k_pool[0][:].indirect(offsets[:]))
@@ -168,12 +171,14 @@ def tile_attend_gat_tnh_qk_ts_kernel(tc, qT, kT, vT, doT, rw, ts, qm, offs, out_
         v_values = values("v_values", W)
         v_planes = v_values[:].rearrange("p (s j) -> p j s", j=PACK)
 
+        v_late = keep.tile([P, 2, N], F32, name="v_late")
         slope = []
         weight = keep.tile([P, PACK, R], F32, name="weight")
         squared = keep.tile([P, PACK, R], F32, name="squared")
         for t in range(PACK):
             if t < PACK - 1:
-                nc.vector.tensor_copy(v_planes[:, t, :], v_pool[t][:].indirect(offsets[:]))
+                gathered = v_planes[:, t, :] if t < 2 else v_late[:, 0, :]
+                nc.vector.tensor_copy(gathered, v_pool[t][:].indirect(offsets[:]))
             score = product(t, k_d, E4, t, q_d, E4)
             nc.scalar.activation(weight[:, t, :], score[:], ACT.Tanh, scale=ts_col[:, t:t + 1])
             nc.scalar.activation(squared[:, t, :], weight[:, t, :], ACT.Square)
@@ -187,10 +192,15 @@ def tile_attend_gat_tnh_qk_ts_kernel(tc, qT, kT, vT, doT, rw, ts, qm, offs, out_
         v_e = [quantized("v_e%d" % t, P) for t in range(PACK)]
         for h in range(2):
             nc.vector.tensor_copy(
-                v_planes[:, PACK - 1, h * HALF:(h + 1) * HALF], v_pool[PACK - 1][:].indirect(list_halves[h])
+                v_late[:, 1, h * HALF:(h + 1) * HALF], v_pool[PACK - 1][:].indirect(list_halves[h])
             )
         for t in range(PACK):
-            quantize(v_e[t], E4, 0, v_values[:, t * W:(t + 1) * W])
+            block = v_values[:, t * W:(t + 1) * W]
+            nc.scalar.copy(
+                block.rearrange("p (s j) -> p s j", j=PACK)[:, :, 2:],
+                v_late[:, :, t * P:(t + 1) * P].rearrange("p j s -> p s j"),
+            )
+            quantize(v_e[t], E4, 0, block)
 
         ds = [keep.tile([P, R], BF16, name="ds%d" % t) for t in range(PACK)]
         for t in range(PACK):
@@ -225,38 +235,45 @@ def tile_attend_gat_tnh_qk_ts_kernel(tc, qT, kT, vT, doT, rw, ts, qm, offs, out_
             nc.vector.tensor_copy(placed[c % WINDOWS][:].indirect(offsets[:]), dk_listed[:])
             store(c)
 
-        def place_half(h):
-            dk = product(h, qm_r[0], E4, 0, grads, E5, HALF * (h + 1))
-            dk_listed = keep.tile([P, HALF], F32, name="dk_half%d" % h)
-            nc.scalar.copy(dk_listed[:], dk[:, HALF:])
-            nc.vector.tensor_copy(placed[0][:].indirect(list_halves[h]), dk_listed[:])
+        def place_part(c, first, end, number):
+            dk = product(number, qm_r[c], E4, 0, grads, E5, end)
+            dk_listed = keep.tile([P, end - first], F32, name="dk_part%d_%d" % (c, first))
+            nc.scalar.copy(dk_listed[:], dk[:, W - (end - first):])
+            part = placed[c][:].indirect(offsets[:, first // 16:end // 16])
+            if end - first < HALF:
+                nc.vector.tensor_tensor(part, dk_listed[:], zeros[:], ALU.add)
+            else:
+                nc.vector.tensor_copy(part, dk_listed[:])
 
         quantize_qm(0)
-        for h in range(2):
-            quantize_ds_r(2 * h)
-            quantize_ds_r(2 * h + 1)
-            place_half(h)
-        store(0)
-        for c in range(1, PACK):
+        quantize_qm(1)
+        for t in range(PACK):
+            quantize_ds_r(t)
+        place_part(0, 0, P, 0)
+        place_part(1, 0, P, 1)
+        for c in range(2, PACK):
             quantize_qm(c)
+        place_part(0, P, N, 2)
+        store(0)
 
         ds_i_values = values("ds_i_values", W)
         for w in range(2):
-            turn(ds_r_values, w, ds_i_values[:, w * 2 * W:(w + 1) * 2 * W], 2 + w)
+            turn(ds_r_values, w, ds_i_values[:, w * 2 * W:(w + 1) * 2 * W], (3, 0)[w])
         ds_i = quantized("ds_i")
         quantize(ds_i, E5, 0, ds_i_values[:])
-        place(1, 5, "ds_r_values")
+        place_part(1, P, N, 5)
+        store(1)
 
         gq_rows = out_0[0].rearrange("(m u) d -> m u d", u=PACK)
         for pair in range(2):
             gq_out = keep.tile([P, 2, D], F32, name="gq_out%d" % pair)
             for e in range(2):
                 u = 2 * pair + e
-                gq = product((0, 1, 6, 7)[u], ds_i, E5, u, k_i, E4)
+                gq = product((1, 6, 7, 2)[u], ds_i, E5, u, k_i, E4)
                 nc.scalar.copy(
                     gq_out[:, e, :].rearrange("p (c j) -> p c j", j=PACK),
                     gq[:].rearrange("p (j c) -> p c j", j=PACK),
                 )
             nc.scalar.dma_start(gq_rows[:, 2 * pair:2 * pair + 2, :], gq_out[:])
         place(2, 4)
-        place(3, 2)
+        place(3, 3)

@@ -169,16 +169,16 @@ def tile_attend_gat_tnh_qk_ts_kernel(tc, qT, kT, vT, doT, rw, ts, qm, offs, out_
         quantize(grads, E5, 0, do_values[:])
 
         v_values = values("v_values", W)
-        v_planes = v_values[:].rearrange("p (s j) -> p j s", j=PACK)
+        v_pairs = keep.tile([P, 2 * N * 2], BF16, name="v_pairs", align_bytes=64)
+        v_planes = v_pairs[:].rearrange("p (w s e) -> p w e s", w=2, e=2)
+        v_words = v_pairs[:].bitcast(U32).rearrange("p (w s) -> p s w", w=2)
 
-        v_late = keep.tile([P, 2, N], F32, name="v_late")
         slope = []
         weight = keep.tile([P, PACK, R], F32, name="weight")
         squared = keep.tile([P, PACK, R], F32, name="squared")
         for t in range(PACK):
             if t < PACK - 1:
-                gathered = v_planes[:, t, :] if t < 2 else v_late[:, 0, :]
-                nc.vector.tensor_copy(gathered, v_pool[t][:].indirect(offsets[:]))
+                nc.vector.tensor_copy(v_planes[:, t // 2, t % 2, :], v_pool[t][:].indirect(offsets[:]))
             score = product(t, k_d, E4, t, q_d, E4)
             nc.scalar.activation(weight[:, t, :], score[:], ACT.Tanh, scale=ts_col[:, t:t + 1])
             nc.scalar.activation(squared[:, t, :], weight[:, t, :], ACT.Square)
@@ -192,14 +192,11 @@ def tile_attend_gat_tnh_qk_ts_kernel(tc, qT, kT, vT, doT, rw, ts, qm, offs, out_
         v_e = [quantized("v_e%d" % t, P) for t in range(PACK)]
         for h in range(2):
             nc.vector.tensor_copy(
-                v_late[:, 1, h * HALF:(h + 1) * HALF], v_pool[PACK - 1][:].indirect(list_halves[h])
+                v_planes[:, 1, 1, h * HALF:(h + 1) * HALF], v_pool[PACK - 1][:].indirect(list_halves[h])
             )
         for t in range(PACK):
             block = v_values[:, t * W:(t + 1) * W]
-            nc.scalar.copy(
-                block.rearrange("p (s j) -> p s j", j=PACK)[:, :, 2:],
-                v_late[:, :, t * P:(t + 1) * P].rearrange("p j s -> p s j"),
-            )
+            nc.scalar.copy(block.bitcast(U32).rearrange("p (s w) -> p s w", w=2), v_words[:, t * P:(t + 1) * P, :])
             quantize(v_e[t], E4, 0, block)
 
         ds = [keep.tile([P, R], BF16, name="ds%d" % t) for t in range(PACK)]

@@ -232,12 +232,14 @@ def tile_attend_gat_tnh_qk_ts_kernel(tc, qT, kT, vT, doT, rw, ts, qm, offs, out_
             nc.vector.tensor_copy(placed[c % WINDOWS][:].indirect(offsets[:]), dk_listed[:])
             store(c)
 
-        def place_part(c, first, end, number):
+        def place_part(c, first, end, number, by_scalar=False):
             dk = product(number, qm_r[c], E4, 0, grads, E5, end)
             dk_listed = keep.tile([P, end - first], F32, name="dk_part%d_%d" % (c, first))
             nc.scalar.copy(dk_listed[:], dk[:, W - (end - first):])
             part = placed[c][:].indirect(offsets[:, first // 16:end // 16])
-            if end - first < HALF:
+            if by_scalar:
+                nc.scalar.activation(part, dk_listed[:], ACT.Copy)
+            elif end - first < HALF:
                 nc.vector.tensor_tensor(part, dk_listed[:], zeros[:], ALU.add)
             else:
                 nc.vector.tensor_copy(part, dk_listed[:])
@@ -252,14 +254,19 @@ def tile_attend_gat_tnh_qk_ts_kernel(tc, qT, kT, vT, doT, rw, ts, qm, offs, out_
             quantize_qm(c)
         place_part(0, P, N, 2)
         store(0)
+        dk_2 = product(4, qm_r[2], E4, 0, grads, E5, W)
+        dk_listed_2 = keep.tile([P, N], F32, name="dk_listed2", tag="dk_listed2", align_bytes=64)
+        nc.scalar.copy(dk_listed_2[:], dk_2[:])
+        place_part(1, P, N, 5, True)
+        store(1)
+        nc.vector.tensor_copy(placed[2][:].indirect(offsets[:]), dk_listed_2[:])
+        store(2)
 
         ds_i_values = values("ds_i_values", W)
         for w in range(2):
-            turn(ds_r_values, w, ds_i_values[:, w * 2 * W:(w + 1) * 2 * W], (3, 0)[w])
-        ds_i = quantized("ds_i")
+            turn(ds_r_values, w, ds_i_values[:, w * 2 * W:(w + 1) * 2 * W], (4, 5)[w])
+        ds_i = quantized("ds_i", W, "dk_listed2")
         quantize(ds_i, E5, 0, ds_i_values[:])
-        place_part(1, P, N, 5)
-        store(1)
 
         gq_rows = out_0[0].rearrange("(m u) d -> m u d", u=PACK)
         for pair in range(2):
@@ -272,5 +279,4 @@ def tile_attend_gat_tnh_qk_ts_kernel(tc, qT, kT, vT, doT, rw, ts, qm, offs, out_
                     gq[:].rearrange("p (j c) -> p c j", j=PACK),
                 )
             nc.scalar.dma_start(gq_rows[:, 2 * pair:2 * pair + 2, :], gq_out[:])
-        place(2, 4)
         place(3, 3)

@@ -49,15 +49,15 @@ def tile_attend_gat_tnh_qk_ts_kernel(tc, qT, kT, vT, doT, rw, ts, qm, offs, out_
                 in_=source,
             )
 
-        def product(number, stationary, fmt_s, block, moving, fmt_m, first=0):
-            acc = bank(number, [P, W])
+        def product(number, stationary, fmt_s, block, moving, fmt_m, first=0, width=W):
+            acc = bank(number, [P, width])
             cols = slice(block * P, (block + 1) * P)
             nc.tensor.matmul_mx(
                 out=acc[:],
                 lhsT=stationary[0][:, cols].bitcast(fmt_s),
                 lhsT_scale=stationary[1][:, cols],
-                rhs=moving[0][:, first:first + W].bitcast(fmt_m),
-                rhs_scale=moving[1][:, first:first + W],
+                rhs=moving[0][:, first:first + width].bitcast(fmt_m),
+                rhs_scale=moving[1][:, first:first + width],
                 start=True,
                 stop=True,
             )
@@ -71,8 +71,8 @@ def tile_attend_gat_tnh_qk_ts_kernel(tc, qT, kT, vT, doT, rw, ts, qm, offs, out_
 
         def deal(copy, target, rows, first, end):
             copy(
-                target.rearrange("p (u m j) -> p m j u", u=PACK, j=PACK)[:, first:end],
-                rows[:].rearrange("p j (m u) -> p m j u", u=PACK)[:, first:end],
+                target[:].rearrange("p (w m e j) -> p m j w e", w=2, e=2, j=PACK)[:, first:end],
+                rows[:].rearrange("p j (m w e) -> p m j w e", w=2, e=2)[:, first:end],
             )
 
         def turn(source, w, target, number):
@@ -108,7 +108,8 @@ def tile_attend_gat_tnh_qk_ts_kernel(tc, qT, kT, vT, doT, rw, ts, qm, offs, out_
         q_raw = load("q_raw", [P, PACK, R], qT[0].rearrange("(p j) r -> p j r", j=PACK))
         do_raw = load("do_raw", [P, PACK, R], doT[0].rearrange("(p j) r -> p j r", j=PACK))
         v_pool = [load("v_pool%d" % j, [P, T], v_rows[:, j, :]) for j in range(PACK)]
-        qm_raw = load("qm_raw", [P, PACK, D], qm[0].rearrange("(p j) d -> p j d", j=PACK))
+        qm_rows = qm[0].rearrange("(p j) d -> p j d", j=PACK)
+        qm_raw = [load("qm_raw%d" % h, [P, PACK, HALF], qm_rows[:, :, h * HALF:(h + 1) * HALF]) for h in range(2)]
 
         ident = keep.tile([P, P], F32, name="ident")
         make_identity(nc, ident[:])
@@ -117,9 +118,6 @@ def tile_attend_gat_tnh_qk_ts_kernel(tc, qT, kT, vT, doT, rw, ts, qm, offs, out_
         for c in range(WINDOWS):
             engine = nc.vector if c < 1 else nc.gpsimd
             engine.memset(placed[c][:].bitcast(I32), 0)
-
-        zeros = keep.tile([P, P], F32, name="zeros")
-        nc.gpsimd.memset(zeros[:], 0.0)
 
         k_values = values("k_values", W)
         k_planes = k_values[:].rearrange("p (s j) -> p j s", j=PACK)
@@ -140,7 +138,9 @@ def tile_attend_gat_tnh_qk_ts_kernel(tc, qT, kT, vT, doT, rw, ts, qm, offs, out_
             nc.tensor.transpose(rw_wide[:, t, :], rw_neg[:, t:t + 1].to_broadcast([P, P]), ident[:])
 
         rw_row = keep.tile([P, R], F32, name="rw_row")
-        nc.scalar.copy(rw_row[:].rearrange("p (m u) -> p m u", u=PACK), rw_wide[:].rearrange("p u m -> p m u"))
+        nc.scalar.copy(
+            rw_row[:].rearrange("p (w m e) -> p w m e", w=2, e=2), rw_wide[:].rearrange("p (w e) m -> p w m e", w=2)
+        )
 
         for j in range(1, PACK):
             nc.vector.tensor_copy(k_planes[:, j, :], k_pool[j][:].indirect(offsets[:]))
@@ -152,9 +152,9 @@ def tile_attend_gat_tnh_qk_ts_kernel(tc, qT, kT, vT, doT, rw, ts, qm, offs, out_
 
         q_d = quantized("q_d")
         q_values = values("q_values", R)
-        share = R - P
-        interleave(nc.vector.tensor_copy, q_values[:, :share * PACK], q_raw[:, :, :share])
-        interleave(nc.scalar.copy, q_values[:, share * PACK:], q_raw[:, :, share:])
+        share = 3 * P // 4
+        deal(nc.vector.tensor_copy, q_values, q_raw, 0, share)
+        deal(nc.scalar.copy, q_values, q_raw, share, P)
         quantize(q_d, E4, 0, q_values[:])
         k_i_second = values("k_i_second", HALF, "q_raw")
         turn(k_values, 1, k_i_second[:], 7)
@@ -163,8 +163,8 @@ def tile_attend_gat_tnh_qk_ts_kernel(tc, qT, kT, vT, doT, rw, ts, qm, offs, out_
 
         grads = quantized("do_then_ds_r", 2 * W)
         do_values = values("do_values", R)
-        interleave(nc.vector.tensor_copy, do_values[:, :share * PACK], do_raw[:, :, :share])
-        interleave(nc.scalar.copy, do_values[:, share * PACK:], do_raw[:, :, share:])
+        deal(nc.vector.tensor_copy, do_values, do_raw, 0, share)
+        deal(nc.scalar.copy, do_values, do_raw, share, P)
         quantize(k_i, E4, HALF, k_i_second[:])
         quantize(grads, E5, 0, do_values[:])
 
@@ -204,11 +204,12 @@ def tile_attend_gat_tnh_qk_ts_kernel(tc, qT, kT, vT, doT, rw, ts, qm, offs, out_
             dp = product(t, v_e[t], E4, 0, grads, E5)
             nc.vector.scalar_tensor_tensor(ds[t][:], dp[:], ts_col[:, t:t + 1], slope[t][:], ALU.mult, ALU.mult)
 
-        qm_values = values("qm_values", D, "v_pool3")
-        qm_r = [quantized("qm_r%d" % c, P, "slope%d" % (c - 1) if c else None) for c in range(PACK)]
+        qm_values = values("qm_values", HALF, "v_pool3")
+        qm_r = [quantized("qm_r%d" % c, P, "slope0" if c else None) for c in range(2)]
+        qm_late = quantized("qm_late", HALF)
 
         def quantize_qm(c):
-            interleave(nc.scalar.copy, qm_values[:, c * W:(c + 1) * W], qm_raw[:, :, c * P:(c + 1) * P])
+            interleave(nc.scalar.copy, qm_values[:, c * W:(c + 1) * W], qm_raw[0][:, :, c * P:(c + 1) * P])
             quantize(qm_r[c], E4, 0, qm_values[:, c * W:(c + 1) * W])
 
         ds_r_values = values("ds_r_values", W)
@@ -217,7 +218,7 @@ def tile_attend_gat_tnh_qk_ts_kernel(tc, qT, kT, vT, doT, rw, ts, qm, offs, out_
             ds_words = ds[t][:].bitcast(F32)
             ds_turned = bank((5, 6, 7, 4)[t], [P, 2, P])
             for w in range(2):
-                nc.tensor.transpose(ds_turned[:, w, :], ds_words[:, w::2], ident[:])
+                nc.tensor.transpose(ds_turned[:, w, :], ds_words[:, w * P:(w + 1) * P], ident[:])
             block = ds_r_values[:, t * W:(t + 1) * W]
             nc.scalar.copy(block.bitcast(F32).rearrange("p (m w) -> p m w", w=2), ds_turned[:].rearrange("p w m -> p m w"))
             quantize(grads, E5, W + t * P, block)
@@ -225,58 +226,55 @@ def tile_attend_gat_tnh_qk_ts_kernel(tc, qT, kT, vT, doT, rw, ts, qm, offs, out_
         def store(c):
             nc.sync.dma_start(out_1[c * P:(c + 1) * P, :], placed[c % WINDOWS][:])
 
-        def place(c, number, tag=None):
-            dk = product(number, qm_r[c], E4, 0, grads, E5, W)
-            dk_listed = keep.tile([P, N], F32, name="dk_listed%d" % c, tag=tag or "dk_listed%d" % c, align_bytes=64)
-            nc.scalar.copy(dk_listed[:], dk[:])
-            nc.vector.tensor_copy(placed[c % WINDOWS][:].indirect(offsets[:]), dk_listed[:])
-            store(c)
+        def keys_gradient(c, first, end, number, copy, tag=None):
+            stationary, block = (qm_r[c], 0) if c < 2 else (qm_late, c - 2)
+            dk = product(number, stationary, E4, block, grads, E5, W + first, end - first)
+            name = "dk_listed%d_%d" % (c, first)
+            dk_listed = keep.tile([P, end - first], F32, name=name, tag=tag or name, align_bytes=64)
+            copy(dk_listed[:], dk[:])
+            return dk_listed
 
-        def place_part(c, first, end, number, by_scalar=False):
-            dk = product(number, qm_r[c], E4, 0, grads, E5, end)
-            dk_listed = keep.tile([P, end - first], F32, name="dk_part%d_%d" % (c, first))
-            nc.scalar.copy(dk_listed[:], dk[:, W - (end - first):])
-            part = placed[c][:].indirect(offsets[:, first // 16:end // 16])
-            if by_scalar:
-                nc.scalar.activation(part, dk_listed[:], ACT.Copy)
-            elif end - first < HALF:
-                nc.vector.tensor_tensor(part, dk_listed[:], zeros[:], ALU.add)
-            else:
-                nc.vector.tensor_copy(part, dk_listed[:])
+        def place_by_scalar(c, first, end, dk_listed):
+            nc.scalar.activation(placed[c % WINDOWS][:].indirect(offsets[:, first // 16:end // 16]), dk_listed, ACT.Copy)
+
+        def place_by_vector(c, first, end, dk_listed):
+            nc.vector.tensor_copy(placed[c % WINDOWS][:].indirect(offsets[:, first // 16:end // 16]), dk_listed)
 
         quantize_qm(0)
         quantize_qm(1)
-        for t in range(PACK):
-            quantize_ds_r(t)
-        place_part(0, 0, P, 0)
-        place_part(1, 0, P, 1)
-        for c in range(2, PACK):
-            quantize_qm(c)
-        place_part(0, P, N, 2)
+        for h in range(2):
+            quantize_ds_r(2 * h)
+            quantize_ds_r(2 * h + 1)
+            part = keys_gradient(0, h * HALF, (h + 1) * HALF, h, nc.vector.tensor_copy, ("qm_raw0", None)[h])
+            place_by_scalar(0, h * HALF, (h + 1) * HALF, part[:])
         store(0)
-        dk_2 = product(4, qm_r[2], E4, 0, grads, E5, W)
-        dk_listed_2 = keep.tile([P, N], F32, name="dk_listed2", tag="dk_listed2", align_bytes=64)
-        nc.scalar.copy(dk_listed_2[:], dk_2[:])
-        place_part(1, P, N, 5, True)
+        qm_late_values = values("qm_late_values", HALF, "slope3")
+        interleave(nc.vector.tensor_copy, qm_late_values[:], qm_raw[1][:])
+        quantize(qm_late, E4, 0, qm_late_values[:])
+        place_by_vector(1, 0, N, keys_gradient(1, 0, N, 2, nc.vector.tensor_copy)[:])
         store(1)
-        nc.vector.tensor_copy(placed[2][:].indirect(offsets[:]), dk_listed_2[:])
+        place_by_scalar(2, 0, HALF, keys_gradient(2, 0, HALF, 3, nc.scalar.copy, "dk_listed0_256")[:])
+        place_by_vector(2, HALF, N, keys_gradient(2, HALF, N, 4, nc.vector.tensor_copy)[:])
         store(2)
 
-        ds_i_values = values("ds_i_values", W)
+        ds_i_values = values("ds_i_values", W, "dk_listed0_256")
         for w in range(2):
-            turn(ds_r_values, w, ds_i_values[:, w * 2 * W:(w + 1) * 2 * W], (4, 5)[w])
-        ds_i = quantized("ds_i", W, "dk_listed2")
-        quantize(ds_i, E5, 0, ds_i_values[:])
+            turn(ds_r_values, w, ds_i_values[:, w * 2 * W:(w + 1) * 2 * W], (2, 4)[w])
+        dk_3 = keys_gradient(3, 0, N, 2, nc.vector.tensor_copy)
+        ds_i = [quantized("ds_i0", HALF, "dk_listed2_256"), quantized("ds_i1", HALF)]
+        for w in range(2):
+            quantize(ds_i[w], E5, 0, ds_i_values[:, w * 2 * W:(w + 1) * 2 * W])
+        place_by_vector(3, 0, N, dk_3[:])
 
         gq_rows = out_0[0].rearrange("(m u) d -> m u d", u=PACK)
         for pair in range(2):
             gq_out = keep.tile([P, 2, D], F32, name="gq_out%d" % pair)
             for e in range(2):
                 u = 2 * pair + e
-                gq = product((1, 6, 7, 2)[u], ds_i, E5, u, k_i, E4)
+                gq = product((0, 1, 5, 6)[u], ds_i[pair], E5, e, k_i, E4)
                 nc.scalar.copy(
                     gq_out[:, e, :].rearrange("p (c j) -> p c j", j=PACK),
                     gq[:].rearrange("p (j c) -> p c j", j=PACK),
                 )
             nc.scalar.dma_start(gq_rows[:, 2 * pair:2 * pair + 2, :], gq_out[:])
-        place(3, 3)
+        store(3)

@@ -183,11 +183,14 @@ def tile_attend_gat_tnh_qk_ts_kernel(tc, qT, kT, vT, doT, rw, ts, qm, offs, out_
             nc.scalar.activation(weight[:, t, :], score[:], ACT.Tanh, scale=ts_col[:, t:t + 1])
             nc.scalar.activation(squared[:, t, :], weight[:, t, :], ACT.Square)
             slope.append(keep.tile([P, R], F32, name="slope%d" % t, tag="slope%d" % t, align_bytes=64))
-            if t < 2:
-                nc.gpsimd.tensor_scalar(weight[:, t, :], squared[:, t, :], 1.0, -1.0, ALU.mult, ALU.add)
+            if t == 0:
+                nc.vector.scalar_tensor_tensor(slope[t][:], squared[:, t, :], -1.0, rw_row[:], ALU.add, ALU.mult)
             else:
-                nc.scalar.activation(weight[:, t, :], squared[:, t, :], ACT.Identity, bias=-1.0)
-            nc.gpsimd.tensor_tensor(slope[t][:], weight[:, t, :], rw_row[:], ALU.mult)
+                if t == 1:
+                    nc.gpsimd.tensor_scalar(weight[:, t, :], squared[:, t, :], 1.0, -1.0, ALU.mult, ALU.add)
+                else:
+                    nc.scalar.activation(weight[:, t, :], squared[:, t, :], ACT.Identity, bias=-1.0)
+                nc.gpsimd.tensor_tensor(slope[t][:], weight[:, t, :], rw_row[:], ALU.mult)
 
         v_e = [quantized("v_e%d" % t, P) for t in range(PACK)]
         for h in range(2):

@@ -21,25 +21,28 @@ P = 128
 PACK = 4
 W = 512
 HALF = W // 2
-WINDOWS = 3
+RUN = 8
+DO_SHARE = 28
 
 
 def tile_attend_gat_tnh_qk_ts_kernel(tc, qT, kT, vT, doT, rw, ts, qm, offs, out_0, out_1):
     nc = tc.nc
     with ExitStack() as ctx:
         keep = ctx.enter_context(tc.tile_pool(name="keep", bufs=1))
+        late = ctx.enter_context(tc.tile_pool(name="late", bufs=1))
         psum = ctx.enter_context(tc.psum_pool(name="psum", bufs=1))
 
         def bank(number, shape):
             return psum.tile(shape, F32, name="bank%d" % number, tag="bank%d" % number)
 
+        def tile(name, shape, dtype, tag=None):
+            return keep.tile(shape, dtype, name=name, tag=tag or name, align_bytes=64)
+
         def quantized(name, width=W, tag=None):
-            codes = keep.tile([P, width], U32, name=name + "_codes", tag=tag or name + "_codes", align_bytes=64)
-            scales = keep.tile([P, width], U8, name=name + "_scales", align_bytes=64)
-            return codes, scales
+            return tile(name + "_codes", [P, width], U32, tag), tile(name + "_scales", [P, width], U8)
 
         def values(name, columns, tag=None):
-            return keep.tile([P, columns * PACK], BF16, name=name, tag=tag or name, align_bytes=64)
+            return tile(name, [P, columns * PACK], BF16, tag)
 
         def quantize(op, fmt, first, source):
             count = source.shape[1] // PACK
@@ -49,11 +52,11 @@ def tile_attend_gat_tnh_qk_ts_kernel(tc, qT, kT, vT, doT, rw, ts, qm, offs, out_
                 in_=source,
             )
 
-        def product(number, stationary, fmt_s, block, moving, fmt_m, first=0, width=W):
-            acc = bank(number, [P, width])
+        def product(acc, stationary, fmt_s, block, moving, fmt_m, first=0):
+            width = acc.shape[1]
             cols = slice(block * P, (block + 1) * P)
             nc.tensor.matmul_mx(
-                out=acc[:],
+                out=acc,
                 lhsT=stationary[0][:, cols].bitcast(fmt_s),
                 lhsT_scale=stationary[1][:, cols],
                 rhs=moving[0][:, first:first + width].bitcast(fmt_m),
@@ -61,223 +64,256 @@ def tile_attend_gat_tnh_qk_ts_kernel(tc, qT, kT, vT, doT, rw, ts, qm, offs, out_
                 start=True,
                 stop=True,
             )
-            return acc
 
-        def interleave(copy, target, rows, run=PACK):
+        def interleave(copy, target, rows):
             copy(
-                target.rearrange("p (c i j) -> p c j i", i=run, j=PACK),
-                rows.rearrange("p j (c i) -> p c j i", i=run),
+                target.rearrange("p (c i j) -> p c j i", i=PACK, j=PACK),
+                rows.rearrange("p j (c i) -> p c j i", i=PACK),
             )
 
         def deal(copy, target, rows, first, end):
             copy(
-                target[:].rearrange("p (w m e j) -> p m j w e", w=2, e=2, j=PACK)[:, first:end],
-                rows[:].rearrange("p j (m w e) -> p m j w e", w=2, e=2)[:, first:end],
+                target[:].rearrange("p (u m e j) -> p m j u e", u=2, e=2, j=PACK)[:, first:end],
+                rows[:].rearrange("p j (m u e) -> p m j u e", u=2, e=2)[:, first:end],
             )
 
-        def turn(source, w, target, number):
-            words = source[:].bitcast(F32).rearrange("p (s i w) -> p w i s", i=PACK, w=2)
-            turned = bank(number, [P, PACK, P])
-            for i in range(PACK):
-                nc.tensor.transpose(turned[:, i, :], words[:, w, i, :], ident[:])
-            nc.scalar.copy(
-                target.rearrange("s (e p i) -> s e p i", e=2, i=PACK),
-                turned[:].rearrange("s i p -> s (i p)").bitcast(BF16).rearrange("s (i p e) -> s e p i", i=PACK, e=2),
-            )
+        def gather_plane(target, j, pool):
+            planes = target[:].rearrange("p (t g a j) -> p j g t a", t=PACK, a=RUN, j=PACK)
+            nc.vector.tensor_copy(planes[:, j], pool[:].indirect(offsets[:]))
+
+        def turn(source, w, turned, places):
+            words = source[:].bitcast(F32).rearrange("p (t m w) -> p w t m", t=PACK, w=2)
+            for t in places:
+                nc.tensor.transpose(turned[:, t, :], words[:, w, t, :], ident[:])
 
         offsets = keep.tile([P, N // 16], U16, name="offsets")
-        nc.sync.dma_start(offsets[:], offs)
-        list_halves = [offsets[:, h * HALF // 16:(h + 1) * HALF // 16] for h in range(2)]
-
-        ts_pool = keep.tile([P, T], F32, name="ts_pool")
+        ts_pool = tile("ts_pool", [P, T], F32)
         nc.vector.memset(ts_pool[:].bitcast(I32), 0)
-
-        rw_col = keep.tile([P, PACK], F32, name="rw_col")
+        rw_col = tile("rw_col", [P, PACK], F32)
 
         def load(name, shape, rows):
-            landed = keep.tile(shape, F32, name=name, tag=name, align_bytes=64)
+            landed = tile(name, shape, F32)
             nc.sync.dma_start(landed[:], rows)
             return landed
 
         k_rows = kT.rearrange("(p j) t -> p j t", j=PACK)
         v_rows = vT.rearrange("(p j) t -> p j t", j=PACK)
-        k_pool = [load("k_pool%d" % j, [P, T], k_rows[:, j, :]) for j in range(2)]
+        q_raw = load("q_raw", [P, PACK, R], qT[0].rearrange("(p j) r -> p j r", j=PACK))
+        nc.sync.dma_start(offsets[:], offs)
+        k_pool = [load("k_pool0", [P, T], k_rows[:, 0, :])]
         nc.sync.dma_start(ts_pool[0:1, :], ts[0:1, :])
         nc.sync.dma_start(rw_col[:], rw[0].rearrange("(p t) o -> p (t o)", t=PACK))
-        k_pool += [load("k_pool%d" % j, [P, T], k_rows[:, j, :]) for j in range(2, PACK)]
-        q_raw = load("q_raw", [P, PACK, R], qT[0].rearrange("(p j) r -> p j r", j=PACK))
-        do_raw = load("do_raw", [P, PACK, R], doT[0].rearrange("(p j) r -> p j r", j=PACK))
+        k_pool += [load("k_pool%d" % j, [P, T], k_rows[:, j, :]) for j in range(1, PACK)]
         v_pool = [load("v_pool%d" % j, [P, T], v_rows[:, j, :]) for j in range(PACK)]
+        do_rows = doT[0].rearrange("(p j) r -> p j r", j=PACK)
+        do_raw = [load("do_raw%d" % h, [P, PACK, HALF], do_rows[:, :, h * HALF:(h + 1) * HALF]) for h in range(2)]
         qm_rows = qm[0].rearrange("(p j) d -> p j d", j=PACK)
-        qm_raw = [load("qm_raw%d" % h, [P, PACK, HALF], qm_rows[:, :, h * HALF:(h + 1) * HALF]) for h in range(2)]
+        qm_raw = late.tile([P, PACK, D], F32, name="qm_raw", align_bytes=64, offset=0)
+        for h in range(2):
+            nc.sync.dma_start(qm_raw[:, :, h * HALF:(h + 1) * HALF], qm_rows[:, :, h * HALF:(h + 1) * HALF])
 
-        ident = keep.tile([P, P], F32, name="ident")
+        ident = tile("ident", [P, P], F32)
         make_identity(nc, ident[:])
 
-        placed = [keep.tile([P, T], F32, name="placed%d" % c) for c in range(WINDOWS)]
-        for c in range(WINDOWS):
+        placed = [tile("placed%d" % c, [P, T], F32) for c in range(PACK)]
+        for c in range(PACK):
             engine = nc.vector if c < 1 else nc.gpsimd
             engine.memset(placed[c][:].bitcast(I32), 0)
 
-        k_values = values("k_values", W)
-        k_planes = k_values[:].rearrange("p (s j) -> p j s", j=PACK)
-        nc.vector.tensor_copy(k_planes[:, 0, :], k_pool[0][:].indirect(offsets[:]))
+        q_values = values("q_values", R)
+        interleave(nc.vector.tensor_copy, q_values[:], q_raw[:])
+        q_d = quantized("q_d")
+        quantize(q_d, E4, 0, q_values[:])
 
-        ts_listed = keep.tile([P, N], F32, name="ts_listed")
-        nc.vector.tensor_copy(ts_listed[:], ts_pool[:].indirect(offsets[:]))
-        ts_turned = bank(5, [P, PACK, P])
+        k_values = values("k_values", W)
+        gather_plane(k_values, 0, k_pool[0])
+
+        ts_listed = tile("ts_listed", [P, N], F32)
+        nc.vector.tensor_copy(
+            ts_listed[:].rearrange("p (t g a) -> p g t a", t=PACK, a=RUN), ts_pool[:].indirect(offsets[:])
+        )
+        ts_turned = bank(6, [P, PACK, P])
         for t in range(PACK):
             nc.tensor.transpose(ts_turned[:, t, :], ts_listed[:, t * P:(t + 1) * P], ident[:])
-        ts_col = keep.tile([P, PACK], F32, name="ts_col")
+        ts_col = tile("ts_col", [P, PACK], F32)
         nc.scalar.copy(ts_col[:], ts_turned[:, :, 0])
+        ts_neg = tile("ts_neg", [P, PACK], F32)
+        nc.gpsimd.tensor_scalar(ts_neg[:], ts_col[:], -1.0, 0.0, ALU.mult, ALU.add)
 
-        rw_neg = keep.tile([P, PACK], F32, name="rw_neg")
-        nc.vector.tensor_scalar(rw_neg[:], rw_col[:], -1.0, None, ALU.mult)
-        rw_wide = bank(4, [P, PACK, P])
-        for t in range(PACK):
-            nc.tensor.transpose(rw_wide[:, t, :], rw_neg[:, t:t + 1].to_broadcast([P, P]), ident[:])
-
-        rw_row = keep.tile([P, R], F32, name="rw_row")
+        rw_wide = bank(7, [P, PACK, P])
+        for j in range(PACK):
+            nc.tensor.transpose(rw_wide[:, j, :], rw_col[:, j:j + 1].to_broadcast([P, P]), ident[:])
+        rw_row = tile("rw_row", [P, R], F32)
         nc.scalar.copy(
-            rw_row[:].rearrange("p (w m e) -> p w m e", w=2, e=2), rw_wide[:].rearrange("p (w e) m -> p w m e", w=2)
+            rw_row[:].rearrange("m (h j q) -> m h j q", h=2, j=PACK), rw_wide[:].rearrange("m j (h q) -> m h j q", h=2)
         )
 
-        for j in range(1, PACK):
-            nc.vector.tensor_copy(k_planes[:, j, :], k_pool[j][:].indirect(offsets[:]))
+        factor = tile("factor", [P, R], F32)
+        nc.gpsimd.tensor_scalar(factor[:], rw_row[:], ts_neg[:, 0:1], 0.0, ALU.mult, ALU.add)
+
+        def keys_along_slots(w, number, tag):
+            turned = bank(number, [P, PACK, P])
+            turn(k_values, w, turned, range(PACK))
+            target = values("k_i_values%d" % w, HALF)
+            nc.scalar.copy(
+                target[:].rearrange("m (e p t) -> m e p t", e=2, t=PACK),
+                turned[:].rearrange("m t p -> m (t p)").bitcast(BF16).rearrange("m (t p e) -> m e p t", t=PACK, e=2),
+            )
+            op = quantized("k_i%d" % w, HALF, tag)
+            return op, target
+
+        gather_plane(k_values, 1, k_pool[1])
+        k_i_first, k_i_first_values = keys_along_slots(0, 4, "k_pool2")
+        gather_plane(k_values, 2, k_pool[2])
+        quantize(k_i_first, E4, 0, k_i_first_values[:])
+        gather_plane(k_values, 3, k_pool[3])
         k_d = quantized("k_d")
         quantize(k_d, E4, 0, k_values[:])
-
-        k_i_first = values("k_i_first", HALF)
-        turn(k_values, 0, k_i_first[:], 6)
-
-        q_d = quantized("q_d")
-        q_values = values("q_values", R)
-        share = 3 * P // 4
-        deal(nc.vector.tensor_copy, q_values, q_raw, 0, share)
-        deal(nc.scalar.copy, q_values, q_raw, share, P)
-        quantize(q_d, E4, 0, q_values[:])
-        k_i_second = values("k_i_second", HALF, "q_raw")
-        turn(k_values, 1, k_i_second[:], 7)
-        k_i = quantized("k_i", tag="q_values")
-        quantize(k_i, E4, 0, k_i_first[:])
-
-        grads = quantized("do_then_ds_r", 2 * W)
-        do_values = values("do_values", R)
-        deal(nc.vector.tensor_copy, do_values, do_raw, 0, share)
-        deal(nc.scalar.copy, do_values, do_raw, share, P)
-        quantize(k_i, E4, HALF, k_i_second[:])
-        quantize(grads, E5, 0, do_values[:])
+        k_i_second, k_i_second_values = keys_along_slots(1, 5, "v_pool0")
+        k_i = [k_i_first, k_i_second]
 
         v_values = values("v_values", W)
-        v_pairs = keep.tile([P, 2 * N * 2], BF16, name="v_pairs", align_bytes=64)
-        v_planes = v_pairs[:].rearrange("p (w s e) -> p w e s", w=2, e=2)
-        v_words = v_pairs[:].bitcast(U32).rearrange("p (w s) -> p s w", w=2)
-
-        slope = []
-        weight = keep.tile([P, PACK, R], F32, name="weight")
-        squared = keep.tile([P, PACK, R], F32, name="squared")
+        gather_plane(v_values, 0, v_pool[0])
+        quantize(k_i_second, E4, 0, k_i_second_values[:])
+        slope = tile("slope", [P, PACK, R], F32, "k_i_values1")
+        weight = tile("weight", [P, PACK, R], F32)
+        squared = tile("squared", [P, PACK, R], F32)
         for t in range(PACK):
-            if t < PACK - 1:
-                nc.vector.tensor_copy(v_planes[:, t // 2, t % 2, :], v_pool[t][:].indirect(offsets[:]))
-            score = product(t, k_d, E4, t, q_d, E4)
-            nc.scalar.activation(weight[:, t, :], score[:], ACT.Tanh, scale=ts_col[:, t:t + 1])
-            nc.scalar.activation(squared[:, t, :], weight[:, t, :], ACT.Square)
-            slope.append(keep.tile([P, R], F32, name="slope%d" % t, tag="slope%d" % t, align_bytes=64))
-            if t == 0:
-                nc.vector.scalar_tensor_tensor(slope[t][:], squared[:, t, :], -1.0, rw_row[:], ALU.add, ALU.mult)
-            else:
-                if t == 1:
-                    nc.gpsimd.tensor_scalar(weight[:, t, :], squared[:, t, :], 1.0, -1.0, ALU.mult, ALU.add)
-                else:
-                    nc.scalar.activation(weight[:, t, :], squared[:, t, :], ACT.Identity, bias=-1.0)
-                nc.gpsimd.tensor_tensor(slope[t][:], weight[:, t, :], rw_row[:], ALU.mult)
-
-        v_e = [quantized("v_e%d" % t, P) for t in range(PACK)]
-        for h in range(2):
-            nc.vector.tensor_copy(
-                v_planes[:, 1, 1, h * HALF:(h + 1) * HALF], v_pool[PACK - 1][:].indirect(list_halves[h])
+            if t:
+                gather_plane(v_values, t, v_pool[t])
+            score = bank(t, [P, R])
+            product(score[:], k_d, E4, t, q_d, E4)
+            nc.scalar.activation(
+                weight[:, t, :].rearrange("m (h j q) -> m h j q", h=2, j=PACK),
+                score[:].rearrange("m (h q j) -> m h j q", h=2, j=PACK),
+                ACT.Tanh,
+                scale=ts_col[:, t:t + 1],
             )
-        for t in range(PACK):
-            block = v_values[:, t * W:(t + 1) * W]
-            nc.scalar.copy(block.bitcast(U32).rearrange("p (s w) -> p s w", w=2), v_words[:, t * P:(t + 1) * P, :])
-            quantize(v_e[t], E4, 0, block)
+            nc.scalar.activation(squared[:, t, :], weight[:, t, :], ACT.Square)
+            if t == 0:
+                nc.vector.scalar_tensor_tensor(slope[:, t, :], squared[:, t, :], -1.0, factor[:], ALU.add, ALU.mult)
+                continue
+            if t == 1:
+                nc.gpsimd.tensor_scalar(
+                    weight[:, t, :], squared[:, t, :], ts_neg[:, t:t + 1], ts_col[:, t:t + 1], ALU.mult, ALU.add
+                )
+            else:
+                nc.scalar.activation(
+                    weight[:, t, :], squared[:, t, :], ACT.Identity, bias=ts_col[:, t:t + 1], scale=ts_neg[:, t:t + 1]
+                )
+            nc.gpsimd.tensor_tensor(slope[:, t, :], weight[:, t, :], rw_row[:], ALU.mult)
 
-        ds = [keep.tile([P, R], BF16, name="ds%d" % t) for t in range(PACK)]
-        for t in range(PACK):
-            dp = product(t, v_e[t], E4, 0, grads, E5)
-            nc.vector.scalar_tensor_tensor(ds[t][:], dp[:], ts_col[:, t:t + 1], slope[t][:], ALU.mult, ALU.mult)
+        v_e = quantized("v_e")
+        quantize(v_e, E4, 0, v_values[:])
 
-        qm_values = values("qm_values", HALF, "v_pool3")
-        qm_r = [quantized("qm_r%d" % c, P, "slope0" if c else None) for c in range(2)]
-        qm_late = quantized("qm_late", HALF)
+        do_e = [quantized("do_e%d" % h, HALF) for h in range(2)]
+        do_values = [values("do_values%d" % h, HALF) for h in range(2)]
+        deal(nc.scalar.copy, do_values[0], do_raw[0], 0, P // 2)
+        quantize(do_e[0], E5, 0, do_values[0][:])
+        deal(nc.vector.tensor_copy, do_values[1], do_raw[1], 0, DO_SHARE)
+        deal(nc.scalar.copy, do_values[1], do_raw[1], DO_SHARE, P // 2)
+        quantize(do_e[1], E5, 0, do_values[1][:])
 
-        def quantize_qm(c):
-            interleave(nc.scalar.copy, qm_values[:, c * W:(c + 1) * W], qm_raw[0][:, :, c * P:(c + 1) * P])
-            quantize(qm_r[c], E4, 0, qm_values[:, c * W:(c + 1) * W])
+        ds_i_values = values("ds_i_values", R, "do_raw1")
+        ds_view = ds_i_values[:].rearrange("m (u e h q t) -> m h u e q t", u=2, e=2, h=2, t=PACK)
+        slope_view = slope[:].rearrange("m t (h u e q) -> m h u e q t", h=2, u=2, e=2)
+        for h in range(2):
+            for u in range(2):
+                dp = bank(2 * h + u, [P, PACK, P])
+                for t in range(PACK):
+                    product(dp[:, t, :], v_e, E4, t, do_e[h], E5, u * P)
+                dp_view = dp[:].rearrange("m t (q e) -> m e q t", e=2)
+                for part in (slice(0, 1), slice(1, 2)) if h and u else (slice(0, 2),):
+                    nc.vector.tensor_tensor(ds_view[:, h, u, part], dp_view[:, part], slope_view[:, h, u, part], ALU.mult)
 
-        ds_r_values = values("ds_r_values", W)
+        qm_values = values("qm_values", D)
+        for c in range(PACK):
+            interleave(nc.scalar.copy, qm_values[:, c * W:(c + 1) * W], qm_raw[:, :, c * P:(c + 1) * P])
 
-        def quantize_ds_r(t):
-            ds_words = ds[t][:].bitcast(F32)
-            ds_turned = bank((5, 6, 7, 4)[t], [P, 2, P])
+        ds_turned = [bank(4 + w, [P, PACK, P]) for w in range(2)]
+        for j in range(PACK):
             for w in range(2):
-                nc.tensor.transpose(ds_turned[:, w, :], ds_words[:, w * P:(w + 1) * P], ident[:])
-            block = ds_r_values[:, t * W:(t + 1) * W]
-            nc.scalar.copy(block.bitcast(F32).rearrange("p (m w) -> p m w", w=2), ds_turned[:].rearrange("p w m -> p m w"))
-            quantize(grads, E5, W + t * P, block)
+                turn(ds_i_values, w, ds_turned[w], [j])
 
-        def store(c):
-            nc.sync.dma_start(out_1[c * P:(c + 1) * P, :], placed[c % WINDOWS][:])
+        ds_r_values = late.tile([P, N * PACK], BF16, name="ds_r_values", align_bytes=64, offset=0)
+
+        def quantized_late(name, width, first):
+            codes = late.tile([P, width], U32, name=name + "_codes", align_bytes=64, offset=4 * first)
+            return codes, tile(name + "_scales", [P, width], U8)
+
+        ds_i = [quantized_late("ds_i%d" % u, HALF, 2 * W + u * HALF) for u in range(2)]
+        qm_first = quantized_late("qm_first", P, 3 * W)
+        quantize(ds_i[0], E5, 0, ds_i_values[:, :2 * W])
+        quantize(qm_first, E4, 0, qm_values[:, :W])
+
+        ds_r = quantized("ds_r")
+        ds_r_view = ds_r_values[:].rearrange("p (g w e a j) -> p w g e a j", w=2, e=2, a=RUN, j=PACK)
+
+        def copy_turned(h, w, copy):
+            groups = slice(h * RUN, (h + 1) * RUN)
+            halves = ds_turned[w][:].rearrange("p j m -> p (j m)").bitcast(BF16)
+            copy(ds_r_view[:, w, groups], halves.rearrange("p (j g a e) -> p g e a j", j=PACK, a=RUN, e=2)[:, groups])
+
+        def quantize_ds_r(h):
+            quantize(ds_r, E5, h * HALF, ds_r_values[:, h * 2 * W:(h + 1) * 2 * W])
+
+        gq_rows = out_0[0].rearrange("(m j) d -> m j d", j=PACK)
+        gq_out = [tile("gq_out%d" % u, [P, 2, D], F32) for u in range(2)]
+
+        def queries_gradient(u, e, number, copy):
+            gq = bank(number, [P, 2, HALF])
+            for w in range(2):
+                product(gq[:, w, :], ds_i[u], E5, e, k_i[w], E4)
+            copy(
+                gq_out[u][:, e, :].rearrange("m (p j) -> m p j", j=PACK),
+                gq[:].rearrange("m w (e p) -> m p (w e)", e=2),
+            )
+
+        def store_queries(u):
+            nc.sync.dma_start(gq_rows[:, 2 * u:2 * u + 2, :], gq_out[u][:])
+
+        qm_rest = quantized("qm_rest", 3 * P)
 
         def keys_gradient(c, first, end, number, copy, tag=None):
-            stationary, block = (qm_r[c], 0) if c < 2 else (qm_late, c - 2)
-            dk = product(number, stationary, E4, block, grads, E5, W + first, end - first)
-            name = "dk_listed%d_%d" % (c, first)
-            dk_listed = keep.tile([P, end - first], F32, name=name, tag=tag or name, align_bytes=64)
+            stationary, block = (qm_rest, c - 1) if c else (qm_first, 0)
+            dk = bank(number, [P, end - first])
+            product(dk[:], stationary, E4, block, ds_r, E5, first)
+            dk_listed = tile("dk_listed%d_%d" % (c, first), [P, end - first], F32, tag)
             copy(dk_listed[:], dk[:])
             return dk_listed
 
         def place_by_scalar(c, first, end, dk_listed):
-            nc.scalar.activation(placed[c % WINDOWS][:].indirect(offsets[:, first // 16:end // 16]), dk_listed, ACT.Copy)
+            nc.scalar.activation(placed[c][:].indirect(offsets[:, first // 16:end // 16]), dk_listed, ACT.Copy)
 
-        def place_by_vector(c, first, end, dk_listed):
-            nc.vector.tensor_copy(placed[c % WINDOWS][:].indirect(offsets[:, first // 16:end // 16]), dk_listed)
+        def place_by_vector(c, dk_listed):
+            nc.vector.tensor_copy(placed[c][:].indirect(offsets[:]), dk_listed)
 
-        quantize_qm(0)
-        quantize_qm(1)
+        def store_keys(c):
+            nc.sync.dma_start(out_1[c * P:(c + 1) * P, :], placed[c][:])
+
+        copy_turned(0, 0, nc.vector.tensor_copy)
+        copy_turned(0, 1, nc.scalar.copy)
+        quantize_ds_r(0)
+        copy_turned(1, 0, nc.scalar.copy)
+        copy_turned(1, 1, nc.scalar.copy)
+        quantize(ds_i[1], E5, 0, ds_i_values[:, 2 * W:])
+        dk_first = keys_gradient(0, 0, HALF, 2, nc.vector.tensor_copy)
+        quantize(qm_rest, E4, 0, qm_values[:, W:])
+        queries_gradient(0, 0, 6, nc.scalar.copy)
+        queries_gradient(0, 1, 7, nc.vector.tensor_copy)
+        store_queries(0)
+        place_by_scalar(0, 0, HALF, dk_first[:])
+        quantize_ds_r(1)
+        queries_gradient(1, 0, 0, nc.vector.tensor_copy)
+        queries_gradient(1, 1, 1, nc.vector.tensor_copy)
+        store_queries(1)
+        place_by_scalar(0, HALF, N, keys_gradient(0, HALF, N, 3, nc.vector.tensor_copy)[:])
+        store_keys(0)
+        place_by_vector(1, keys_gradient(1, 0, N, 6, nc.vector.tensor_copy)[:])
+        store_keys(1)
+        dk_2 = keys_gradient(2, 0, N, 7, nc.scalar.copy, "dk_listed0_256")
         for h in range(2):
-            quantize_ds_r(2 * h)
-            quantize_ds_r(2 * h + 1)
-            part = keys_gradient(0, h * HALF, (h + 1) * HALF, h, nc.vector.tensor_copy, ("qm_raw0", None)[h])
-            place_by_scalar(0, h * HALF, (h + 1) * HALF, part[:])
-        store(0)
-        qm_late_values = values("qm_late_values", HALF, "slope3")
-        interleave(nc.vector.tensor_copy, qm_late_values[:], qm_raw[1][:])
-        quantize(qm_late, E4, 0, qm_late_values[:])
-        place_by_vector(1, 0, N, keys_gradient(1, 0, N, 2, nc.vector.tensor_copy)[:])
-        store(1)
-        place_by_scalar(2, 0, HALF, keys_gradient(2, 0, HALF, 3, nc.scalar.copy, "dk_listed0_256")[:])
-        place_by_vector(2, HALF, N, keys_gradient(2, HALF, N, 4, nc.vector.tensor_copy)[:])
-        store(2)
-
-        ds_i_values = values("ds_i_values", W, "dk_listed0_256")
-        for w in range(2):
-            turn(ds_r_values, w, ds_i_values[:, w * 2 * W:(w + 1) * 2 * W], (2, 4)[w])
-        dk_3 = keys_gradient(3, 0, N, 2, nc.vector.tensor_copy)
-        ds_i = [quantized("ds_i0", HALF, "dk_listed2_256"), quantized("ds_i1", HALF)]
-        for w in range(2):
-            quantize(ds_i[w], E5, 0, ds_i_values[:, w * 2 * W:(w + 1) * 2 * W])
-        place_by_vector(3, 0, N, dk_3[:])
-
-        gq_rows = out_0[0].rearrange("(m u) d -> m u d", u=PACK)
-        for pair in range(2):
-            gq_out = keep.tile([P, 2, D], F32, name="gq_out%d" % pair)
-            for e in range(2):
-                u = 2 * pair + e
-                gq = product((0, 1, 5, 6)[u], ds_i[pair], E5, e, k_i, E4)
-                nc.scalar.copy(
-                    gq_out[:, e, :].rearrange("p (c j) -> p c j", j=PACK),
-                    gq[:].rearrange("p (j c) -> p c j", j=PACK),
-                )
-            nc.scalar.dma_start(gq_rows[:, 2 * pair:2 * pair + 2, :], gq_out[:])
-        store(3)
+            place_by_scalar(2, h * HALF, (h + 1) * HALF, dk_2[:, h * HALF:(h + 1) * HALF])
+        store_keys(2)
+        place_by_vector(3, keys_gradient(3, 0, N, 4, nc.vector.tensor_copy, "dk_listed1_0")[:])
+        store_keys(3)

@@ -115,18 +115,23 @@ def tile_attend_gat_tnh_qk_ts_kernel(tc, qT, kT, vT, doT, rw, ts, qm, offs, out_
         ident = tile("ident", [P, P], F32)
         make_identity(nc, ident[:])
 
-        placed = [tile("placed%d" % c, [P, T], F32) for c in range(PACK)]
-        for c in range(PACK):
-            engine = nc.vector if c < 1 else nc.gpsimd
-            engine.memset(placed[c][:].bitcast(I32), 0)
+        placed = []
+
+        def zero_window(engine, tag=None):
+            placed.append(tile("placed%d" % len(placed), [P, T], F32, tag))
+            engine.memset(placed[-1][:].bitcast(I32), 0)
+
+        zero_window(nc.vector)
 
         q_values = values("q_values", R)
         interleave(nc.vector.tensor_copy, q_values[:], q_raw[:])
         q_d = quantized("q_d")
         quantize(q_d, E4, 0, q_values[:])
+        zero_window(nc.gpsimd, "q_values")
 
         k_values = values("k_values", W)
         gather_plane(k_values, 0, k_pool[0])
+        zero_window(nc.gpsimd, "k_pool0")
 
         ts_listed = tile("ts_listed", [P, N], F32)
         nc.vector.tensor_copy(
@@ -151,31 +156,30 @@ def tile_attend_gat_tnh_qk_ts_kernel(tc, qT, kT, vT, doT, rw, ts, qm, offs, out_
         factor = tile("factor", [P, R], F32)
         nc.gpsimd.tensor_scalar(factor[:], rw_row[:], ts_neg[:, 0:1], 0.0, ALU.mult, ALU.add)
 
-        def keys_along_slots(w, number, tag):
-            turned = bank(number, [P, PACK, P])
+        k_i_values = values("k_i_values", D)
+
+        def turn_keys(w):
+            turned = bank(4 + w, [P, PACK, P])
             turn(k_values, w, turned, range(PACK))
-            target = values("k_i_values%d" % w, HALF)
             nc.scalar.copy(
-                target[:].rearrange("m (e p t) -> m e p t", e=2, t=PACK),
+                k_i_values[:, w * 2 * W:(w + 1) * 2 * W].rearrange("m (e p t) -> m e p t", e=2, t=PACK),
                 turned[:].rearrange("m t p -> m (t p)").bitcast(BF16).rearrange("m (t p e) -> m e p t", t=PACK, e=2),
             )
-            op = quantized("k_i%d" % w, HALF, tag)
-            return op, target
 
         gather_plane(k_values, 1, k_pool[1])
-        k_i_first, k_i_first_values = keys_along_slots(0, 4, "k_pool2")
+        zero_window(nc.gpsimd, "k_pool1")
+        turn_keys(0)
         gather_plane(k_values, 2, k_pool[2])
-        quantize(k_i_first, E4, 0, k_i_first_values[:])
         gather_plane(k_values, 3, k_pool[3])
         k_d = quantized("k_d")
         quantize(k_d, E4, 0, k_values[:])
-        k_i_second, k_i_second_values = keys_along_slots(1, 5, "v_pool0")
-        k_i = [k_i_first, k_i_second]
+        turn_keys(1)
 
         v_values = values("v_values", W)
         gather_plane(v_values, 0, v_pool[0])
-        quantize(k_i_second, E4, 0, k_i_second_values[:])
-        slope = tile("slope", [P, PACK, R], F32, "k_i_values1")
+        k_i = quantized("k_i", D, "v_pool0")
+        quantize(k_i, E4, 0, k_i_values[:])
+        slope = tile("slope", [P, PACK, R], F32, "k_i_values")
         weight = tile("weight", [P, PACK, R], F32)
         squared = tile("squared", [P, PACK, R], F32)
         for t in range(PACK):
@@ -193,7 +197,7 @@ def tile_attend_gat_tnh_qk_ts_kernel(tc, qT, kT, vT, doT, rw, ts, qm, offs, out_
             if t == 0:
                 nc.vector.scalar_tensor_tensor(slope[:, t, :], squared[:, t, :], -1.0, factor[:], ALU.add, ALU.mult)
                 continue
-            if t == 1:
+            if t < PACK - 1:
                 nc.gpsimd.tensor_scalar(
                     weight[:, t, :], squared[:, t, :], ts_neg[:, t:t + 1], ts_col[:, t:t + 1], ALU.mult, ALU.add
                 )
@@ -261,12 +265,11 @@ def tile_attend_gat_tnh_qk_ts_kernel(tc, qT, kT, vT, doT, rw, ts, qm, offs, out_
         gq_out = [tile("gq_out%d" % u, [P, 2, D], F32) for u in range(2)]
 
         def queries_gradient(u, e, number, copy):
-            gq = bank(number, [P, 2, HALF])
-            for w in range(2):
-                product(gq[:, w, :], ds_i[u], E5, e, k_i[w], E4)
+            gq = bank(number, [P, D])
+            product(gq[:], ds_i[u], E5, e, k_i, E4)
             copy(
                 gq_out[u][:, e, :].rearrange("m (p j) -> m p j", j=PACK),
-                gq[:].rearrange("m w (e p) -> m p (w e)", e=2),
+                gq[:].rearrange("m (j p) -> m p j", j=PACK),
             )
 
         def store_queries(u):

@@ -98,12 +98,14 @@ def tile_attend_gat_tnh_qk_ts_kernel(tc, qT, kT, vT, doT, rw, ts, qm, offs, out_
 
         k_rows = kT.rearrange("(p j) t -> p j t", j=PACK)
         v_rows = vT.rearrange("(p j) t -> p j t", j=PACK)
-        q_raw = load("q_raw", [P, PACK, R], qT[0].rearrange("(p j) r -> p j r", j=PACK))
         nc.sync.dma_start(offsets[:], offs)
         k_pool = [load("k_pool0", [P, T], k_rows[:, 0, :])]
+        k_pool.append(load("k_pool1", [P, T], k_rows[:, 1, :]))
         nc.sync.dma_start(ts_pool[0:1, :], ts[0:1, :])
         nc.sync.dma_start(rw_col[:], rw[0].rearrange("(p t) o -> p (t o)", t=PACK))
-        k_pool += [load("k_pool%d" % j, [P, T], k_rows[:, j, :]) for j in range(1, PACK)]
+        k_pool += [load("k_pool%d" % j, [P, T], k_rows[:, j, :]) for j in range(2, PACK)]
+        q_rows = qT[0].rearrange("(p j) r -> p j r", j=PACK)
+        q_raw = [load("q_raw%d" % h, [P, PACK, HALF], q_rows[:, :, h * HALF:(h + 1) * HALF]) for h in range(2)]
         v_pool = [load("v_pool%d" % j, [P, T], v_rows[:, j, :]) for j in range(PACK)]
         do_rows = doT[0].rearrange("(p j) r -> p j r", j=PACK)
         do_raw = [load("do_raw%d" % h, [P, PACK, HALF], do_rows[:, :, h * HALF:(h + 1) * HALF]) for h in range(2)]
@@ -122,12 +124,7 @@ def tile_attend_gat_tnh_qk_ts_kernel(tc, qT, kT, vT, doT, rw, ts, qm, offs, out_
             engine.memset(placed[-1][:].bitcast(I32), 0)
 
         zero_window(nc.vector)
-
-        q_values = values("q_values", R)
-        interleave(nc.vector.tensor_copy, q_values[:], q_raw[:])
-        q_d = quantized("q_d")
-        quantize(q_d, E4, 0, q_values[:])
-        zero_window(nc.gpsimd, "q_values")
+        zero_window(nc.vector)
 
         k_values = values("k_values", W)
         gather_plane(k_values, 0, k_pool[0])
@@ -137,6 +134,7 @@ def tile_attend_gat_tnh_qk_ts_kernel(tc, qT, kT, vT, doT, rw, ts, qm, offs, out_
         nc.vector.tensor_copy(
             ts_listed[:].rearrange("p (t g a) -> p g t a", t=PACK, a=RUN), ts_pool[:].indirect(offsets[:])
         )
+        zero_window(nc.gpsimd, "ts_pool")
         ts_turned = bank(6, [P, PACK, P])
         for t in range(PACK):
             nc.tensor.transpose(ts_turned[:, t, :], ts_listed[:, t * P:(t + 1) * P], ident[:])
@@ -153,60 +151,66 @@ def tile_attend_gat_tnh_qk_ts_kernel(tc, qT, kT, vT, doT, rw, ts, qm, offs, out_
             rw_row[:].rearrange("m (h j q) -> m h j q", h=2, j=PACK), rw_wide[:].rearrange("m j (h q) -> m h j q", h=2)
         )
 
-        factor = tile("factor", [P, R], F32)
-        nc.gpsimd.tensor_scalar(factor[:], rw_row[:], ts_neg[:, 0:1], 0.0, ALU.mult, ALU.add)
+        k_i_values = []
 
-        k_i_values = values("k_i_values", D)
-
-        def turn_keys(w):
+        def turn_keys(w, tag=None):
+            k_i_values.append(values("k_i_values%d" % w, HALF, tag))
             turned = bank(4 + w, [P, PACK, P])
             turn(k_values, w, turned, range(PACK))
             nc.scalar.copy(
-                k_i_values[:, w * 2 * W:(w + 1) * 2 * W].rearrange("m (e p t) -> m e p t", e=2, t=PACK),
+                k_i_values[w][:].rearrange("m (e p t) -> m e p t", e=2, t=PACK),
                 turned[:].rearrange("m t p -> m (t p)").bitcast(BF16).rearrange("m (t p e) -> m e p t", t=PACK, e=2),
             )
 
         gather_plane(k_values, 1, k_pool[1])
-        zero_window(nc.gpsimd, "k_pool1")
         turn_keys(0)
         gather_plane(k_values, 2, k_pool[2])
         gather_plane(k_values, 3, k_pool[3])
         k_d = quantized("k_d")
         quantize(k_d, E4, 0, k_values[:])
-        turn_keys(1)
+
+        q_d = [quantized("q_d%d" % h, HALF) for h in range(2)]
+        q_values = [values("q_values%d" % h, HALF) for h in range(2)]
+        interleave(nc.scalar.copy, q_values[0][:], q_raw[0][:])
+        turn_keys(1, "q_raw0")
+        quantize(q_d[0], E4, 0, q_values[0][:])
+        interleave(nc.vector.tensor_copy, q_values[1][:], q_raw[1][:])
+        quantize(q_d[1], E4, 0, q_values[1][:])
+        k_i = quantized("k_i", D, "q_values1")
+        for w in range(2):
+            quantize(k_i, E4, w * HALF, k_i_values[w][:])
+
+        slope = [tile("slope%d" % h, [P, PACK, HALF], F32) for h in range(2)]
+        for h in range(2):
+            weight = tile("weight%d" % h, [P, PACK, HALF], F32)
+            squared = tile("squared%d" % h, [P, PACK, HALF], F32)
+            for pair in range(2):
+                places = range(2 * pair, 2 * pair + 2)
+                score = bank(pair, [P, 2, HALF])
+                for t in places:
+                    product(score[:, t % 2, :], k_d, E4, t, q_d[h], E4)
+                for t in places:
+                    nc.scalar.activation(
+                        weight[:, t, :].rearrange("m (j q) -> m j q", j=PACK),
+                        score[:, t % 2, :].rearrange("m (q j) -> m j q", j=PACK),
+                        ACT.Tanh,
+                        scale=ts_col[:, t:t + 1],
+                    )
+            for pair in range(2):
+                both = slice(2 * pair, 2 * pair + 2)
+                nc.scalar.activation(squared[:, both, :], weight[:, both, :], ACT.Square)
+                for t in range(2 * pair, 2 * pair + 2):
+                    plus, minus = ts_col[:, t:t + 1], ts_neg[:, t:t + 1]
+                    if h == 0 and pair == 0:
+                        nc.gpsimd.tensor_scalar(weight[:, t, :], squared[:, t, :], minus, plus, ALU.mult, ALU.add)
+                    else:
+                        nc.scalar.activation(weight[:, t, :], squared[:, t, :], ACT.Identity, bias=plus, scale=minus)
+                gates = rw_row[:, h * HALF:(h + 1) * HALF].unsqueeze(1).to_broadcast([P, 2, HALF])
+                nc.gpsimd.tensor_tensor(slope[h][:, both, :], weight[:, both, :], gates, ALU.mult)
 
         v_values = values("v_values", W)
-        gather_plane(v_values, 0, v_pool[0])
-        k_i = quantized("k_i", D, "v_pool0")
-        quantize(k_i, E4, 0, k_i_values[:])
-        slope = tile("slope", [P, PACK, R], F32, "k_i_values")
-        weight = tile("weight", [P, PACK, R], F32)
-        squared = tile("squared", [P, PACK, R], F32)
-        for t in range(PACK):
-            if t:
-                gather_plane(v_values, t, v_pool[t])
-            score = bank(t, [P, R])
-            product(score[:], k_d, E4, t, q_d, E4)
-            nc.scalar.activation(
-                weight[:, t, :].rearrange("m (h j q) -> m h j q", h=2, j=PACK),
-                score[:].rearrange("m (h q j) -> m h j q", h=2, j=PACK),
-                ACT.Tanh,
-                scale=ts_col[:, t:t + 1],
-            )
-            nc.scalar.activation(squared[:, t, :], weight[:, t, :], ACT.Square)
-            if t == 0:
-                nc.vector.scalar_tensor_tensor(slope[:, t, :], squared[:, t, :], -1.0, factor[:], ALU.add, ALU.mult)
-                continue
-            if t < PACK - 1:
-                nc.gpsimd.tensor_scalar(
-                    weight[:, t, :], squared[:, t, :], ts_neg[:, t:t + 1], ts_col[:, t:t + 1], ALU.mult, ALU.add
-                )
-            else:
-                nc.scalar.activation(
-                    weight[:, t, :], squared[:, t, :], ACT.Identity, bias=ts_col[:, t:t + 1], scale=ts_neg[:, t:t + 1]
-                )
-            nc.gpsimd.tensor_tensor(slope[:, t, :], weight[:, t, :], rw_row[:], ALU.mult)
-
+        for j in range(PACK):
+            gather_plane(v_values, j, v_pool[j])
         v_e = quantized("v_e")
         quantize(v_e, E4, 0, v_values[:])
 
@@ -220,15 +224,15 @@ def tile_attend_gat_tnh_qk_ts_kernel(tc, qT, kT, vT, doT, rw, ts, qm, offs, out_
 
         ds_i_values = values("ds_i_values", R, "do_raw1")
         ds_view = ds_i_values[:].rearrange("m (u e h q t) -> m h u e q t", u=2, e=2, h=2, t=PACK)
-        slope_view = slope[:].rearrange("m t (h u e q) -> m h u e q t", h=2, u=2, e=2)
         for h in range(2):
+            slope_view = slope[h][:].rearrange("m t (u e q) -> m u e q t", u=2, e=2)
             for u in range(2):
                 dp = bank(2 * h + u, [P, PACK, P])
                 for t in range(PACK):
                     product(dp[:, t, :], v_e, E4, t, do_e[h], E5, u * P)
                 dp_view = dp[:].rearrange("m t (q e) -> m e q t", e=2)
                 for part in (slice(0, 1), slice(1, 2)) if h and u else (slice(0, 2),):
-                    nc.vector.tensor_tensor(ds_view[:, h, u, part], dp_view[:, part], slope_view[:, h, u, part], ALU.mult)
+                    nc.vector.tensor_tensor(ds_view[:, h, u, part], dp_view[:, part], slope_view[:, u, part], ALU.mult)
 
         qm_values = values("qm_values", D)
         for c in range(PACK):

@@ -117,24 +117,24 @@ def tile_attend_gat_tnh_qk_ts_kernel(tc, qT, kT, vT, doT, rw, ts, qm, offs, out_
         ident = tile("ident", [P, P], F32)
         make_identity(nc, ident[:])
 
-        placed = []
+        placed = {}
 
-        def zero_window(engine, tag=None):
-            placed.append(tile("placed%d" % len(placed), [P, T], F32, tag))
-            engine.memset(placed[-1][:].bitcast(I32), 0)
+        def zero_window(c, engine, window):
+            placed[c] = window
+            engine.memset(window[:].bitcast(I32), 0)
 
-        zero_window(nc.vector)
-        zero_window(nc.vector)
+        for c in (1, 3):
+            zero_window(c, nc.vector, late.tile([P, T], F32, name="placed%d" % c, align_bytes=64, offset=4 * T * (c + 1) // 2))
 
         k_values = values("k_values", W)
         gather_plane(k_values, 0, k_pool[0])
-        zero_window(nc.gpsimd, "k_pool0")
+        zero_window(0, nc.gpsimd, tile("placed0", [P, T], F32, "k_pool0"))
 
         ts_listed = tile("ts_listed", [P, N], F32)
         nc.vector.tensor_copy(
             ts_listed[:].rearrange("p (t g a) -> p g t a", t=PACK, a=RUN), ts_pool[:].indirect(offsets[:])
         )
-        zero_window(nc.gpsimd, "ts_pool")
+        zero_window(2, nc.gpsimd, tile("placed2", [P, T], F32, "ts_pool"))
         ts_turned = bank(6, [P, PACK, P])
         for t in range(PACK):
             nc.tensor.transpose(ts_turned[:, t, :], ts_listed[:, t * P:(t + 1) * P], ident[:])

@@ -98,8 +98,8 @@ def tile_attend_gat_tnh_qk_ts_kernel(tc, qT, kT, vT, doT, rw, ts, qm, offs, out_
 
         k_rows = kT.rearrange("(p j) t -> p j t", j=PACK)
         v_rows = vT.rearrange("(p j) t -> p j t", j=PACK)
-        nc.sync.dma_start(offsets[:], offs)
         k_pool = [load("k_pool0", [P, T], k_rows[:, 0, :])]
+        nc.sync.dma_start(offsets[:], offs)
         k_pool.append(load("k_pool1", [P, T], k_rows[:, 1, :]))
         nc.sync.dma_start(ts_pool[0:1, :], ts[0:1, :])
         nc.sync.dma_start(rw_col[:], rw[0].rearrange("(p t) o -> p (t o)", t=PACK))
@@ -223,16 +223,16 @@ def tile_attend_gat_tnh_qk_ts_kernel(tc, qT, kT, vT, doT, rw, ts, qm, offs, out_
         quantize(do_e[1], E5, 0, do_values[1][:])
 
         ds_i_values = values("ds_i_values", R, "do_raw1")
-        ds_view = ds_i_values[:].rearrange("m (u e h q t) -> m h u e q t", u=2, e=2, h=2, t=PACK)
+        ds_view = ds_i_values[:].rearrange("m (u e h c i t) -> m h u e c t i", u=2, e=2, h=2, i=PACK, t=PACK)
         for h in range(2):
-            slope_view = slope[h][:].rearrange("m t (u e q) -> m u e q t", u=2, e=2)
+            slope_view = slope[h][:].rearrange("m t (u e c i) -> m u e c t i", u=2, e=2, i=PACK)
             for u in range(2):
                 dp = bank(2 * h + u, [P, PACK, P])
                 for t in range(PACK):
                     product(dp[:, t, :], v_e, E4, t, do_e[h], E5, u * P)
-                dp_view = dp[:].rearrange("m t (q e) -> m e q t", e=2)
-                for part in (slice(0, 1), slice(1, 2)) if h and u else (slice(0, 2),):
-                    nc.vector.tensor_tensor(ds_view[:, h, u, part], dp_view[:, part], slope_view[:, u, part], ALU.mult)
+                dp_view = dp[:].rearrange("m t (c i e) -> m e c t i", i=PACK, e=2)
+                for e in range(2):
+                    nc.vector.tensor_tensor(ds_view[:, h, u, e], dp_view[:, e], slope_view[:, u, e], ALU.mult)
 
         qm_values = values("qm_values", D)
         for c in range(PACK):
@@ -311,8 +311,8 @@ def tile_attend_gat_tnh_qk_ts_kernel(tc, qT, kT, vT, doT, rw, ts, qm, offs, out_
         store_queries(0)
         place_by_scalar(0, 0, HALF, dk_first[:])
         quantize_ds_r(1)
-        queries_gradient(1, 0, 0, nc.vector.tensor_copy)
-        queries_gradient(1, 1, 1, nc.vector.tensor_copy)
+        queries_gradient(1, 0, 2, nc.vector.tensor_copy)
+        queries_gradient(1, 1, 7, nc.vector.tensor_copy)
         store_queries(1)
         place_by_scalar(0, HALF, N, keys_gradient(0, HALF, N, 3, nc.vector.tensor_copy)[:])
         store_keys(0)

@@ -281,22 +281,27 @@ def tile_attend_gat_tnh_qk_ts_kernel(tc, qT, kT, vT, doT, rw, ts, qm, offs, out_
 
         qm_rest = quantized("qm_rest", 3 * P)
 
-        def keys_gradient(c, first, end, number, copy, tag=None):
+        dk_listed = [tile("dk_listed%d" % c, [P, N], F32) for c in range(PACK)]
+
+        def keys_gradient(c, first, end, number):
             stationary, block = (qm_rest, c - 1) if c else (qm_first, 0)
             dk = bank(number, [P, end - first])
             product(dk[:], stationary, E4, block, ds_r, E5, first)
-            dk_listed = tile("dk_listed%d_%d" % (c, first), [P, end - first], F32, tag)
-            copy(dk_listed[:], dk[:])
-            return dk_listed
+            return dk
 
-        def place_by_scalar(c, first, end, dk_listed):
-            nc.scalar.activation(placed[c][:].indirect(offsets[:, first // 16:end // 16]), dk_listed, ACT.Copy)
+        def place_by_scalar(c, h):
+            window = placed[c][:].indirect(offsets[:, h * HALF // 16:(h + 1) * HALF // 16])
+            nc.scalar.activation(window, dk_listed[c][:, h * HALF:(h + 1) * HALF], ACT.Copy)
 
-        def place_by_vector(c, dk_listed):
-            nc.vector.tensor_copy(placed[c][:].indirect(offsets[:]), dk_listed)
+        def place_by_vector(c):
+            nc.vector.tensor_copy(placed[c][:].indirect(offsets[:]), dk_listed[c][:])
 
-        def store_keys(c):
-            nc.sync.dma_start(out_1[c * P:(c + 1) * P, :], placed[c][:])
+        def store_keys(c, queue):
+            queue.dma_start(out_1[c * P:(c + 1) * P, :], placed[c][:])
+
+        def half_by_vector(c, h, number):
+            dk = keys_gradient(c, h * HALF, (h + 1) * HALF, number)
+            nc.vector.tensor_copy(dk_listed[c][:, h * HALF:(h + 1) * HALF], dk[:])
 
         copy_turned(0, 0, nc.vector.tensor_copy)
         copy_turned(0, 1, nc.scalar.copy)
@@ -304,23 +309,29 @@ def tile_attend_gat_tnh_qk_ts_kernel(tc, qT, kT, vT, doT, rw, ts, qm, offs, out_
         copy_turned(1, 0, nc.scalar.copy)
         copy_turned(1, 1, nc.scalar.copy)
         quantize(ds_i[1], E5, 0, ds_i_values[:, 2 * W:])
-        dk_first = keys_gradient(0, 0, HALF, 2, nc.vector.tensor_copy)
+        half_by_vector(0, 0, 2)
         quantize(qm_rest, E4, 0, qm_values[:, W:])
         queries_gradient(0, 0, 6, nc.scalar.copy)
         queries_gradient(0, 1, 7, nc.vector.tensor_copy)
         store_queries(0)
-        place_by_scalar(0, 0, HALF, dk_first[:])
+        place_by_scalar(0, 0)
         quantize_ds_r(1)
         queries_gradient(1, 0, 2, nc.vector.tensor_copy)
         queries_gradient(1, 1, 7, nc.vector.tensor_copy)
         store_queries(1)
-        place_by_scalar(0, HALF, N, keys_gradient(0, HALF, N, 3, nc.vector.tensor_copy)[:])
-        store_keys(0)
-        place_by_vector(1, keys_gradient(1, 0, N, 6, nc.vector.tensor_copy)[:])
-        store_keys(1)
-        dk_2 = keys_gradient(2, 0, N, 7, nc.scalar.copy, "dk_listed0_256")
+        half_by_vector(0, 1, 3)
+        place_by_scalar(0, 1)
+        store_keys(0, nc.sync)
+        nc.vector.tensor_copy(dk_listed[1][:], keys_gradient(1, 0, N, 6)[:])
+        place_by_vector(1)
+        store_keys(1, nc.sync)
+        dk_2 = keys_gradient(2, 0, N, 3)
         for h in range(2):
-            place_by_scalar(2, h * HALF, (h + 1) * HALF, dk_2[:, h * HALF:(h + 1) * HALF])
-        store_keys(2)
-        place_by_vector(3, keys_gradient(3, 0, N, 4, nc.vector.tensor_copy, "dk_listed1_0")[:])
-        store_keys(3)
+            nc.scalar.copy(dk_listed[2][:, h * HALF:(h + 1) * HALF], dk_2[:, h * HALF:(h + 1) * HALF])
+        for h in range(2):
+            place_by_scalar(2, h)
+        store_keys(2, nc.scalar)
+        half_by_vector(3, 0, 7)
+        half_by_vector(3, 1, 6)
+        place_by_vector(3)
+        store_keys(3, nc.sync)

@@ -299,9 +299,9 @@ def tile_attend_gat_tnh_qk_ts_kernel(tc, qT, kT, vT, doT, rw, ts, qm, offs, out_
         def store_keys(c, queue):
             queue.dma_start(out_1[c * P:(c + 1) * P, :], placed[c][:])
 
-        def half_by_vector(c, h, number):
+        def half_of_keys(c, h, number, copy):
             dk = keys_gradient(c, h * HALF, (h + 1) * HALF, number)
-            nc.vector.tensor_copy(dk_listed[c][:, h * HALF:(h + 1) * HALF], dk[:])
+            copy(dk_listed[c][:, h * HALF:(h + 1) * HALF], dk[:])
 
         copy_turned(0, 0, nc.vector.tensor_copy)
         copy_turned(0, 1, nc.scalar.copy)
@@ -309,7 +309,7 @@ def tile_attend_gat_tnh_qk_ts_kernel(tc, qT, kT, vT, doT, rw, ts, qm, offs, out_
         copy_turned(1, 0, nc.scalar.copy)
         copy_turned(1, 1, nc.scalar.copy)
         quantize(ds_i[1], E5, 0, ds_i_values[:, 2 * W:])
-        half_by_vector(0, 0, 2)
+        half_of_keys(0, 0, 2, nc.vector.tensor_copy)
         quantize(qm_rest, E4, 0, qm_values[:, W:])
         queries_gradient(0, 0, 6, nc.scalar.copy)
         queries_gradient(0, 1, 7, nc.vector.tensor_copy)
@@ -319,7 +319,7 @@ def tile_attend_gat_tnh_qk_ts_kernel(tc, qT, kT, vT, doT, rw, ts, qm, offs, out_
         queries_gradient(1, 0, 2, nc.vector.tensor_copy)
         queries_gradient(1, 1, 7, nc.vector.tensor_copy)
         store_queries(1)
-        half_by_vector(0, 1, 3)
+        half_of_keys(0, 1, 3, nc.vector.tensor_copy)
         place_by_scalar(0, 1)
         store_keys(0, nc.sync)
         nc.vector.tensor_copy(dk_listed[1][:], keys_gradient(1, 0, N, 6)[:])
@@ -328,10 +328,10 @@ def tile_attend_gat_tnh_qk_ts_kernel(tc, qT, kT, vT, doT, rw, ts, qm, offs, out_
         dk_2 = keys_gradient(2, 0, N, 3)
         for h in range(2):
             nc.scalar.copy(dk_listed[2][:, h * HALF:(h + 1) * HALF], dk_2[:, h * HALF:(h + 1) * HALF])
+        half_of_keys(3, 0, 7, nc.vector.tensor_copy)
+        half_of_keys(3, 1, 6, nc.scalar.copy)
         for h in range(2):
             place_by_scalar(2, h)
         store_keys(2, nc.scalar)
-        half_by_vector(3, 0, 7)
-        half_by_vector(3, 1, 6)
         place_by_vector(3)
         store_keys(3, nc.sync)

@@ -234,36 +234,40 @@ def tile_attend_gat_tnh_qk_ts_kernel(tc, qT, kT, vT, doT, rw, ts, qm, offs, out_
                 for e in range(2):
                     nc.vector.tensor_tensor(ds_view[:, h, u, e], dp_view[:, e], slope_view[:, u, e], ALU.mult)
 
-        qm_values = values("qm_values", D)
+        qm_values = [values("qm_values0", P), values("qm_values1", P), values("qm_values2", 2 * P)]
         for c in range(PACK):
-            interleave(nc.scalar.copy, qm_values[:, c * W:(c + 1) * W], qm_raw[:, :, c * P:(c + 1) * P])
+            target = qm_values[min(c, 2)][:, (c // 3) * W:(c // 3 + 1) * W]
+            interleave(nc.scalar.copy, target, qm_raw[:, :, c * P:(c + 1) * P])
 
         ds_turned = [bank(4 + w, [P, PACK, P]) for w in range(2)]
         for j in range(PACK):
             for w in range(2):
                 turn(ds_i_values, w, ds_turned[w], [j])
 
-        ds_r_values = late.tile([P, N * PACK], BF16, name="ds_r_values", align_bytes=64, offset=0)
+        ds_r_values = [
+            late.tile([P, HALF * PACK], BF16, name="ds_r_values%d" % h, align_bytes=64, offset=h * 4 * W)
+            for h in range(2)
+        ]
 
         def quantized_late(name, width, first):
             codes = late.tile([P, width], U32, name=name + "_codes", align_bytes=64, offset=4 * first)
             return codes, tile(name + "_scales", [P, width], U8)
 
-        ds_i = [quantized_late("ds_i%d" % u, HALF, 2 * W + u * HALF) for u in range(2)]
-        qm_first = quantized_late("qm_first", P, 3 * W)
+        ds_i = [quantized_late("ds_i0", HALF, 2 * W)]
+        qm_r = [quantized_late("qm_r%d" % c, P, 3 * W + c * P) for c in range(2)]
         quantize(ds_i[0], E5, 0, ds_i_values[:, :2 * W])
-        quantize(qm_first, E4, 0, qm_values[:, :W])
+        quantize(qm_r[0], E4, 0, qm_values[0][:])
 
         ds_r = quantized("ds_r")
-        ds_r_view = ds_r_values[:].rearrange("p (g w e a j) -> p w g e a j", w=2, e=2, a=RUN, j=PACK)
 
         def copy_turned(h, w, copy):
-            groups = slice(h * RUN, (h + 1) * RUN)
+            target = ds_r_values[h][:].rearrange("p (g w e a j) -> p w g e a j", w=2, e=2, a=RUN, j=PACK)
             halves = ds_turned[w][:].rearrange("p j m -> p (j m)").bitcast(BF16)
-            copy(ds_r_view[:, w, groups], halves.rearrange("p (j g a e) -> p g e a j", j=PACK, a=RUN, e=2)[:, groups])
+            source = halves.rearrange("p (j g a e) -> p g e a j", j=PACK, a=RUN, e=2)
+            copy(target[:, w], source[:, h * RUN:(h + 1) * RUN])
 
         def quantize_ds_r(h):
-            quantize(ds_r, E5, h * HALF, ds_r_values[:, h * 2 * W:(h + 1) * 2 * W])
+            quantize(ds_r, E5, h * HALF, ds_r_values[h][:])
 
         gq_rows = out_0[0].rearrange("(m j) d -> m j d", j=PACK)
         gq_out = [tile("gq_out%d" % u, [P, 2, D], F32) for u in range(2)]
@@ -279,12 +283,10 @@ def tile_attend_gat_tnh_qk_ts_kernel(tc, qT, kT, vT, doT, rw, ts, qm, offs, out_
         def store_queries(u):
             nc.sync.dma_start(gq_rows[:, 2 * u:2 * u + 2, :], gq_out[u][:])
 
-        qm_rest = quantized("qm_rest", 3 * P)
-
         dk_listed = [tile("dk_listed%d" % c, [P, N], F32) for c in range(PACK)]
 
         def keys_gradient(c, first, end, number):
-            stationary, block = (qm_rest, c - 1) if c else (qm_first, 0)
+            stationary, block = qm_r[min(c, 2)], c // 3
             dk = bank(number, [P, end - first])
             product(dk[:], stationary, E4, block, ds_r, E5, first)
             return dk
@@ -306,18 +308,22 @@ def tile_attend_gat_tnh_qk_ts_kernel(tc, qT, kT, vT, doT, rw, ts, qm, offs, out_
         copy_turned(0, 0, nc.vector.tensor_copy)
         copy_turned(0, 1, nc.scalar.copy)
         quantize_ds_r(0)
+        quantize(qm_r[1], E4, 0, qm_values[1][:])
         copy_turned(1, 0, nc.scalar.copy)
         copy_turned(1, 1, nc.scalar.copy)
-        quantize(ds_i[1], E5, 0, ds_i_values[:, 2 * W:])
         half_of_keys(0, 0, 2, nc.vector.tensor_copy)
-        quantize(qm_rest, E4, 0, qm_values[:, W:])
+        ds_i.append(quantized("ds_i1", HALF, "qm_values1"))
+        quantize(ds_i[1], E5, 0, ds_i_values[:, 2 * W:])
+        qm_r.append(quantized_late("qm_r2", 2 * P, 0))
+        quantize(qm_r[2], E4, 0, qm_values[2][:])
         queries_gradient(0, 0, 6, nc.scalar.copy)
-        queries_gradient(0, 1, 7, nc.vector.tensor_copy)
+        queries_gradient(0, 1, 7, nc.scalar.copy)
         store_queries(0)
         place_by_scalar(0, 0)
         quantize_ds_r(1)
-        queries_gradient(1, 0, 2, nc.vector.tensor_copy)
-        queries_gradient(1, 1, 7, nc.vector.tensor_copy)
+        half_of_keys(3, 1, 2, nc.scalar.copy)
+        queries_gradient(1, 0, 0, nc.vector.tensor_copy)
+        queries_gradient(1, 1, 1, nc.vector.tensor_copy)
         store_queries(1)
         half_of_keys(0, 1, 3, nc.vector.tensor_copy)
         place_by_scalar(0, 1)
@@ -328,8 +334,7 @@ def tile_attend_gat_tnh_qk_ts_kernel(tc, qT, kT, vT, doT, rw, ts, qm, offs, out_
         dk_2 = keys_gradient(2, 0, N, 3)
         for h in range(2):
             nc.scalar.copy(dk_listed[2][:, h * HALF:(h + 1) * HALF], dk_2[:, h * HALF:(h + 1) * HALF])
-        half_of_keys(3, 0, 7, nc.vector.tensor_copy)
-        half_of_keys(3, 1, 6, nc.scalar.copy)
+        half_of_keys(3, 0, 1, nc.vector.tensor_copy)
         for h in range(2):
             place_by_scalar(2, h)
         store_keys(2, nc.scalar)

@@ -241,7 +241,7 @@ def tile_attend_gat_tnh_qk_ts_kernel(tc, qT, kT, vT, doT, rw, ts, qm, offs, out_
 
         ds_turned = [bank(4 + w, [P, PACK, P]) for w in range(2)]
         for j in range(PACK):
-            for w in range(2):
+            for w in (1, 0):
                 turn(ds_i_values, w, ds_turned[w], [j])
 
         ds_r_values = [

from contextlib import ExitStack

import concourse.mybir as mybir
from concourse.masks import make_identity

N, T, D, DV, R = 512, 2048, 512, 512, 512
FLOPS = 2 * N * R * (3 * D + DV)

F32 = mybir.dt.float32
BF16 = mybir.dt.bfloat16
I32 = mybir.dt.int32
U32 = mybir.dt.uint32
U16 = mybir.dt.uint16
U8 = mybir.dt.uint8
E4 = mybir.dt.float8_e4m3fn_x4
E5 = mybir.dt.float8_e5m2_x4
ACT = mybir.ActivationFunctionType
ALU = mybir.AluOpType

P = 128
PACK = 4
W = 512
HALF = W // 2
RUN = 8
DO_SHARE = 28


def tile_attend_gat_tnh_qk_ts_kernel(tc, qT, kT, vT, doT, rw, ts, qm, offs, out_0, out_1):
    nc = tc.nc
    with ExitStack() as ctx:
        keep = ctx.enter_context(tc.tile_pool(name="keep", bufs=1))
        late = ctx.enter_context(tc.tile_pool(name="late", bufs=1))
        psum = ctx.enter_context(tc.psum_pool(name="psum", bufs=1))

        def bank(number, shape):
            return psum.tile(shape, F32, name="bank%d" % number, tag="bank%d" % number)

        def tile(name, shape, dtype, tag=None):
            return keep.tile(shape, dtype, name=name, tag=tag or name, align_bytes=64)

        def quantized(name, width=W, tag=None):
            return tile(name + "_codes", [P, width], U32, tag), tile(name + "_scales", [P, width], U8)

        def values(name, columns, tag=None):
            return tile(name, [P, columns * PACK], BF16, tag)

        def quantize(op, fmt, first, source):
            count = source.shape[1] // PACK
            nc.vector.quantize_mx(
                out=op[0][:, first:first + count].bitcast(fmt),
                scales=op[1][:, first:first + count],
                in_=source,
            )

        def product(acc, stationary, fmt_s, block, moving, fmt_m, first=0):
            width = acc.shape[1]
            cols = slice(block * P, (block + 1) * P)
            nc.tensor.matmul_mx(
                out=acc,
                lhsT=stationary[0][:, cols].bitcast(fmt_s),
                lhsT_scale=stationary[1][:, cols],
                rhs=moving[0][:, first:first + width].bitcast(fmt_m),
                rhs_scale=moving[1][:, first:first + width],
                start=True,
                stop=True,
            )

        def interleave(copy, target, rows):
            copy(
                target.rearrange("p (c i j) -> p c j i", i=PACK, j=PACK),
                rows.rearrange("p j (c i) -> p c j i", i=PACK),
            )

        def deal(copy, target, rows, first, end):
            copy(
                target[:].rearrange("p (u m e j) -> p m j u e", u=2, e=2, j=PACK)[:, first:end],
                rows[:].rearrange("p j (m u e) -> p m j u e", u=2, e=2)[:, first:end],
            )

        def gather_plane(target, j, pool):
            planes = target[:].rearrange("p (t g a j) -> p j g t a", t=PACK, a=RUN, j=PACK)
            nc.vector.tensor_copy(planes[:, j], pool[:].indirect(offsets[:]))

        def turn(source, w, turned, places):
            words = source[:].bitcast(F32).rearrange("p (t m w) -> p w t m", t=PACK, w=2)
            for t in places:
                nc.tensor.transpose(turned[:, t, :], words[:, w, t, :], ident[:])

        offsets = keep.tile([P, N // 16], U16, name="offsets")
        ts_pool = tile("ts_pool", [P, T], F32)
        nc.vector.memset(ts_pool[:].bitcast(I32), 0)
        rw_col = tile("rw_col", [P, PACK], F32)

        def load(name, shape, rows):
            landed = tile(name, shape, F32)
            nc.sync.dma_start(landed[:], rows)
            return landed

        k_rows = kT.rearrange("(p j) t -> p j t", j=PACK)
        v_rows = vT.rearrange("(p j) t -> p j t", j=PACK)
        k_pool = [load("k_pool0", [P, T], k_rows[:, 0, :])]
        nc.sync.dma_start(offsets[:], offs)
        k_pool.append(load("k_pool1", [P, T], k_rows[:, 1, :]))
        nc.sync.dma_start(ts_pool[0:1, :], ts[0:1, :])
        nc.sync.dma_start(rw_col[:], rw[0].rearrange("(p t) o -> p (t o)", t=PACK))
        k_pool += [load("k_pool%d" % j, [P, T], k_rows[:, j, :]) for j in range(2, PACK)]
        q_rows = qT[0].rearrange("(p j) r -> p j r", j=PACK)
        q_raw = [load("q_raw%d" % h, [P, PACK, HALF], q_rows[:, :, h * HALF:(h + 1) * HALF]) for h in range(2)]
        v_pool = [load("v_pool%d" % j, [P, T], v_rows[:, j, :]) for j in range(PACK)]
        do_rows = doT[0].rearrange("(p j) r -> p j r", j=PACK)
        do_raw = [load("do_raw%d" % h, [P, PACK, HALF], do_rows[:, :, h * HALF:(h + 1) * HALF]) for h in range(2)]
        qm_rows = qm[0].rearrange("(p j) d -> p j d", j=PACK)
        qm_raw = late.tile([P, PACK, D], F32, name="qm_raw", align_bytes=64, offset=0)
        for h in range(2):
            nc.sync.dma_start(qm_raw[:, :, h * HALF:(h + 1) * HALF], qm_rows[:, :, h * HALF:(h + 1) * HALF])

        ident = tile("ident", [P, P], F32)
        make_identity(nc, ident[:])

        placed = {}

        def zero_window(c, engine, window):
            placed[c] = window
            engine.memset(window[:].bitcast(I32), 0)

        for c in (1, 3):
            zero_window(c, nc.vector, late.tile([P, T], F32, name="placed%d" % c, align_bytes=64, offset=4 * T * (c + 1) // 2))

        k_values = values("k_values", W)
        gather_plane(k_values, 0, k_pool[0])
        zero_window(0, nc.gpsimd, tile("placed0", [P, T], F32, "k_pool0"))

        ts_listed = tile("ts_listed", [P, N], F32)
        nc.vector.tensor_copy(
            ts_listed[:].rearrange("p (t g a) -> p g t a", t=PACK, a=RUN), ts_pool[:].indirect(offsets[:])
        )
        zero_window(2, nc.gpsimd, tile("placed2", [P, T], F32, "ts_pool"))
        ts_turned = bank(6, [P, PACK, P])
        for t in range(PACK):
            nc.tensor.transpose(ts_turned[:, t, :], ts_listed[:, t * P:(t + 1) * P], ident[:])
        ts_col = tile("ts_col", [P, PACK], F32)
        nc.scalar.copy(ts_col[:], ts_turned[:, :, 0])
        ts_neg = tile("ts_neg", [P, PACK], F32)
        nc.gpsimd.tensor_scalar(ts_neg[:], ts_col[:], -1.0, 0.0, ALU.mult, ALU.add)

        rw_wide = bank(7, [P, PACK, P])
        for j in range(PACK):
            nc.tensor.transpose(rw_wide[:, j, :], rw_col[:, j:j + 1].to_broadcast([P, P]), ident[:])
        rw_row = tile("rw_row", [P, R], F32)
        nc.scalar.copy(
            rw_row[:].rearrange("m (h j q) -> m h j q", h=2, j=PACK), rw_wide[:].rearrange("m j (h q) -> m h j q", h=2)
        )

        k_i_values = []

        def turn_keys(w, tag=None):
            k_i_values.append(values("k_i_values%d" % w, HALF, tag))
            turned = bank(4 + w, [P, PACK, P])
            turn(k_values, w, turned, range(PACK))
            nc.scalar.copy(
                k_i_values[w][:].rearrange("m (e p t) -> m e p t", e=2, t=PACK),
                turned[:].rearrange("m t p -> m (t p)").bitcast(BF16).rearrange("m (t p e) -> m e p t", t=PACK, e=2),
            )

        gather_plane(k_values, 1, k_pool[1])
        turn_keys(0)
        gather_plane(k_values, 2, k_pool[2])
        gather_plane(k_values, 3, k_pool[3])
        k_d = quantized("k_d")
        quantize(k_d, E4, 0, k_values[:])

        q_d = [quantized("q_d%d" % h, HALF) for h in range(2)]
        q_values = [values("q_values%d" % h, HALF) for h in range(2)]
        interleave(nc.scalar.copy, q_values[0][:], q_raw[0][:])
        turn_keys(1, "q_raw0")
        quantize(q_d[0], E4, 0, q_values[0][:])
        interleave(nc.vector.tensor_copy, q_values[1][:], q_raw[1][:])
        quantize(q_d[1], E4, 0, q_values[1][:])
        k_i = quantized("k_i", D, "q_values1")
        for w in range(2):
            quantize(k_i, E4, w * HALF, k_i_values[w][:])

        slope = [tile("slope%d" % h, [P, PACK, HALF], F32) for h in range(2)]
        for h in range(2):
            weight = tile("weight%d" % h, [P, PACK, HALF], F32)
            squared = tile("squared%d" % h, [P, PACK, HALF], F32)
            for pair in range(2):
                places = range(2 * pair, 2 * pair + 2)
                score = bank(pair, [P, 2, HALF])
                for t in places:
                    product(score[:, t % 2, :], k_d, E4, t, q_d[h], E4)
                for t in places:
                    nc.scalar.activation(
                        weight[:, t, :].rearrange("m (j q) -> m j q", j=PACK),
                        score[:, t % 2, :].rearrange("m (q j) -> m j q", j=PACK),
                        ACT.Tanh,
                        scale=ts_col[:, t:t + 1],
                    )
            for pair in range(2):
                both = slice(2 * pair, 2 * pair + 2)
                nc.scalar.activation(squared[:, both, :], weight[:, both, :], ACT.Square)
                for t in range(2 * pair, 2 * pair + 2):
                    plus, minus = ts_col[:, t:t + 1], ts_neg[:, t:t + 1]
                    if h == 0 and pair == 0:
                        nc.gpsimd.tensor_scalar(weight[:, t, :], squared[:, t, :], minus, plus, ALU.mult, ALU.add)
                    else:
                        nc.scalar.activation(weight[:, t, :], squared[:, t, :], ACT.Identity, bias=plus, scale=minus)
                gates = rw_row[:, h * HALF:(h + 1) * HALF].unsqueeze(1).to_broadcast([P, 2, HALF])
                nc.gpsimd.tensor_tensor(slope[h][:, both, :], weight[:, both, :], gates, ALU.mult)

        v_values = values("v_values", W)
        for j in range(PACK):
            gather_plane(v_values, j, v_pool[j])
        v_e = quantized("v_e")
        quantize(v_e, E4, 0, v_values[:])

        do_e = [quantized("do_e%d" % h, HALF) for h in range(2)]
        do_values = [values("do_values%d" % h, HALF) for h in range(2)]
        deal(nc.scalar.copy, do_values[0], do_raw[0], 0, P // 2)
        quantize(do_e[0], E5, 0, do_values[0][:])
        deal(nc.vector.tensor_copy, do_values[1], do_raw[1], 0, DO_SHARE)
        deal(nc.scalar.copy, do_values[1], do_raw[1], DO_SHARE, P // 2)
        quantize(do_e[1], E5, 0, do_values[1][:])

        ds_i_values = values("ds_i_values", R, "do_raw1")
        ds_view = ds_i_values[:].rearrange("m (u e h c i t) -> m h u e c t i", u=2, e=2, h=2, i=PACK, t=PACK)
        for h in range(2):
            slope_view = slope[h][:].rearrange("m t (u e c i) -> m u e c t i", u=2, e=2, i=PACK)
            for u in range(2):
                dp = bank(2 * h + u, [P, PACK, P])
                for t in range(PACK):
                    product(dp[:, t, :], v_e, E4, t, do_e[h], E5, u * P)
                dp_view = dp[:].rearrange("m t (c i e) -> m e c t i", i=PACK, e=2)
                for e in range(2):
                    nc.vector.tensor_tensor(ds_view[:, h, u, e], dp_view[:, e], slope_view[:, u, e], ALU.mult)

        qm_values = [values("qm_values0", P), values("qm_values1", P), values("qm_values2", 2 * P)]
        for c in range(PACK):
            target = qm_values[min(c, 2)][:, (c // 3) * W:(c // 3 + 1) * W]
            interleave(nc.scalar.copy, target, qm_raw[:, :, c * P:(c + 1) * P])

        ds_turned = [bank(4 + w, [P, PACK, P]) for w in range(2)]
        for j in range(PACK):
            for w in (1, 0):
                turn(ds_i_values, w, ds_turned[w], [j])

        ds_r_values = [
            late.tile([P, HALF * PACK], BF16, name="ds_r_values%d" % h, align_bytes=64, offset=h * 4 * W)
            for h in range(2)
        ]

        def quantized_late(name, width, first):
            codes = late.tile([P, width], U32, name=name + "_codes", align_bytes=64, offset=4 * first)
            return codes, tile(name + "_scales", [P, width], U8)

        ds_i = [quantized_late("ds_i0", HALF, 2 * W)]
        qm_r = [quantized_late("qm_r%d" % c, P, 3 * W + c * P) for c in range(2)]
        quantize(ds_i[0], E5, 0, ds_i_values[:, :2 * W])
        quantize(qm_r[0], E4, 0, qm_values[0][:])

        ds_r = quantized("ds_r")

        def copy_turned(h, w, copy):
            target = ds_r_values[h][:].rearrange("p (g w e a j) -> p w g e a j", w=2, e=2, a=RUN, j=PACK)
            halves = ds_turned[w][:].rearrange("p j m -> p (j m)").bitcast(BF16)
            source = halves.rearrange("p (j g a e) -> p g e a j", j=PACK, a=RUN, e=2)
            copy(target[:, w], source[:, h * RUN:(h + 1) * RUN])

        def quantize_ds_r(h):
            quantize(ds_r, E5, h * HALF, ds_r_values[h][:])

        gq_rows = out_0[0].rearrange("(m j) d -> m j d", j=PACK)
        gq_out = [tile("gq_out%d" % u, [P, 2, D], F32) for u in range(2)]

        def queries_gradient(u, e, number, copy):
            gq = bank(number, [P, D])
            product(gq[:], ds_i[u], E5, e, k_i, E4)
            copy(
                gq_out[u][:, e, :].rearrange("m (p j) -> m p j", j=PACK),
                gq[:].rearrange("m (j p) -> m p j", j=PACK),
            )

        def store_queries(u):
            nc.sync.dma_start(gq_rows[:, 2 * u:2 * u + 2, :], gq_out[u][:])

        dk_listed = [tile("dk_listed%d" % c, [P, N], F32) for c in range(PACK)]

        def keys_gradient(c, first, end, number):
            stationary, block = qm_r[min(c, 2)], c // 3
            dk = bank(number, [P, end - first])
            product(dk[:], stationary, E4, block, ds_r, E5, first)
            return dk

        def place_by_scalar(c, h):
            window = placed[c][:].indirect(offsets[:, h * HALF // 16:(h + 1) * HALF // 16])
            nc.scalar.activation(window, dk_listed[c][:, h * HALF:(h + 1) * HALF], ACT.Copy)

        def place_by_vector(c):
            nc.vector.tensor_copy(placed[c][:].indirect(offsets[:]), dk_listed[c][:])

        def store_keys(c, queue):
            queue.dma_start(out_1[c * P:(c + 1) * P, :], placed[c][:])

        def half_of_keys(c, h, number, copy):
            dk = keys_gradient(c, h * HALF, (h + 1) * HALF, number)
            copy(dk_listed[c][:, h * HALF:(h + 1) * HALF], dk[:])

        copy_turned(0, 0, nc.vector.tensor_copy)
        copy_turned(0, 1, nc.scalar.copy)
        quantize_ds_r(0)
        quantize(qm_r[1], E4, 0, qm_values[1][:])
        copy_turned(1, 0, nc.scalar.copy)
        copy_turned(1, 1, nc.scalar.copy)
        half_of_keys(0, 0, 2, nc.vector.tensor_copy)
        ds_i.append(quantized("ds_i1", HALF, "qm_values1"))
        quantize(ds_i[1], E5, 0, ds_i_values[:, 2 * W:])
        qm_r.append(quantized_late("qm_r2", 2 * P, 0))
        quantize(qm_r[2], E4, 0, qm_values[2][:])
        queries_gradient(0, 0, 6, nc.scalar.copy)
        queries_gradient(0, 1, 7, nc.scalar.copy)
        store_queries(0)
        place_by_scalar(0, 0)
        quantize_ds_r(1)
        half_of_keys(3, 1, 2, nc.scalar.copy)
        queries_gradient(1, 0, 0, nc.vector.tensor_copy)
        queries_gradient(1, 1, 1, nc.vector.tensor_copy)
        store_queries(1)
        half_of_keys(0, 1, 3, nc.vector.tensor_copy)
        place_by_scalar(0, 1)
        store_keys(0, nc.sync)
        nc.vector.tensor_copy(dk_listed[1][:], keys_gradient(1, 0, N, 6)[:])
        place_by_vector(1)
        store_keys(1, nc.sync)
        dk_2 = keys_gradient(2, 0, N, 3)
        for h in range(2):
            nc.scalar.copy(dk_listed[2][:, h * HALF:(h + 1) * HALF], dk_2[:, h * HALF:(h + 1) * HALF])
        half_of_keys(3, 0, 1, nc.vector.tensor_copy)
        for h in range(2):
            place_by_scalar(2, h)
        store_keys(2, nc.scalar)
        place_by_vector(3)
        store_keys(3, nc.sync)
